import numpy as np
import ml_dtypes


def mxq(x, axis, fmt="e4m3"):
    dtype, down = {"e4m3": (ml_dtypes.float8_e4m3fn, 7), "e5m2": (ml_dtypes.float8_e5m2, 14)}[fmt]
    v = np.moveaxis(np.asarray(x, np.float32).astype(ml_dtypes.bfloat16).astype(np.float64), axis, -1)
    blocks = v.reshape(v.shape[:-1] + (-1, 32))
    amax = np.abs(blocks).max(-1, keepdims=True)
    byte = np.maximum(np.where(amax > 0, np.frexp(amax)[1] - 1 + 127, 0) - down, 1)
    scale = np.exp2(byte - 127.0)
    codes = (blocks / scale).astype(np.float32).astype(dtype).astype(np.float64)
    return np.moveaxis((codes * scale).reshape(v.shape), -1, axis)


WIDE = False


def mx_kscale(k):
    if not WIDE:
        return np.ones(k)
    levels = np.array([10, -10, 5, -5, 0])
    if k % 512:
        return np.exp2(np.random.permutation(np.resize(levels, k // 32))).repeat(32)
    a = np.empty((k // 512, 16))
    for p in range(k // 512):
        a[p, :8] = np.random.permutation(np.resize(levels, 8))
        for g in range(8):
            far = levels[np.abs(levels - a[p, g]) >= 10]
            a[p, g + 8] = far[np.random.randint(len(far))]
    return np.exp2(a.ravel()).repeat(32)


def f64(x):
    return np.asarray(x).astype(np.float64)


def striped(idx):
    return np.tile(idx.reshape(-1, 16).T, (8, 1)).astype(np.uint16)


def unstriped(offs):
    return offs[:16].T.reshape(-1).astype(np.int64)


K, T, E, C, N = 1024, 1536, 24, 128, 128


def by_expert(wq, xq):
    return np.concatenate([wq[e].T @ xq[:, e * C:(e + 1) * C] for e in range(E)], axis=1)


def setup_inputs():
    n = np.random.standard_normal
    s = mx_kscale(K)[:, None]
    first = np.random.permutation(np.repeat(np.arange(E), T // E))
    second = (first + 1 + np.random.permutation(np.repeat(np.arange(E - 1), -(-T // (E - 1)))[:T])) % E
    while np.bincount(second, minlength=E).max() != T // E:
        load = np.bincount(second, minlength=E); hi, lo = int(load.argmax()), int(load.argmin())
        t = np.flatnonzero((second == hi) & (first != lo))[0]; second[t] = lo
    slot_token = np.empty(E * C, np.int64); pos = np.empty((2, T), np.int64); fill = np.zeros(E, np.int64)
    place = np.stack([np.random.permutation(C) for _ in range(E)])
    for r, deal in enumerate((first, second)):
        for t in np.random.permutation(T):
            e = deal[t]; j = e * C + place[e, fill[e]]; fill[e] += 1; slot_token[j] = t; pos[r, t] = j
    g = np.random.uniform(0.2, 0.8, T)
    return {
        "xT": (n((K, T)) * s).astype(np.float32),
        "w": (n((E + 1, K, N)) / np.sqrt(K) / s[None]).astype(np.float32),
        "b": (0.3 * n((N, E + 1))).astype(np.float32),
        "gate": np.stack([np.tile(g, (N, 1)), np.tile(1.0 - g, (N, 1))]).astype(np.float32),
        "offs": striped(slot_token),
        "pos1": striped(pos[0]),
        "pos2": striped(pos[1]),
    }


def reference(xT, w, b, gate, offs, pos1, pos2):
    idx = unstriped(offs)
    wq = mxq(f64(w), 1, "e4m3")
    xs = mxq(f64(xT), 0, "e4m3")
    ys = (wq[E].T @ xs) + f64(b)[:, E:]
    xq = mxq(f64(xT)[:, idx], 0, "e4m3")
    y = by_expert(wq, xq)
    y = y + np.repeat(f64(b)[:, :E], C, axis=1)
    return ys + f64(gate[0]) * y[:, unstriped(pos1)] + f64(gate[1]) * y[:, unstriped(pos2)]

@@ -1,0 +1,253 @@
+from contextlib import ExitStack
+
+import concourse.mybir as mybir
+
+P = 128
+K, T, E, C, N = 1024, 1536, 24, 128, 128
+S = E * C
+G = 2
+Q = 3
+SQ = S // Q
+
+F32 = mybir.dt.float32
+BF16 = mybir.dt.bfloat16
+U32 = mybir.dt.uint32
+U16 = mybir.dt.uint16
+U8 = mybir.dt.uint8
+FP8X4 = mybir.dt.float8_e4m3fn_x4
+ADD = mybir.AluOpType.add
+MULT = mybir.AluOpType.mult
+IDENTITY = mybir.ActivationFunctionType.Identity
+
+FLOPS = 2 * K * N * (S + T)
+
+W_VECTOR = (8, 16, 23)
+
+
+def tile_moe_shr_lin_bias_kernel(tc, xT, w, b, gate, offs, pos1, pos2, out):
+    nc = tc.nc
+    with ExitStack() as ctx:
+        held = ctx.enter_context(tc.tile_pool(name="held", bufs=1))
+        ring = ctx.enter_context(tc.tile_pool(name="ring", bufs=1))
+        psum = ctx.enter_context(tc.psum_pool(name="psum", bufs=1))
+
+        offs_t = held.tile([P, S // 16], U16, name="offs_t")
+        pos1_t = held.tile([P, T // 16], U16, name="pos1_t")
+        pos2_t = held.tile([P, T // 16], U16, name="pos2_t")
+        b_t = held.tile([P, E + 1], F32, name="b_t")
+        sc = held.tile([P, G, S], U32, name="sc", align_bytes=64)
+        ss = held.tile([P, G, S], U8, name="ss", align_bytes=64)
+        xc = held.tile([P, G, T], U32, name="xc", align_bytes=64)
+        xs = held.tile([P, G, T], U8, name="xs", align_bytes=64)
+        wc = held.tile([P, E + 1, G, N], U32, name="wc", align_bytes=64)
+        ws = held.tile([P, E + 1, G, N], U8, name="ws", align_bytes=64)
+
+        x_view = xT.rearrange("(g p j) t -> g p j t", g=G, j=4)
+        w_view = w.rearrange("e (g p j) n -> p e g j n", g=G, j=4)
+        gate_view = gate.rearrange("r p t -> p r t")
+
+        nc.sync.dma_start(offs_t[:], offs)
+
+        tables = []
+        for g in range(G):
+            table = ring.tile([P, 2, 2 * T], BF16, name="table%d" % g, tag="t12", bufs=2, align_bytes=64)
+            tables.append(table)
+
+        def raw_tile(name, width):
+            return ring.tile([P, 2, width], F32, name=name, tag="raw", bufs=7, align_bytes=64)
+
+        def load_and_cast_x(g, u, t0, width, cut, engine):
+            raw = raw_tile("xraw", width)
+            for c in range(0, width, cut):
+                nc.sync.dma_start(raw[:, :, c : c + cut], x_view[g, :, 2 * u : 2 * u + 2, t0 + c : t0 + c + cut])
+                dst = tables[g][:, u, 2 * (t0 + c) : 2 * (t0 + c + cut)].rearrange("p (n e) -> p n e", e=2)
+                src = raw[:, :, c : c + cut].rearrange("p e n -> p n e")
+                if engine == "V":
+                    nc.vector.tensor_copy(dst, src)
+                else:
+                    nc.scalar.copy(dst, src)
+
+        planes = {}
+
+        def gather(g, u, q):
+            if u == 0:
+                planes[g, q] = ring.tile([P, 2, 2 * SQ], BF16, name="planes", tag="planes", bufs=4, align_bytes=64)
+            nc.vector.tensor_copy(
+                planes[g, q][:, u, :].bitcast(U32),
+                tables[g][:, u, :].bitcast(U32).indirect(offs_t[:, q * SQ // 16 : (q + 1) * SQ // 16]),
+            )
+
+        grouped = {}
+
+        def interleave(g, q):
+            t = ring.tile([P, 4 * SQ], BF16, name="grouped", tag="grouped", bufs=3, align_bytes=64)
+            dst = t[:].bitcast(F32).rearrange("p (n u) -> p n u", u=2)
+            src = planes[g, q][:].rearrange("p u m -> p (u m)").bitcast(F32).rearrange("p (u n) -> p n u", u=2)
+            nc.scalar.copy(dst, src)
+            grouped[g, q] = t
+
+        def quantise_slots(g, q):
+            cols = slice(q * SQ, (q + 1) * SQ)
+            nc.vector.quantize_mx(out=sc[:, g, cols].bitcast(FP8X4), scales=ss[:, g, cols], in_=grouped[g, q][:])
+
+        wgrouped = {}
+
+        def load_and_cast_w(e0, n, split):
+            raw = raw_tile("wraw", n * 4 * N)
+            halves = raw[:].rearrange("p a b -> p (a b)").rearrange("p (e g m) -> p e g m", g=G, m=4 * N)
+            nc.sync.dma_start(halves.rearrange("p e g (j n) -> p e g j n", j=4), w_view[:, e0 : e0 + n])
+            t = ring.tile([P, n, G * 4 * N], BF16, name="wgrouped", tag="wgrouped", bufs=5, align_bytes=64)
+            for k in range(0, n, split):
+                dst = t[:, k : k + split, :].rearrange("p e (a c i t) -> p (e a) c t i", c=N // 4, i=4, t=4)
+                src = halves[:, k : k + split].rearrange("p e g (t c i) -> p (e g) c t i", t=4, i=4)
+                if e0 + k in W_VECTOR:
+                    nc.vector.tensor_copy(dst, src)
+                else:
+                    nc.scalar.copy(dst, src)
+            wgrouped[e0] = t
+
+        def quantise_w(e0, n, k=0):
+            nc.vector.quantize_mx(
+                out=wc[:, e0 + k : e0 + k + n].rearrange("p e g n -> p (e g n)").bitcast(FP8X4),
+                scales=ws[:, e0 + k : e0 + k + n].rearrange("p e g n -> p (e g n)"),
+                in_=wgrouped[e0][:, k : k + n, :].rearrange("p e m -> p (e m)"),
+            )
+
+        def multiply(bank, e, codes, scales, cols):
+            for g in range(G):
+                nc.tensor.matmul_mx(
+                    out=bank,
+                    lhsT=wc[:, e, g, :].bitcast(FP8X4),
+                    lhsT_scale=ws[:, e, g, :],
+                    rhs=codes[:, g, cols].bitcast(FP8X4),
+                    rhs_scale=scales[:, g, cols],
+                    start=(g == 0),
+                    stop=(g == G - 1),
+                )
+
+        def group_tokens(g, t0, n, on_vector):
+            t = ring.tile([P, 4 * n], BF16, name="xgrouped", tag="grouped", bufs=3, align_bytes=64)
+            dst = t[:].bitcast(F32).rearrange("p (n u) -> p n u", u=2)
+            words = tables[g][:].rearrange("p u m -> p (u m)").bitcast(F32).rearrange("p (u n) -> p n u", u=2)
+            if on_vector:
+                nc.vector.tensor_copy(dst, words[:, t0 : t0 + n, :])
+            else:
+                nc.scalar.copy(dst, words[:, t0 : t0 + n, :])
+            return t
+
+        def quantise_tokens(t, g, t0, n):
+            cols = slice(t0, t0 + n)
+            nc.vector.quantize_mx(out=xc[:, g, cols].bitcast(FP8X4), scales=xs[:, g, cols], in_=t[:])
+
+        def token_steps(g, on_vector):
+            a = group_tokens(g, 0, 1024, on_vector)
+            c = group_tokens(g, 1024, 512, on_vector)
+            quantise_tokens(a, g, 0, 1024)
+            quantise_tokens(c, g, 1024, 512)
+
+        def expert_bank(e0, n):
+            bank = psum.tile([P, 4 * C], F32, name="bank", tag="bank", bufs=4)
+            for k in range(n):
+                cols = slice((e0 + k) * C, (e0 + k + 1) * C)
+                multiply(bank[:, k * C : (k + 1) * C], e0 + k, sc, ss, cols)
+            for k in range(n):
+                e = e0 + k
+                nc.scalar.activation(
+                    y[:, e * C : (e + 1) * C], bank[:, k * C : (k + 1) * C], IDENTITY, bias=b_t[:, e : e + 1]
+                )
+
+        load_and_cast_x(0, 0, 0, 1024, 512, "V")
+        load_and_cast_x(0, 0, 1024, 512, 256, "V")
+        load_and_cast_x(0, 1, 0, 1024, 512, "S")
+        load_and_cast_x(0, 1, 1024, 512, 512, "S")
+        load_and_cast_x(1, 0, 0, 1024, 1024, "S")
+        load_and_cast_x(1, 0, 1024, 512, 512, "S")
+        load_and_cast_x(1, 1, 0, 1024, 1024, "S")
+        load_and_cast_x(1, 1, 1024, 512, 512, "S")
+        nc.sync.dma_start(b_t[:], b)
+        nc.sync.dma_start(pos1_t[:], pos1)
+        nc.sync.dma_start(pos2_t[:], pos2)
+
+        for u in range(2):
+            for q in range(Q):
+                gather(0, u, q)
+        for q in range(Q):
+            interleave(0, q)
+        pairs = E // 2
+        gates = []
+        cuts = ((0, 1024), (1024, 1536))
+        for i in range(3):
+            load_and_cast_w(2 * i, 2, 2)
+        for i in range(2):
+            quantise_w(2 * i, 2)
+        for q in range(Q):
+            gather(1, 0, q)
+            gather(1, 1, q)
+            interleave(1, q)
+            quantise_slots(0, q)
+            load_and_cast_w(2 * (3 + q), 2, 2)
+            quantise_w(2 * (2 + q), 2)
+        for q in range(Q):
+            quantise_slots(1, q)
+        token_steps(0, True)
+        y = ring.tile([P, S], F32, name="y", tag="t12", bufs=2, align_bytes=64)
+        for i in range(6, pairs):
+            if i == 9:
+                load_and_cast_w(E, 1, 1)
+                for t0, t1 in cuts:
+                    t = raw_tile("gates", t1 - t0)
+                    nc.sync.dma_start(t[:], gate_view[:, :, t0:t1])
+                    gates.append(t)
+            load_and_cast_w(2 * i, 2, 2 if i < pairs - 1 else 1)
+            quantise_w(2 * (i - 1), 2)
+            if i == 6:
+                expert_bank(0, 4)
+                expert_bank(4, 4)
+            elif i % 2 == 1:
+                expert_bank(2 * (i - 3), 4)
+        quantise_w(E - 2, 1)
+        quantise_w(E - 2, 1, 1)
+        expert_bank(20, 2)
+        expert_bank(22, 2)
+        token_steps(1, True)
+        quantise_w(E, 1)
+        shared = []
+        for c in range(3):
+            bank = psum.tile([P, 512], F32, name="shared%d" % c)
+            multiply(bank[:], E, xc, xs, slice(c * 512, (c + 1) * 512))
+            shared.append(bank)
+
+        first = ring.tile([P, T], F32, name="first", tag="planes", bufs=4, align_bytes=64)
+        second = ring.tile([P, T], F32, name="second", tag="planes", bufs=4, align_bytes=64)
+        total = ring.tile([P, T], F32, name="total", tag="planes", bufs=4, align_bytes=64)
+
+        def fetch(dst, pos, r, k):
+            t0, t1 = cuts[k]
+            nc.vector.tensor_tensor(dst[:, t0:t1], y[:].indirect(pos[:, t0 // 16 : t1 // 16]), gates[k][:, r, :], MULT)
+
+        def add_shared(t0, t1):
+            c = t0 // 512
+            nc.vector.scalar_tensor_tensor(
+                out=total[:, t0:t1],
+                in0=shared[c][:, t0 - 512 * c : t1 - 512 * c],
+                scalar=b_t[:, E : E + 1],
+                in1=first[:, t0:t1],
+                op0=ADD,
+                op1=ADD,
+            )
+
+        def add_second(t0, t1):
+            nc.vector.tensor_tensor(total[:, t0:t1], total[:, t0:t1], second[:, t0:t1], ADD)
+            nc.sync.dma_start(out[:, t0:t1], total[:, t0:t1])
+
+        fetch(first, pos1_t, 0, 0)
+        fetch(second, pos2_t, 1, 0)
+        add_shared(0, 512)
+        add_shared(512, 1024)
+        fetch(first, pos1_t, 0, 1)
+        add_second(0, 1024)
+        fetch(second, pos2_t, 1, 1)
+        add_shared(1024, 1280)
+        add_shared(1280, 1536)
+        add_second(1024, 1280)
+        add_second(1280, 1536)

@@ -21,7 +21,8 @@ IDENTITY = mybir.ActivationFunctionType.Identity
 
 FLOPS = 2 * K * N * (S + T)
 
-W_VECTOR = (8, 16, 23)
+W_GPSIMD = (2, 4, 6, 10, 14, 16)
+GPSIMD_RUN = 512
 
 
 def tile_moe_shr_lin_bias_kernel(tc, xT, w, b, gate, offs, pos1, pos2, out):
@@ -54,7 +55,7 @@ def tile_moe_shr_lin_bias_kernel(tc, xT, w, b, gate, offs, pos1, pos2, out):
             tables.append(table)
 
         def raw_tile(name, width):
-            return ring.tile([P, 2, width], F32, name=name, tag="raw", bufs=7, align_bytes=64)
+            return ring.tile([P, 2, width], F32, name=name, tag="raw", bufs=5, align_bytes=64)
 
         def load_and_cast_x(g, u, t0, width, cut, engine):
             raw = raw_tile("xraw", width)
@@ -64,8 +65,12 @@ def tile_moe_shr_lin_bias_kernel(tc, xT, w, b, gate, offs, pos1, pos2, out):
                 src = raw[:, :, c : c + cut].rearrange("p e n -> p n e")
                 if engine == "V":
                     nc.vector.tensor_copy(dst, src)
-                else:
+                elif engine == "S":
                     nc.scalar.copy(dst, src)
+                else:
+                    for m in range(0, cut, GPSIMD_RUN // 2):
+                        run = slice(m, m + GPSIMD_RUN // 2)
+                        nc.gpsimd.tensor_scalar(dst[:, run, :], src[:, run, :], 1.0, 0.0, MULT, ADD)
 
         planes = {}
 
@@ -79,11 +84,14 @@ def tile_moe_shr_lin_bias_kernel(tc, xT, w, b, gate, offs, pos1, pos2, out):
 
         grouped = {}
 
-        def interleave(g, q):
-            t = ring.tile([P, 4 * SQ], BF16, name="grouped", tag="grouped", bufs=3, align_bytes=64)
+        def interleave(g, q, on_vector=False):
+            t = ring.tile([P, 4 * SQ], BF16, name="grouped", tag="grouped", bufs=4, align_bytes=64)
             dst = t[:].bitcast(F32).rearrange("p (n u) -> p n u", u=2)
             src = planes[g, q][:].rearrange("p u m -> p (u m)").bitcast(F32).rearrange("p (u n) -> p n u", u=2)
-            nc.scalar.copy(dst, src)
+            if on_vector:
+                nc.vector.tensor_copy(dst, src)
+            else:
+                nc.scalar.copy(dst, src)
             grouped[g, q] = t
 
         def quantise_slots(g, q):
@@ -96,12 +104,15 @@ def tile_moe_shr_lin_bias_kernel(tc, xT, w, b, gate, offs, pos1, pos2, out):
             raw = raw_tile("wraw", n * 4 * N)
             halves = raw[:].rearrange("p a b -> p (a b)").rearrange("p (e g m) -> p e g m", g=G, m=4 * N)
             nc.sync.dma_start(halves.rearrange("p e g (j n) -> p e g j n", j=4), w_view[:, e0 : e0 + n])
-            t = ring.tile([P, n, G * 4 * N], BF16, name="wgrouped", tag="wgrouped", bufs=5, align_bytes=64)
+            t = ring.tile([P, n, G * 4 * N], BF16, name="wgrouped", tag="wgrouped", bufs=8, align_bytes=64)
             for k in range(0, n, split):
                 dst = t[:, k : k + split, :].rearrange("p e (a c i t) -> p (e a) c t i", c=N // 4, i=4, t=4)
                 src = halves[:, k : k + split].rearrange("p e g (t c i) -> p (e g) c t i", t=4, i=4)
-                if e0 + k in W_VECTOR:
-                    nc.vector.tensor_copy(dst, src)
+                if e0 in W_GPSIMD:
+                    dst = t[:, k : k + split, :].rearrange("p e (a n t) -> p (e a) n t", n=N, t=4)
+                    src = halves[:, k : k + split].rearrange("p e g (t n) -> p (e g) n t", t=4)
+                    for a in range(split * G):
+                        nc.gpsimd.tensor_scalar(dst[:, a], src[:, a], 1.0, 0.0, MULT, ADD)
                 else:
                     nc.scalar.copy(dst, src)
             wgrouped[e0] = t
@@ -126,7 +137,7 @@ def tile_moe_shr_lin_bias_kernel(tc, xT, w, b, gate, offs, pos1, pos2, out):
                 )
 
         def group_tokens(g, t0, n, on_vector):
-            t = ring.tile([P, 4 * n], BF16, name="xgrouped", tag="grouped", bufs=3, align_bytes=64)
+            t = ring.tile([P, 4 * n], BF16, name="xgrouped", tag="grouped", bufs=4, align_bytes=64)
             dst = t[:].bitcast(F32).rearrange("p (n u) -> p n u", u=2)
             words = tables[g][:].rearrange("p u m -> p (u m)").bitcast(F32).rearrange("p (u n) -> p n u", u=2)
             if on_vector:
@@ -145,72 +156,76 @@ def tile_moe_shr_lin_bias_kernel(tc, xT, w, b, gate, offs, pos1, pos2, out):
             quantise_tokens(a, g, 0, 1024)
             quantise_tokens(c, g, 1024, 512)
 
-        def expert_bank(e0, n):
-            bank = psum.tile([P, 4 * C], F32, name="bank", tag="bank", bufs=4)
-            for k in range(n):
-                cols = slice((e0 + k) * C, (e0 + k + 1) * C)
-                multiply(bank[:, k * C : (k + 1) * C], e0 + k, sc, ss, cols)
-            for k in range(n):
-                e = e0 + k
+        def expert_bank(*experts):
+            bank = psum.tile([P, 4 * C], F32, name="bank", tag="bank", bufs=5)
+            for k, e in enumerate(experts):
+                multiply(bank[:, k * C : (k + 1) * C], e, sc, ss, slice(e * C, (e + 1) * C))
+            for k, e in enumerate(experts):
                 nc.scalar.activation(
                     y[:, e * C : (e + 1) * C], bank[:, k * C : (k + 1) * C], IDENTITY, bias=b_t[:, e : e + 1]
                 )
 
         load_and_cast_x(0, 0, 0, 1024, 512, "V")
         load_and_cast_x(0, 0, 1024, 512, 256, "V")
-        load_and_cast_x(0, 1, 0, 1024, 512, "S")
-        load_and_cast_x(0, 1, 1024, 512, 512, "S")
-        load_and_cast_x(1, 0, 0, 1024, 1024, "S")
-        load_and_cast_x(1, 0, 1024, 512, 512, "S")
-        load_and_cast_x(1, 1, 0, 1024, 1024, "S")
-        load_and_cast_x(1, 1, 1024, 512, 512, "S")
+        load_and_cast_x(0, 1, 0, 768, 768, "S")
+        load_and_cast_x(0, 1, 768, 768, 768, "S")
+        for q in range(Q):
+            gather(0, 0, q)
+            gather(0, 1, q)
+        token_steps(0, False)
+        for e0 in (0, 2, 4):
+            load_and_cast_w(e0, 2, 2)
+        for q in range(Q):
+            interleave(0, q)
+        for u in range(2):
+            load_and_cast_x(1, u, 0, 768, 768, "S")
+            load_and_cast_x(1, u, 768, 768, 768, "S")
         nc.sync.dma_start(b_t[:], b)
         nc.sync.dma_start(pos1_t[:], pos1)
         nc.sync.dma_start(pos2_t[:], pos2)
-
-        for u in range(2):
-            for q in range(Q):
-                gather(0, u, q)
         for q in range(Q):
-            interleave(0, q)
-        pairs = E // 2
-        gates = []
-        cuts = ((0, 1024), (1024, 1536))
-        for i in range(3):
-            load_and_cast_w(2 * i, 2, 2)
-        for i in range(2):
-            quantise_w(2 * i, 2)
+            quantise_slots(0, q)
+            quantise_w(2 * q, 2)
         for q in range(Q):
             gather(1, 0, q)
             gather(1, 1, q)
-            interleave(1, q)
-            quantise_slots(0, q)
-            load_and_cast_w(2 * (3 + q), 2, 2)
-            quantise_w(2 * (2 + q), 2)
+        load_and_cast_w(6, 2, 2)
+        token_steps(1, False)
+        for e0 in (8, 10, 12):
+            load_and_cast_w(e0, 2, 2)
+        interleave(1, 0)
+        load_and_cast_w(14, 2, 2)
+        interleave(1, 1)
+        load_and_cast_w(16, 2, 2)
+        interleave(1, 2, True)
+        for e0 in (6, 8, 10):
+            quantise_w(e0, 2)
         for q in range(Q):
             quantise_slots(1, q)
-        token_steps(0, True)
+            quantise_w(12 + 2 * q, 2)
         y = ring.tile([P, S], F32, name="y", tag="t12", bufs=2, align_bytes=64)
-        for i in range(6, pairs):
-            if i == 9:
-                load_and_cast_w(E, 1, 1)
-                for t0, t1 in cuts:
-                    t = raw_tile("gates", t1 - t0)
-                    nc.sync.dma_start(t[:], gate_view[:, :, t0:t1])
-                    gates.append(t)
-            load_and_cast_w(2 * i, 2, 2 if i < pairs - 1 else 1)
-            quantise_w(2 * (i - 1), 2)
-            if i == 6:
-                expert_bank(0, 4)
-                expert_bank(4, 4)
-            elif i % 2 == 1:
-                expert_bank(2 * (i - 3), 4)
+        load_and_cast_w(18, 2, 2)
+        quantise_w(18, 2)
+        expert_bank(0, 1, 12, 13)
+        expert_bank(2, 3, 14, 15)
+        load_and_cast_w(20, 2, 2)
+        quantise_w(20, 2)
+        expert_bank(4, 5, 16, 17)
+        expert_bank(6, 7, 18, 19)
+        load_and_cast_w(22, 2, 1)
         quantise_w(E - 2, 1)
+        expert_bank(8, 9, 20, 21)
         quantise_w(E - 2, 1, 1)
-        expert_bank(20, 2)
-        expert_bank(22, 2)
-        token_steps(1, True)
+        expert_bank(10, 11, 22)
+        expert_bank(23)
+        load_and_cast_w(E, 1, 1)
         quantise_w(E, 1)
+        gates = []
+        cuts = ((0, 1024), (1024, 1536))
+        for t0, t1 in cuts:
+            t = raw_tile("gates", t1 - t0)
+            nc.sync.dma_start(t[:], gate_view[:, :, t0:t1])
+            gates.append(t)
         shared = []
         for c in range(3):
             bank = psum.tile([P, 512], F32, name="shared%d" % c)

@@ -1,6 +1,7 @@
 from contextlib import ExitStack
 
 import concourse.mybir as mybir
+from concourse.masks import make_identity
 
 P = 128
 K, T, E, C, N = 1024, 1536, 24, 128, 128
@@ -19,10 +20,11 @@ ADD = mybir.AluOpType.add
 MULT = mybir.AluOpType.mult
 IDENTITY = mybir.ActivationFunctionType.Identity
 
-FLOPS = 2 * K * N * (S + T)
+PLANE_SLOTS = ("planes0", "planes1", "planes2", "planes1", "planes0", "table0")
 
-W_GPSIMD = (2, 4, 6, 10, 14, 16)
-GPSIMD_RUN = 512
+CHAIN = (8, 22)
+
+FLOPS = 2 * K * N * (S + T)
 
 
 def tile_moe_shr_lin_bias_kernel(tc, xT, w, b, gate, offs, pos1, pos2, out):
@@ -38,8 +40,7 @@ def tile_moe_shr_lin_bias_kernel(tc, xT, w, b, gate, offs, pos1, pos2, out):
         b_t = held.tile([P, E + 1], F32, name="b_t")
         sc = held.tile([P, G, S], U32, name="sc", align_bytes=64)
         ss = held.tile([P, G, S], U8, name="ss", align_bytes=64)
-        xc = held.tile([P, G, T], U32, name="xc", align_bytes=64)
-        xs = held.tile([P, G, T], U8, name="xs", align_bytes=64)
+        ident = held.tile([P, P], F32, name="ident")
         wc = held.tile([P, E + 1, G, N], U32, name="wc", align_bytes=64)
         ws = held.tile([P, E + 1, G, N], U8, name="ws", align_bytes=64)
 
@@ -48,80 +49,93 @@ def tile_moe_shr_lin_bias_kernel(tc, xT, w, b, gate, offs, pos1, pos2, out):
         gate_view = gate.rearrange("r p t -> p r t")
 
         nc.sync.dma_start(offs_t[:], offs)
+        make_identity(nc, ident[:])
+        sc_pass = [sc[:, g, :] for g in range(G)]
+        ss_pass = [ss[:, g, :] for g in range(G)]
+        xc_pass = [held.tile([P, T], U32, name="xc0", align_bytes=64)]
+        xs_pass = [held.tile([P, T], U8, name="xs0", align_bytes=64)]
 
         tables = []
         for g in range(G):
-            table = ring.tile([P, 2, 2 * T], BF16, name="table%d" % g, tag="t12", bufs=2, align_bytes=64)
+            table = ring.tile([P, 2, 2 * T], BF16, name="table%d" % g, tag="table%d" % g, bufs=1, align_bytes=64)
             tables.append(table)
 
-        def raw_tile(name, width):
-            return ring.tile([P, 2, width], F32, name=name, tag="raw", bufs=5, align_bytes=64)
+        def raw_tile(name, width, tag="raw", bufs=5):
+            return ring.tile([P, 2, width], F32, name=name, tag=tag, bufs=bufs, align_bytes=64)
 
-        def load_and_cast_x(g, u, t0, width, cut, engine):
-            raw = raw_tile("xraw", width)
+        def load_and_cast_x(g, u, t0, width, cut, engine, tag="raw", bufs=5):
+            raw = raw_tile("xraw", width, tag, bufs)
             for c in range(0, width, cut):
                 nc.sync.dma_start(raw[:, :, c : c + cut], x_view[g, :, 2 * u : 2 * u + 2, t0 + c : t0 + c + cut])
                 dst = tables[g][:, u, 2 * (t0 + c) : 2 * (t0 + c + cut)].rearrange("p (n e) -> p n e", e=2)
                 src = raw[:, :, c : c + cut].rearrange("p e n -> p n e")
                 if engine == "V":
                     nc.vector.tensor_copy(dst, src)
-                elif engine == "S":
-                    nc.scalar.copy(dst, src)
                 else:
-                    for m in range(0, cut, GPSIMD_RUN // 2):
-                        run = slice(m, m + GPSIMD_RUN // 2)
-                        nc.gpsimd.tensor_scalar(dst[:, run, :], src[:, run, :], 1.0, 0.0, MULT, ADD)
+                    nc.scalar.copy(dst, src)
 
         planes = {}
 
         def gather(g, u, q):
             if u == 0:
-                planes[g, q] = ring.tile([P, 2, 2 * SQ], BF16, name="planes", tag="planes", bufs=4, align_bytes=64)
+                planes[g, q] = ring.tile([P, 2, 2 * SQ], BF16, name="planes", tag=PLANE_SLOTS[Q * g + q], bufs=1, align_bytes=64)
+            window = tables[g][:].rearrange("p u m -> p (u m)") if (g, u) == (1, 0) else tables[g][:, u, :]
             nc.vector.tensor_copy(
                 planes[g, q][:, u, :].bitcast(U32),
-                tables[g][:, u, :].bitcast(U32).indirect(offs_t[:, q * SQ // 16 : (q + 1) * SQ // 16]),
+                window.bitcast(U32).indirect(offs_t[:, q * SQ // 16 : (q + 1) * SQ // 16]),
             )
 
         grouped = {}
 
-        def interleave(g, q, on_vector=False):
-            t = ring.tile([P, 4 * SQ], BF16, name="grouped", tag="grouped", bufs=4, align_bytes=64)
-            dst = t[:].bitcast(F32).rearrange("p (n u) -> p n u", u=2)
+        def interleave(g, q, tag="grouped", bufs=3, t=None):
+            if t is None:
+                t = ring.tile([P, 4 * SQ], BF16, name="grouped", tag=tag, bufs=bufs, align_bytes=64)[:]
+            dst = t.bitcast(F32).rearrange("p (n u) -> p n u", u=2)
             src = planes[g, q][:].rearrange("p u m -> p (u m)").bitcast(F32).rearrange("p (u n) -> p n u", u=2)
-            if on_vector:
-                nc.vector.tensor_copy(dst, src)
-            else:
-                nc.scalar.copy(dst, src)
+            nc.scalar.copy(dst, src)
             grouped[g, q] = t
 
         def quantise_slots(g, q):
             cols = slice(q * SQ, (q + 1) * SQ)
-            nc.vector.quantize_mx(out=sc[:, g, cols].bitcast(FP8X4), scales=ss[:, g, cols], in_=grouped[g, q][:])
+            nc.vector.quantize_mx(out=sc[:, g, cols].bitcast(FP8X4), scales=ss[:, g, cols], in_=grouped[g, q])
 
         wgrouped = {}
+        raws = {}
 
-        def load_and_cast_w(e0, n, split):
-            raw = raw_tile("wraw", n * 4 * N)
+        def load_w(e0, n):
+            raw = raw_tile("wraw", n * 4 * N, "chain", 1) if e0 in CHAIN else raw_tile("wraw", n * 4 * N)
+            raws[e0] = raw
             halves = raw[:].rearrange("p a b -> p (a b)").rearrange("p (e g m) -> p e g m", g=G, m=4 * N)
             nc.sync.dma_start(halves.rearrange("p e g (j n) -> p e g j n", j=4), w_view[:, e0 : e0 + n])
-            t = ring.tile([P, n, G * 4 * N], BF16, name="wgrouped", tag="wgrouped", bufs=8, align_bytes=64)
+            return halves
+
+        def load_and_cast_w(e0, n, split, t=None):
+            halves = load_w(e0, n)
+            if t is None:
+                t = ring.tile([P, n, G * 4 * N], BF16, name="wgrouped", tag="wgrouped", bufs=5, align_bytes=64)[:]
             for k in range(0, n, split):
                 dst = t[:, k : k + split, :].rearrange("p e (a c i t) -> p (e a) c t i", c=N // 4, i=4, t=4)
                 src = halves[:, k : k + split].rearrange("p e g (t c i) -> p (e g) c t i", t=4, i=4)
-                if e0 in W_GPSIMD:
-                    dst = t[:, k : k + split, :].rearrange("p e (a n t) -> p (e a) n t", n=N, t=4)
-                    src = halves[:, k : k + split].rearrange("p e g (t n) -> p (e g) n t", t=4)
-                    for a in range(split * G):
-                        nc.gpsimd.tensor_scalar(dst[:, a], src[:, a], 1.0, 0.0, MULT, ADD)
-                else:
-                    nc.scalar.copy(dst, src)
-            wgrouped[e0] = t
+                nc.scalar.copy(dst, src)
+            for k in range(n):
+                wgrouped[e0 + k] = (t, k)
 
-        def quantise_w(e0, n, k=0):
+        def load_and_cast_w_gpsimd(e0, n, tag):
+            t = ring.tile([P, n, G * 4 * N], BF16, name=tag, tag=tag, bufs=1, align_bytes=64)
+            for k in range(0, n, 2):
+                halves = load_w(e0 + k, min(2, n))
+                dst = t[:, k : k + min(2, n), :].rearrange("p e (a n t) -> p (e a) n t", n=N, t=4)
+                src = halves.rearrange("p e g (t n) -> p (e g) n t", t=4)
+                nc.gpsimd.tensor_scalar(dst, src, 1.0, 0.0, MULT, ADD)
+            for k in range(n):
+                wgrouped[e0 + k] = (t, k)
+
+        def quantise_w(e0, n):
+            t, k = wgrouped[e0]
             nc.vector.quantize_mx(
-                out=wc[:, e0 + k : e0 + k + n].rearrange("p e g n -> p (e g n)").bitcast(FP8X4),
-                scales=ws[:, e0 + k : e0 + k + n].rearrange("p e g n -> p (e g n)"),
-                in_=wgrouped[e0][:, k : k + n, :].rearrange("p e m -> p (e m)"),
+                out=wc[:, e0 : e0 + n].rearrange("p e g n -> p (e g n)").bitcast(FP8X4),
+                scales=ws[:, e0 : e0 + n].rearrange("p e g n -> p (e g n)"),
+                in_=t[:, k : k + n, :].rearrange("p e m -> p (e m)"),
             )
 
         def multiply(bank, e, codes, scales, cols):
@@ -130,96 +144,105 @@ def tile_moe_shr_lin_bias_kernel(tc, xT, w, b, gate, offs, pos1, pos2, out):
                     out=bank,
                     lhsT=wc[:, e, g, :].bitcast(FP8X4),
                     lhsT_scale=ws[:, e, g, :],
-                    rhs=codes[:, g, cols].bitcast(FP8X4),
-                    rhs_scale=scales[:, g, cols],
+                    rhs=codes[g][:, cols].bitcast(FP8X4),
+                    rhs_scale=scales[g][:, cols],
                     start=(g == 0),
                     stop=(g == G - 1),
                 )
 
-        def group_tokens(g, t0, n, on_vector):
-            t = ring.tile([P, 4 * n], BF16, name="xgrouped", tag="grouped", bufs=4, align_bytes=64)
+        def group_tokens(g, t0, n, tag="grouped", bufs=3):
+            t = ring.tile([P, 4 * n], BF16, name="xgrouped", tag=tag, bufs=bufs, align_bytes=64)
             dst = t[:].bitcast(F32).rearrange("p (n u) -> p n u", u=2)
             words = tables[g][:].rearrange("p u m -> p (u m)").bitcast(F32).rearrange("p (u n) -> p n u", u=2)
-            if on_vector:
-                nc.vector.tensor_copy(dst, words[:, t0 : t0 + n, :])
-            else:
-                nc.scalar.copy(dst, words[:, t0 : t0 + n, :])
+            nc.scalar.copy(dst, words[:, t0 : t0 + n, :])
             return t
 
         def quantise_tokens(t, g, t0, n):
             cols = slice(t0, t0 + n)
-            nc.vector.quantize_mx(out=xc[:, g, cols].bitcast(FP8X4), scales=xs[:, g, cols], in_=t[:])
+            nc.vector.quantize_mx(out=xc_pass[g][:, cols].bitcast(FP8X4), scales=xs_pass[g][:, cols], in_=t[:])
 
-        def token_steps(g, on_vector):
-            a = group_tokens(g, 0, 1024, on_vector)
-            c = group_tokens(g, 1024, 512, on_vector)
+        def token_steps(g):
+            a = group_tokens(g, 0, 1024)
+            c = group_tokens(g, 1024, 512, "held", 1)
             quantise_tokens(a, g, 0, 1024)
             quantise_tokens(c, g, 1024, 512)
 
-        def expert_bank(*experts):
-            bank = psum.tile([P, 4 * C], F32, name="bank", tag="bank", bufs=5)
+        def expert_bank(experts, on_vector=False):
+            e0, n = experts[0], len(experts)
+            bank = psum.tile([P, n, C], F32, name="bank", tag="bank", bufs=5)
             for k, e in enumerate(experts):
-                multiply(bank[:, k * C : (k + 1) * C], e, sc, ss, slice(e * C, (e + 1) * C))
-            for k, e in enumerate(experts):
-                nc.scalar.activation(
-                    y[:, e * C : (e + 1) * C], bank[:, k * C : (k + 1) * C], IDENTITY, bias=b_t[:, e : e + 1]
+                multiply(bank[:, k, :], e, sc_pass, ss_pass, slice(e * C, (e + 1) * C))
+            if on_vector:
+                nc.vector.tensor_tensor(
+                    y[:, e0 * C : (e0 + n) * C].rearrange("p (e c) -> p e c", c=C),
+                    bank[:],
+                    b_t[:, e0 : e0 + n].unsqueeze(2).broadcast_to([P, n, C]),
+                    ADD,
                 )
+            else:
+                for k, e in enumerate(experts):
+                    nc.scalar.activation(y[:, e * C : (e + 1) * C], bank[:, k, :], IDENTITY, bias=b_t[:, e : e + 1])
 
         load_and_cast_x(0, 0, 0, 1024, 512, "V")
-        load_and_cast_x(0, 0, 1024, 512, 256, "V")
-        load_and_cast_x(0, 1, 0, 768, 768, "S")
-        load_and_cast_x(0, 1, 768, 768, 768, "S")
+        load_and_cast_x(0, 0, 1024, 512, 256, "V", "chain", 1)
+        load_and_cast_x(0, 1, 0, 1024, 512, "S")
+        load_and_cast_x(0, 1, 1024, 512, 512, "S", "planes2", 1)
         for q in range(Q):
             gather(0, 0, q)
             gather(0, 1, q)
-        token_steps(0, False)
-        for e0 in (0, 2, 4):
-            load_and_cast_w(e0, 2, 2)
-        for q in range(Q):
-            interleave(0, q)
-        for u in range(2):
-            load_and_cast_x(1, u, 0, 768, 768, "S")
-            load_and_cast_x(1, u, 768, 768, 768, "S")
+        load_and_cast_w_gpsimd(0, 4, "wa")
+        load_and_cast_w_gpsimd(4, 2, "wb")
+        token_steps(0)
+        interleave(0, 0)
+        interleave(0, 1)
+        load_and_cast_x(1, 0, 0, 768, 768, "S", "chain", 1)
+        load_and_cast_x(1, 0, 768, 768, 768, "S")
+        interleave(0, 2, "held", 1)
+        load_and_cast_x(1, 1, 0, 768, 768, "S")
+        load_and_cast_x(1, 1, 768, 768, 768, "S")
         nc.sync.dma_start(b_t[:], b)
         nc.sync.dma_start(pos1_t[:], pos1)
         nc.sync.dma_start(pos2_t[:], pos2)
-        for q in range(Q):
-            quantise_slots(0, q)
-            quantise_w(2 * q, 2)
+        quantise_w(0, 4)
+        quantise_slots(0, 0)
+        quantise_slots(0, 1)
+        quantise_w(4, 2)
+        quantise_slots(0, 2)
         for q in range(Q):
             gather(1, 0, q)
             gather(1, 1, q)
-        load_and_cast_w(6, 2, 2)
-        token_steps(1, False)
-        for e0 in (8, 10, 12):
-            load_and_cast_w(e0, 2, 2)
+        load_and_cast_w(10, 2, 2)
+        load_and_cast_w_gpsimd(6, 4, "held")
+        late = [group_tokens(1, 0, 1024, "wa", 1), group_tokens(1, 1024, 512, "tokens", 1)]
+        load_and_cast_w_gpsimd(12, 2, "wb")
         interleave(1, 0)
         load_and_cast_w(14, 2, 2)
+        load_and_cast_w_gpsimd(16, 2, "planes2")
+        load_and_cast_w_gpsimd(18, 2, "wc")
         interleave(1, 1)
-        load_and_cast_w(16, 2, 2)
-        interleave(1, 2, True)
-        for e0 in (6, 8, 10):
-            quantise_w(e0, 2)
-        for q in range(Q):
-            quantise_slots(1, q)
-            quantise_w(12 + 2 * q, 2)
-        y = ring.tile([P, S], F32, name="y", tag="t12", bufs=2, align_bytes=64)
-        load_and_cast_w(18, 2, 2)
-        quantise_w(18, 2)
-        expert_bank(0, 1, 12, 13)
-        expert_bank(2, 3, 14, 15)
-        load_and_cast_w(20, 2, 2)
-        quantise_w(20, 2)
-        expert_bank(4, 5, 16, 17)
-        expert_bank(6, 7, 18, 19)
-        load_and_cast_w(22, 2, 1)
-        quantise_w(E - 2, 1)
-        expert_bank(8, 9, 20, 21)
-        quantise_w(E - 2, 1, 1)
-        expert_bank(10, 11, 22)
-        expert_bank(23)
         load_and_cast_w(E, 1, 1)
+        load_and_cast_w(20, 2, 2)
+        load_and_cast_w(22, 2, 2)
+        interleave(1, 2, t=raws[22][:].rearrange("p a b -> p (a b)").bitcast(BF16))
+        y = ring.tile([P, S], F32, name="y", tag="table0", bufs=1, align_bytes=64)
+        quantise_slots(1, 0)
+        quantise_w(6, 4)
+        quantise_w(10, 2)
+        quantise_slots(1, 1)
+        for e0 in (12, 14, 16, 18):
+            quantise_w(e0, 2)
+        quantise_w(20, 2)
+        quantise_w(22, 2)
+        quantise_slots(1, 2)
+        xc_pass.append(ring.tile([P, T], U32, name="xc1", tag="chain", bufs=1, align_bytes=64))
+        xs_pass.append(ring.tile([P, T], U8, name="xs1", tag="wb", bufs=1, align_bytes=64))
+        for e0 in range(0, 16, 4):
+            expert_bank(range(e0, e0 + 4))
         quantise_w(E, 1)
+        quantise_tokens(late[0], 1, 0, 1024)
+        quantise_tokens(late[1], 1, 1024, 512)
+        expert_bank(range(16, 20), True)
+        expert_bank(range(20, 24), True)
         gates = []
         cuts = ((0, 1024), (1024, 1536))
         for t0, t1 in cuts:
@@ -229,40 +252,50 @@ def tile_moe_shr_lin_bias_kernel(tc, xT, w, b, gate, offs, pos1, pos2, out):
         shared = []
         for c in range(3):
             bank = psum.tile([P, 512], F32, name="shared%d" % c)
-            multiply(bank[:], E, xc, xs, slice(c * 512, (c + 1) * 512))
+            multiply(bank[:], E, xc_pass, xs_pass, slice(c * 512, (c + 1) * 512))
             shared.append(bank)
 
-        first = ring.tile([P, T], F32, name="first", tag="planes", bufs=4, align_bytes=64)
-        second = ring.tile([P, T], F32, name="second", tag="planes", bufs=4, align_bytes=64)
-        total = ring.tile([P, T], F32, name="total", tag="planes", bufs=4, align_bytes=64)
+        first = ring.tile([P, T], F32, name="first", tag="planes0", bufs=1, align_bytes=64)
+        second = ring.tile([P, T], F32, name="second", tag="planes1", bufs=1, align_bytes=64)
+        total = ring.tile([P, T], F32, name="total", tag="wa", bufs=1, align_bytes=64)
+        biased = ring.tile([P, T], F32, name="biased", tag="held", bufs=1, align_bytes=64)
+        turned = ring.tile([P, T], F32, name="turned", tag="planes2", bufs=1, align_bytes=64)
 
-        def fetch(dst, pos, r, k):
-            t0, t1 = cuts[k]
-            nc.vector.tensor_tensor(dst[:, t0:t1], y[:].indirect(pos[:, t0 // 16 : t1 // 16]), gates[k][:, r, :], MULT)
-
-        def add_shared(t0, t1):
-            c = t0 // 512
-            nc.vector.scalar_tensor_tensor(
-                out=total[:, t0:t1],
-                in0=shared[c][:, t0 - 512 * c : t1 - 512 * c],
-                scalar=b_t[:, E : E + 1],
-                in1=first[:, t0:t1],
-                op0=ADD,
-                op1=ADD,
+        def fetch(dst, pos, r, t0, t1):
+            k = t0 // 1024
+            nc.vector.tensor_tensor(
+                dst[:, t0:t1], y[:].indirect(pos[:, t0 // 16 : t1 // 16]), gates[k][:, r, t0 - 1024 * k : t1 - 1024 * k], MULT
             )
 
-        def add_second(t0, t1):
-            nc.vector.tensor_tensor(total[:, t0:t1], total[:, t0:t1], second[:, t0:t1], ADD)
+        sums = []
+        for c in range(3):
+            cols = slice(512 * c, 512 * (c + 1))
+            nc.scalar.activation(biased[:, cols], shared[c][:], IDENTITY, bias=b_t[:, E : E + 1])
+        for c in range(3):
+            fetch(first, pos1_t, 0, 512 * c, 512 * (c + 1))
+        for c in range(3):
+            cols = slice(512 * c, 512 * (c + 1))
+            across = psum.tile([P, 4, P], F32, name="across", tag="bank", bufs=5)
+            for j in range(4):
+                block = slice(512 * c + P * j, 512 * c + P * (j + 1))
+                nc.tensor.matmul(across[:, j, :], biased[:, block], ident[:], start=True, stop=False, is_transpose=True)
+                nc.tensor.matmul(across[:, j, :], first[:, block], ident[:], start=False, stop=True, is_transpose=True)
+            nc.scalar.copy(turned[:, cols], across[:].rearrange("p j n -> p (j n)"))
+            back = psum.tile([P, 4, P], F32, name="back", tag="bank", bufs=5)
+            for j in range(4):
+                nc.tensor.transpose(back[:, j, :], turned[:, 512 * c + P * j : 512 * c + P * (j + 1)], ident[:])
+            sums.append(back[:].rearrange("p j n -> p (j n)"))
+
+        def finish(t0, t1):
+            c = t0 // 512
+            nc.vector.tensor_tensor(total[:, t0:t1], sums[c][:, t0 - 512 * c : t1 - 512 * c], second[:, t0:t1], ADD)
             nc.sync.dma_start(out[:, t0:t1], total[:, t0:t1])
 
-        fetch(first, pos1_t, 0, 0)
-        fetch(second, pos2_t, 1, 0)
-        add_shared(0, 512)
-        add_shared(512, 1024)
-        fetch(first, pos1_t, 0, 1)
-        add_second(0, 1024)
-        fetch(second, pos2_t, 1, 1)
-        add_shared(1024, 1280)
-        add_shared(1280, 1536)
-        add_second(1024, 1280)
-        add_second(1280, 1536)
+        fetch(second, pos2_t, 1, 0, 512)
+        fetch(second, pos2_t, 1, 512, 1024)
+        finish(0, 512)
+        fetch(second, pos2_t, 1, 1024, 1280)
+        finish(512, 1024)
+        fetch(second, pos2_t, 1, 1280, 1536)
+        finish(1024, 1280)
+        finish(1280, 1536)

@@ -20,9 +20,8 @@ ADD = mybir.AluOpType.add
 MULT = mybir.AluOpType.mult
 IDENTITY = mybir.ActivationFunctionType.Identity
 
-PLANE_SLOTS = ("planes0", "planes1", "planes2", "planes1", "planes0", "table0")
-
-CHAIN = (8, 22)
+PIECES = (((0, 1024), (1024, 1024), (2048, 1024)), ((0, 1024), (1024, 1024), (2048, 512), (2560, 512)))
+PLANE_SLOTS = (("planes0", "planes1", "planes2"), ("planes1", "planes0", "planes3", "table0"))
 
 FLOPS = 2 * K * N * (S + T)
 
@@ -48,7 +47,6 @@ def tile_moe_shr_lin_bias_kernel(tc, xT, w, b, gate, offs, pos1, pos2, out):
         w_view = w.rearrange("e (g p j) n -> p e g j n", g=G, j=4)
         gate_view = gate.rearrange("r p t -> p r t")
 
-        nc.sync.dma_start(offs_t[:], offs)
         make_identity(nc, ident[:])
         sc_pass = [sc[:, g, :] for g in range(G)]
         ss_pass = [ss[:, g, :] for g in range(G)]
@@ -60,10 +58,10 @@ def tile_moe_shr_lin_bias_kernel(tc, xT, w, b, gate, offs, pos1, pos2, out):
             table = ring.tile([P, 2, 2 * T], BF16, name="table%d" % g, tag="table%d" % g, bufs=1, align_bytes=64)
             tables.append(table)
 
-        def raw_tile(name, width, tag="raw", bufs=5):
+        def raw_tile(name, width, tag="raw", bufs=6):
             return ring.tile([P, 2, width], F32, name=name, tag=tag, bufs=bufs, align_bytes=64)
 
-        def load_and_cast_x(g, u, t0, width, cut, engine, tag="raw", bufs=5):
+        def load_and_cast_x(g, u, t0, width, cut, engine, tag="raw", bufs=6):
             raw = raw_tile("xraw", width, tag, bufs)
             for c in range(0, width, cut):
                 nc.sync.dma_start(raw[:, :, c : c + cut], x_view[g, :, 2 * u : 2 * u + 2, t0 + c : t0 + c + cut])
@@ -73,37 +71,40 @@ def tile_moe_shr_lin_bias_kernel(tc, xT, w, b, gate, offs, pos1, pos2, out):
                     nc.vector.tensor_copy(dst, src)
                 else:
                     nc.scalar.copy(dst, src)
+            return raw
 
         planes = {}
 
         def gather(g, u, q):
+            s0, n = PIECES[g][q]
             if u == 0:
-                planes[g, q] = ring.tile([P, 2, 2 * SQ], BF16, name="planes", tag=PLANE_SLOTS[Q * g + q], bufs=1, align_bytes=64)
+                planes[g, q] = ring.tile([P, 2, 2 * n], BF16, name="planes", tag=PLANE_SLOTS[g][q], bufs=1, align_bytes=64)
             window = tables[g][:].rearrange("p u m -> p (u m)") if (g, u) == (1, 0) else tables[g][:, u, :]
             nc.vector.tensor_copy(
                 planes[g, q][:, u, :].bitcast(U32),
-                window.bitcast(U32).indirect(offs_t[:, q * SQ // 16 : (q + 1) * SQ // 16]),
+                window.bitcast(U32).indirect(offs_t[:, s0 // 16 : (s0 + n) // 16]),
             )
 
         grouped = {}
 
-        def interleave(g, q, tag="grouped", bufs=3, t=None):
+        def interleave(g, q, tag="grouped", bufs=2, t=None):
             if t is None:
-                t = ring.tile([P, 4 * SQ], BF16, name="grouped", tag=tag, bufs=bufs, align_bytes=64)[:]
+                t = ring.tile([P, 4 * PIECES[g][q][1]], BF16, name="grouped", tag=tag, bufs=bufs, align_bytes=64)[:]
             dst = t.bitcast(F32).rearrange("p (n u) -> p n u", u=2)
             src = planes[g, q][:].rearrange("p u m -> p (u m)").bitcast(F32).rearrange("p (u n) -> p n u", u=2)
             nc.scalar.copy(dst, src)
             grouped[g, q] = t
 
         def quantise_slots(g, q):
-            cols = slice(q * SQ, (q + 1) * SQ)
+            s0, n = PIECES[g][q]
+            cols = slice(s0, s0 + n)
             nc.vector.quantize_mx(out=sc[:, g, cols].bitcast(FP8X4), scales=ss[:, g, cols], in_=grouped[g, q])
 
         wgrouped = {}
         raws = {}
 
         def load_w(e0, n):
-            raw = raw_tile("wraw", n * 4 * N, "chain", 1) if e0 in CHAIN else raw_tile("wraw", n * 4 * N)
+            raw = raw_tile("wraw", n * 4 * N)
             raws[e0] = raw
             halves = raw[:].rearrange("p a b -> p (a b)").rearrange("p (e g m) -> p e g m", g=G, m=4 * N)
             nc.sync.dma_start(halves.rearrange("p e g (j n) -> p e g j n", j=4), w_view[:, e0 : e0 + n])
@@ -112,7 +113,7 @@ def tile_moe_shr_lin_bias_kernel(tc, xT, w, b, gate, offs, pos1, pos2, out):
         def load_and_cast_w(e0, n, split, t=None):
             halves = load_w(e0, n)
             if t is None:
-                t = ring.tile([P, n, G * 4 * N], BF16, name="wgrouped", tag="wgrouped", bufs=5, align_bytes=64)[:]
+                t = ring.tile([P, n, G * 4 * N], BF16, name="wgrouped", tag="wgrouped", bufs=3, align_bytes=64)[:]
             for k in range(0, n, split):
                 dst = t[:, k : k + split, :].rearrange("p e (a c i t) -> p (e a) c t i", c=N // 4, i=4, t=4)
                 src = halves[:, k : k + split].rearrange("p e g (t c i) -> p (e g) c t i", t=4, i=4)
@@ -120,11 +121,12 @@ def tile_moe_shr_lin_bias_kernel(tc, xT, w, b, gate, offs, pos1, pos2, out):
             for k in range(n):
                 wgrouped[e0 + k] = (t, k)
 
-        def load_and_cast_w_gpsimd(e0, n, tag):
-            t = ring.tile([P, n, G * 4 * N], BF16, name=tag, tag=tag, bufs=1, align_bytes=64)
-            for k in range(0, n, 2):
-                halves = load_w(e0 + k, min(2, n))
-                dst = t[:, k : k + min(2, n), :].rearrange("p e (a n t) -> p (e a) n t", n=N, t=4)
+        def load_and_cast_w_gpsimd(e0, n, tag, t=None, step=2):
+            if t is None:
+                t = ring.tile([P, n, G * 4 * N], BF16, name=tag, tag=tag, bufs=1, align_bytes=64)[:]
+            for k in range(0, n, step):
+                halves = load_w(e0 + k, step)
+                dst = t[:, k : k + step, :].rearrange("p e (a n t) -> p (e a) n t", n=N, t=4)
                 src = halves.rearrange("p e g (t n) -> p (e g) n t", t=4)
                 nc.gpsimd.tensor_scalar(dst, src, 1.0, 0.0, MULT, ADD)
             for k in range(n):
@@ -150,7 +152,7 @@ def tile_moe_shr_lin_bias_kernel(tc, xT, w, b, gate, offs, pos1, pos2, out):
                     stop=(g == G - 1),
                 )
 
-        def group_tokens(g, t0, n, tag="grouped", bufs=3):
+        def group_tokens(g, t0, n, tag="grouped", bufs=2):
             t = ring.tile([P, 4 * n], BF16, name="xgrouped", tag=tag, bufs=bufs, align_bytes=64)
             dst = t[:].bitcast(F32).rearrange("p (n u) -> p n u", u=2)
             words = tables[g][:].rearrange("p u m -> p (u m)").bitcast(F32).rearrange("p (u n) -> p n u", u=2)
@@ -163,7 +165,7 @@ def tile_moe_shr_lin_bias_kernel(tc, xT, w, b, gate, offs, pos1, pos2, out):
 
         def token_steps(g):
             a = group_tokens(g, 0, 1024)
-            c = group_tokens(g, 1024, 512, "held", 1)
+            c = group_tokens(g, 1024, 512, "tokens", 1)
             quantise_tokens(a, g, 0, 1024)
             quantise_tokens(c, g, 1024, 512)
 
@@ -183,23 +185,27 @@ def tile_moe_shr_lin_bias_kernel(tc, xT, w, b, gate, offs, pos1, pos2, out):
                 for k, e in enumerate(experts):
                     nc.scalar.activation(y[:, e * C : (e + 1) * C], bank[:, k, :], IDENTITY, bias=b_t[:, e : e + 1])
 
-        load_and_cast_x(0, 0, 0, 1024, 512, "V")
-        load_and_cast_x(0, 0, 1024, 512, 256, "V", "chain", 1)
-        load_and_cast_x(0, 1, 0, 1024, 512, "S")
+        load_and_cast_x(0, 0, 0, 1024, 1024, "V")
+        load_and_cast_x(0, 0, 1024, 512, 512, "V")
+        nc.sync.dma_start(offs_t[:], offs)
+        load_and_cast_x(0, 1, 0, 1024, 512, "S", "held", 1)
         load_and_cast_x(0, 1, 1024, 512, 512, "S", "planes2", 1)
         for q in range(Q):
             gather(0, 0, q)
             gather(0, 1, q)
-        load_and_cast_w_gpsimd(0, 4, "wa")
-        load_and_cast_w_gpsimd(4, 2, "wb")
+        joint = ring.tile([P, 6, G * 4 * N], BF16, name="joint", tag="joint", bufs=1, align_bytes=64)
+        wa = ring.tile([P, 4, G * 4 * N], BF16, name="wa", tag="wa", bufs=1, align_bytes=64)
+        load_and_cast_w_gpsimd(0, 2, None, wa[:], 1)
+        load_and_cast_w_gpsimd(2, 2, None, wa[:, 2:4, :])
+        load_and_cast_w_gpsimd(4, 2, None, joint[:, 4:6, :])
         token_steps(0)
         interleave(0, 0)
-        interleave(0, 1)
-        load_and_cast_x(1, 0, 0, 768, 768, "S", "chain", 1)
-        load_and_cast_x(1, 0, 768, 768, 768, "S")
-        interleave(0, 2, "held", 1)
-        load_and_cast_x(1, 1, 0, 768, 768, "S")
-        load_and_cast_x(1, 1, 768, 768, 768, "S")
+        interleave(0, 1, t=joint[:, 0:4, :].rearrange("p e m -> p (e m)"))
+        load_and_cast_x(1, 0, 0, 1024, 1024, "S")
+        load_and_cast_x(1, 0, 1024, 512, 512, "S")
+        load_and_cast_x(1, 1, 0, 512, 512, "S")
+        raw = load_and_cast_x(1, 1, 512, 1024, 512, "S", "held", 1)
+        interleave(0, 2, t=raw[:].rearrange("p a b -> p (a b)").bitcast(BF16))
         nc.sync.dma_start(b_t[:], b)
         nc.sync.dma_start(pos1_t[:], pos1)
         nc.sync.dma_start(pos2_t[:], pos2)
@@ -207,35 +213,37 @@ def tile_moe_shr_lin_bias_kernel(tc, xT, w, b, gate, offs, pos1, pos2, out):
         quantise_slots(0, 0)
         quantise_slots(0, 1)
         quantise_w(4, 2)
-        quantise_slots(0, 2)
-        for q in range(Q):
+        for q in range(4):
             gather(1, 0, q)
             gather(1, 1, q)
-        load_and_cast_w(10, 2, 2)
-        load_and_cast_w_gpsimd(6, 4, "held")
+        quantise_slots(0, 2)
+        load_and_cast_w_gpsimd(6, 6, "joint")
         late = [group_tokens(1, 0, 1024, "wa", 1), group_tokens(1, 1024, 512, "tokens", 1)]
-        load_and_cast_w_gpsimd(12, 2, "wb")
         interleave(1, 0)
-        load_and_cast_w(14, 2, 2)
-        load_and_cast_w_gpsimd(16, 2, "planes2")
-        load_and_cast_w_gpsimd(18, 2, "wc")
+        twelve = ring.tile([P, 2, G * 4 * N], BF16, name="twelve", tag="wc", bufs=1, align_bytes=64)
+        load_and_cast_w(12, 2, 2, twelve[:])
+        load_and_cast_w_gpsimd(14, 2, "planes2")
         interleave(1, 1)
-        load_and_cast_w(E, 1, 1)
+        interleave(1, 2, "half", 1)
+        load_and_cast_w(16, 2, 2)
+        interleave(1, 3, t=raws[16][:, 0, :].bitcast(BF16))
+        load_and_cast_w(18, 2, 2)
         load_and_cast_w(20, 2, 2)
-        load_and_cast_w(22, 2, 2)
-        interleave(1, 2, t=raws[22][:].rearrange("p a b -> p (a b)").bitcast(BF16))
+        load_and_cast_w(22, 2, 2, raw[:, 0, :].bitcast(BF16).rearrange("p (e m) -> p e m", e=2))
+        load_and_cast_w(E, 1, 1)
         y = ring.tile([P, S], F32, name="y", tag="table0", bufs=1, align_bytes=64)
         quantise_slots(1, 0)
         quantise_w(6, 4)
-        quantise_w(10, 2)
         quantise_slots(1, 1)
-        for e0 in (12, 14, 16, 18):
+        for e0 in (10, 12, 14, 16):
             quantise_w(e0, 2)
+        quantise_slots(1, 2)
+        quantise_slots(1, 3)
+        quantise_w(18, 2)
         quantise_w(20, 2)
         quantise_w(22, 2)
-        quantise_slots(1, 2)
-        xc_pass.append(ring.tile([P, T], U32, name="xc1", tag="chain", bufs=1, align_bytes=64))
-        xs_pass.append(ring.tile([P, T], U8, name="xs1", tag="wb", bufs=1, align_bytes=64))
+        xc_pass.append(ring.tile([P, T], U32, name="xc1", tag="held", bufs=1, align_bytes=64))
+        xs_pass.append(ring.tile([P, T], U8, name="xs1", tag="planes1", bufs=1, align_bytes=64))
         for e0 in range(0, 16, 4):
             expert_bank(range(e0, e0 + 4))
         quantise_w(E, 1)
@@ -251,14 +259,14 @@ def tile_moe_shr_lin_bias_kernel(tc, xT, w, b, gate, offs, pos1, pos2, out):
             gates.append(t)
         shared = []
         for c in range(3):
-            bank = psum.tile([P, 512], F32, name="shared%d" % c)
+            bank = psum.tile([P, 512], F32, name="shared", tag="shared%d" % c, bufs=1)
             multiply(bank[:], E, xc_pass, xs_pass, slice(c * 512, (c + 1) * 512))
             shared.append(bank)
 
         first = ring.tile([P, T], F32, name="first", tag="planes0", bufs=1, align_bytes=64)
         second = ring.tile([P, T], F32, name="second", tag="planes1", bufs=1, align_bytes=64)
         total = ring.tile([P, T], F32, name="total", tag="wa", bufs=1, align_bytes=64)
-        biased = ring.tile([P, T], F32, name="biased", tag="held", bufs=1, align_bytes=64)
+        biased = ring.tile([P, T], F32, name="biased", tag="joint", bufs=1, align_bytes=64)
         turned = ring.tile([P, T], F32, name="turned", tag="planes2", bufs=1, align_bytes=64)
 
         def fetch(dst, pos, r, t0, t1):
@@ -275,7 +283,7 @@ def tile_moe_shr_lin_bias_kernel(tc, xT, w, b, gate, offs, pos1, pos2, out):
             fetch(first, pos1_t, 0, 512 * c, 512 * (c + 1))
         for c in range(3):
             cols = slice(512 * c, 512 * (c + 1))
-            across = psum.tile([P, 4, P], F32, name="across", tag="bank", bufs=5)
+            across = psum.tile([P, 4, P], F32, name="across", tag="shared%d" % c, bufs=1)
             for j in range(4):
                 block = slice(512 * c + P * j, 512 * c + P * (j + 1))
                 nc.tensor.matmul(across[:, j, :], biased[:, block], ident[:], start=True, stop=False, is_transpose=True)

@@ -61,8 +61,8 @@ def tile_moe_shr_lin_bias_kernel(tc, xT, w, b, gate, offs, pos1, pos2, out):
         def raw_tile(name, width, tag="raw", bufs=6):
             return ring.tile([P, 2, width], F32, name=name, tag=tag, bufs=bufs, align_bytes=64)
 
-        def load_and_cast_x(g, u, t0, width, cut, engine, tag="raw", bufs=6):
-            raw = raw_tile("xraw", width, tag, bufs)
+        def load_and_cast_x(g, u, t0, width, cut, engine, tag="raw", bufs=6, room=None):
+            raw = raw_tile("xraw", room or width, tag, bufs)
             for c in range(0, width, cut):
                 nc.sync.dma_start(raw[:, :, c : c + cut], x_view[g, :, 2 * u : 2 * u + 2, t0 + c : t0 + c + cut])
                 dst = tables[g][:, u, 2 * (t0 + c) : 2 * (t0 + c + cut)].rearrange("p (n e) -> p n e", e=2)
@@ -103,15 +103,18 @@ def tile_moe_shr_lin_bias_kernel(tc, xT, w, b, gate, offs, pos1, pos2, out):
         wgrouped = {}
         raws = {}
 
-        def load_w(e0, n):
+        def load_w(e0, n, cut):
             raw = raw_tile("wraw", n * 4 * N)
             raws[e0] = raw
             halves = raw[:].rearrange("p a b -> p (a b)").rearrange("p (e g m) -> p e g m", g=G, m=4 * N)
-            nc.sync.dma_start(halves.rearrange("p e g (j n) -> p e g j n", j=4), w_view[:, e0 : e0 + n])
+            for k in range(0, n, cut):
+                nc.sync.dma_start(
+                    halves[:, k : k + cut].rearrange("p e g (j n) -> p e g j n", j=4), w_view[:, e0 + k : e0 + k + cut]
+                )
             return halves
 
         def load_and_cast_w(e0, n, split, t=None):
-            halves = load_w(e0, n)
+            halves = load_w(e0, n, split)
             if t is None:
                 t = ring.tile([P, n, G * 4 * N], BF16, name="wgrouped", tag="wgrouped", bufs=3, align_bytes=64)[:]
             for k in range(0, n, split):
@@ -124,11 +127,12 @@ def tile_moe_shr_lin_bias_kernel(tc, xT, w, b, gate, offs, pos1, pos2, out):
         def load_and_cast_w_gpsimd(e0, n, tag, t=None, step=2):
             if t is None:
                 t = ring.tile([P, n, G * 4 * N], BF16, name=tag, tag=tag, bufs=1, align_bytes=64)[:]
-            for k in range(0, n, step):
-                halves = load_w(e0 + k, step)
-                dst = t[:, k : k + step, :].rearrange("p e (a n t) -> p (e a) n t", n=N, t=4)
-                src = halves.rearrange("p e g (t n) -> p (e g) n t", t=4)
-                nc.gpsimd.tensor_scalar(dst, src, 1.0, 0.0, MULT, ADD)
+            for k in range(0, n, 2):
+                halves = load_w(e0 + k, 2, step)
+                for m in range(0, 2, step):
+                    dst = t[:, k + m : k + m + step, :].rearrange("p e (a n t) -> p (e a) n t", n=N, t=4)
+                    src = halves[:, m : m + step].rearrange("p e g (t n) -> p (e g) n t", t=4)
+                    nc.gpsimd.tensor_scalar(dst, src, 1.0, 0.0, MULT, ADD)
             for k in range(n):
                 wgrouped[e0 + k] = (t, k)
 
@@ -203,8 +207,8 @@ def tile_moe_shr_lin_bias_kernel(tc, xT, w, b, gate, offs, pos1, pos2, out):
         interleave(0, 1, t=joint[:, 0:4, :].rearrange("p e m -> p (e m)"))
         load_and_cast_x(1, 0, 0, 1024, 1024, "S")
         load_and_cast_x(1, 0, 1024, 512, 512, "S")
-        load_and_cast_x(1, 1, 0, 512, 512, "S")
-        raw = load_and_cast_x(1, 1, 512, 1024, 512, "S", "held", 1)
+        load_and_cast_x(1, 1, 0, 1024, 1024, "S")
+        raw = load_and_cast_x(1, 1, 1024, 512, 512, "S", "held", 1, 1024)
         interleave(0, 2, t=raw[:].rearrange("p a b -> p (a b)").bitcast(BF16))
         nc.sync.dma_start(b_t[:], b)
         nc.sync.dma_start(pos1_t[:], pos1)
@@ -244,11 +248,12 @@ def tile_moe_shr_lin_bias_kernel(tc, xT, w, b, gate, offs, pos1, pos2, out):
         quantise_w(22, 2)
         xc_pass.append(ring.tile([P, T], U32, name="xc1", tag="held", bufs=1, align_bytes=64))
         xs_pass.append(ring.tile([P, T], U8, name="xs1", tag="planes1", bufs=1, align_bytes=64))
-        for e0 in range(0, 16, 4):
+        for e0 in range(0, 12, 4):
             expert_bank(range(e0, e0 + 4))
         quantise_w(E, 1)
         quantise_tokens(late[0], 1, 0, 1024)
         quantise_tokens(late[1], 1, 1024, 512)
+        expert_bank(range(12, 16), True)
         expert_bank(range(16, 20), True)
         expert_bank(range(20, 24), True)
         gates = []

@@ -128,8 +128,8 @@ def tile_moe_shr_lin_bias_kernel(tc, xT, w, b, gate, offs, pos1, pos2, out):
             if t is None:
                 t = ring.tile([P, n, G * 4 * N], BF16, name=tag, tag=tag, bufs=1, align_bytes=64)[:]
             for k in range(0, n, 2):
-                halves = load_w(e0 + k, 2, step)
-                for m in range(0, 2, step):
+                halves = load_w(e0 + k, min(2, n), step)
+                for m in range(0, min(2, n), step):
                     dst = t[:, k + m : k + m + step, :].rearrange("p e (a n t) -> p (e a) n t", n=N, t=4)
                     src = halves[:, m : m + step].rearrange("p e g (t n) -> p (e g) n t", t=4)
                     nc.gpsimd.tensor_scalar(dst, src, 1.0, 0.0, MULT, ADD)
@@ -221,26 +221,29 @@ def tile_moe_shr_lin_bias_kernel(tc, xT, w, b, gate, offs, pos1, pos2, out):
             gather(1, 0, q)
             gather(1, 1, q)
         quantise_slots(0, 2)
-        load_and_cast_w_gpsimd(6, 6, "joint")
+        middle = ring.tile([P, 8, G * 4 * N], BF16, name="middle", tag="joint", bufs=1, align_bytes=64)
+        load_and_cast_w_gpsimd(6, 6, None, middle[:])
         late = [group_tokens(1, 0, 1024, "wa", 1), group_tokens(1, 1024, 512, "tokens", 1)]
         interleave(1, 0)
-        twelve = ring.tile([P, 2, G * 4 * N], BF16, name="twelve", tag="wc", bufs=1, align_bytes=64)
-        load_and_cast_w(12, 2, 2, twelve[:])
-        load_and_cast_w_gpsimd(14, 2, "planes2")
+        load_and_cast_w(12, 2, 2, middle[:, 6:8, :])
+        wgrouped[10] = (middle[:], 4)
+        last = ring.tile([P, 2, G * 4 * N], BF16, name="last", tag="wgrouped", bufs=3, align_bytes=64)
+        load_and_cast_w_gpsimd(E, 1, None, last[:], 1)
+        later = ring.tile([P, 4, G * 4 * N], BF16, name="later", tag="planes2", bufs=1, align_bytes=64)
+        load_and_cast_w_gpsimd(14, 2, None, later[:])
         interleave(1, 1)
         interleave(1, 2, "half", 1)
-        load_and_cast_w(16, 2, 2)
+        load_and_cast_w(16, 2, 2, later[:, 2:4, :])
         interleave(1, 3, t=raws[16][:, 0, :].bitcast(BF16))
         load_and_cast_w(18, 2, 2)
         load_and_cast_w(20, 2, 2)
         load_and_cast_w(22, 2, 2, raw[:, 0, :].bitcast(BF16).rearrange("p (e m) -> p e m", e=2))
-        load_and_cast_w(E, 1, 1)
         y = ring.tile([P, S], F32, name="y", tag="table0", bufs=1, align_bytes=64)
         quantise_slots(1, 0)
         quantise_w(6, 4)
         quantise_slots(1, 1)
-        for e0 in (10, 12, 14, 16):
-            quantise_w(e0, 2)
+        quantise_w(10, 4)
+        quantise_w(14, 4)
         quantise_slots(1, 2)
         quantise_slots(1, 3)
         quantise_w(18, 2)
@@ -248,13 +251,11 @@ def tile_moe_shr_lin_bias_kernel(tc, xT, w, b, gate, offs, pos1, pos2, out):
         quantise_w(22, 2)
         xc_pass.append(ring.tile([P, T], U32, name="xc1", tag="held", bufs=1, align_bytes=64))
         xs_pass.append(ring.tile([P, T], U8, name="xs1", tag="planes1", bufs=1, align_bytes=64))
-        for e0 in range(0, 12, 4):
+        for e0 in range(0, 20, 4):
             expert_bank(range(e0, e0 + 4))
         quantise_w(E, 1)
         quantise_tokens(late[0], 1, 0, 1024)
         quantise_tokens(late[1], 1, 1024, 512)
-        expert_bank(range(12, 16), True)
-        expert_bank(range(16, 20), True)
         expert_bank(range(20, 24), True)
         gates = []
         cuts = ((0, 1024), (1024, 1536))
@@ -304,11 +305,9 @@ def tile_moe_shr_lin_bias_kernel(tc, xT, w, b, gate, offs, pos1, pos2, out):
             nc.vector.tensor_tensor(total[:, t0:t1], sums[c][:, t0 - 512 * c : t1 - 512 * c], second[:, t0:t1], ADD)
             nc.sync.dma_start(out[:, t0:t1], total[:, t0:t1])
 
-        fetch(second, pos2_t, 1, 0, 512)
-        fetch(second, pos2_t, 1, 512, 1024)
+        fetch(second, pos2_t, 1, 0, 1024)
+        fetch(second, pos2_t, 1, 1024, 1536)
         finish(0, 512)
-        fetch(second, pos2_t, 1, 1024, 1280)
         finish(512, 1024)
-        fetch(second, pos2_t, 1, 1280, 1536)
         finish(1024, 1280)
         finish(1280, 1536)

@@ -251,11 +251,12 @@ def tile_moe_shr_lin_bias_kernel(tc, xT, w, b, gate, offs, pos1, pos2, out):
         quantise_w(22, 2)
         xc_pass.append(ring.tile([P, T], U32, name="xc1", tag="held", bufs=1, align_bytes=64))
         xs_pass.append(ring.tile([P, T], U8, name="xs1", tag="planes1", bufs=1, align_bytes=64))
-        for e0 in range(0, 20, 4):
+        for e0 in range(0, 16, 4):
             expert_bank(range(e0, e0 + 4))
         quantise_w(E, 1)
         quantise_tokens(late[0], 1, 0, 1024)
         quantise_tokens(late[1], 1, 1024, 512)
+        expert_bank(range(16, 20), True)
         expert_bank(range(20, 24), True)
         gates = []
         cuts = ((0, 1024), (1024, 1536))
@@ -285,29 +286,27 @@ def tile_moe_shr_lin_bias_kernel(tc, xT, w, b, gate, offs, pos1, pos2, out):
         for c in range(3):
             cols = slice(512 * c, 512 * (c + 1))
             nc.scalar.activation(biased[:, cols], shared[c][:], IDENTITY, bias=b_t[:, E : E + 1])
-        for c in range(3):
-            fetch(first, pos1_t, 0, 512 * c, 512 * (c + 1))
-        for c in range(3):
-            cols = slice(512 * c, 512 * (c + 1))
-            across = psum.tile([P, 4, P], F32, name="across", tag="shared%d" % c, bufs=1)
-            for j in range(4):
-                block = slice(512 * c + P * j, 512 * c + P * (j + 1))
+        for t0, t1 in ((0, 256), (256, 512), (512, 1024), (1024, 1536)):
+            fetch(first, pos1_t, 0, t0, t1)
+        ends = ((0, 512), (512, 1024), (1024, 1280), (1280, 1536))
+        for t0, t1 in ends:
+            blocks = (t1 - t0) // P
+            across = psum.tile([P, blocks, P], F32, name="across", tag="bank", bufs=5)
+            for j in range(blocks):
+                block = slice(t0 + P * j, t0 + P * (j + 1))
                 nc.tensor.matmul(across[:, j, :], biased[:, block], ident[:], start=True, stop=False, is_transpose=True)
                 nc.tensor.matmul(across[:, j, :], first[:, block], ident[:], start=False, stop=True, is_transpose=True)
-            nc.scalar.copy(turned[:, cols], across[:].rearrange("p j n -> p (j n)"))
-            back = psum.tile([P, 4, P], F32, name="back", tag="bank", bufs=5)
-            for j in range(4):
-                nc.tensor.transpose(back[:, j, :], turned[:, 512 * c + P * j : 512 * c + P * (j + 1)], ident[:])
+            nc.scalar.copy(turned[:, t0:t1], across[:].rearrange("p j n -> p (j n)"))
+            if t0 % 512 == 0:
+                back = psum.tile([P, blocks, P], F32, name="back", tag="shared%d" % (t0 // 512), bufs=1)
+            else:
+                back = psum.tile([P, blocks, P], F32, name="back", tag="bank", bufs=5)
+            for j in range(blocks):
+                nc.tensor.transpose(back[:, j, :], turned[:, t0 + P * j : t0 + P * (j + 1)], ident[:])
             sums.append(back[:].rearrange("p j n -> p (j n)"))
-
-        def finish(t0, t1):
-            c = t0 // 512
-            nc.vector.tensor_tensor(total[:, t0:t1], sums[c][:, t0 - 512 * c : t1 - 512 * c], second[:, t0:t1], ADD)
-            nc.sync.dma_start(out[:, t0:t1], total[:, t0:t1])
 
         fetch(second, pos2_t, 1, 0, 1024)
         fetch(second, pos2_t, 1, 1024, 1536)
-        finish(0, 512)
-        finish(512, 1024)
-        finish(1024, 1280)
-        finish(1280, 1536)
+        for (t0, t1), summed in zip(ends, sums):
+            nc.vector.tensor_tensor(total[:, t0:t1], summed, second[:, t0:t1], ADD)
+            nc.sync.dma_start(out[:, t0:t1], total[:, t0:t1])

@@ -118,8 +118,8 @@ def tile_moe_shr_lin_bias_kernel(tc, xT, w, b, gate, offs, pos1, pos2, out):
             if t is None:
                 t = ring.tile([P, n, G * 4 * N], BF16, name="wgrouped", tag="wgrouped", bufs=3, align_bytes=64)[:]
             for k in range(0, n, split):
-                dst = t[:, k : k + split, :].rearrange("p e (a c i t) -> p (e a) c t i", c=N // 4, i=4, t=4)
-                src = halves[:, k : k + split].rearrange("p e g (t c i) -> p (e g) c t i", t=4, i=4)
+                dst = t[:, k : k + split, :].rearrange("p e (a c i t) -> p (e a) c t i", c=N // 2, i=2, t=4)
+                src = halves[:, k : k + split].rearrange("p e g (t c i) -> p (e g) c t i", t=4, i=2)
                 nc.scalar.copy(dst, src)
             for k in range(n):
                 wgrouped[e0 + k] = (t, k)

@@ -23,6 +23,8 @@ IDENTITY = mybir.ActivationFunctionType.Identity
 PIECES = (((0, 1024), (1024, 1024), (2048, 1024)), ((0, 1024), (1024, 1024), (2048, 512), (2560, 512)))
 PLANE_SLOTS = (("planes0", "planes1", "planes2"), ("planes1", "planes0", "planes3", "table0"))
 
+SCALAR_HEAD_TOKENS = 160
+
 FLOPS = 2 * K * N * (S + T)
 
 
@@ -68,7 +70,9 @@ def tile_moe_shr_lin_bias_kernel(tc, xT, w, b, gate, offs, pos1, pos2, out):
                 dst = tables[g][:, u, 2 * (t0 + c) : 2 * (t0 + c + cut)].rearrange("p (n e) -> p n e", e=2)
                 src = raw[:, :, c : c + cut].rearrange("p e n -> p n e")
                 if engine == "V":
-                    nc.vector.tensor_copy(dst, src)
+                    share = cut - SCALAR_HEAD_TOKENS
+                    nc.vector.tensor_copy(dst[:, :share, :], src[:, :share, :])
+                    nc.scalar.copy(dst[:, share:, :], src[:, share:, :])
                 else:
                     nc.scalar.copy(dst, src)
             return raw
@@ -113,14 +117,17 @@ def tile_moe_shr_lin_bias_kernel(tc, xT, w, b, gate, offs, pos1, pos2, out):
                 )
             return halves
 
-        def load_and_cast_w(e0, n, split, t=None):
-            halves = load_w(e0, n, split)
+        def load_and_cast_w(e0, n, split, t=None, on_vector=()):
+            halves = load_w(e0, n, n)
             if t is None:
                 t = ring.tile([P, n, G * 4 * N], BF16, name="wgrouped", tag="wgrouped", bufs=3, align_bytes=64)[:]
             for k in range(0, n, split):
                 dst = t[:, k : k + split, :].rearrange("p e (a c i t) -> p (e a) c t i", c=N // 2, i=2, t=4)
                 src = halves[:, k : k + split].rearrange("p e g (t c i) -> p (e g) c t i", t=4, i=2)
-                nc.scalar.copy(dst, src)
+                if e0 + k in on_vector:
+                    nc.vector.tensor_copy(dst, src)
+                else:
+                    nc.scalar.copy(dst, src)
             for k in range(n):
                 wgrouped[e0 + k] = (t, k)
 
@@ -237,7 +244,7 @@ def tile_moe_shr_lin_bias_kernel(tc, xT, w, b, gate, offs, pos1, pos2, out):
         interleave(1, 3, t=raws[16][:, 0, :].bitcast(BF16))
         load_and_cast_w(18, 2, 2)
         load_and_cast_w(20, 2, 2)
-        load_and_cast_w(22, 2, 2, raw[:, 0, :].bitcast(BF16).rearrange("p (e m) -> p e m", e=2))
+        load_and_cast_w(22, 2, 1, raw[:, 0, :].bitcast(BF16).rearrange("p (e m) -> p e m", e=2), (23,))
         y = ring.tile([P, S], F32, name="y", tag="table0", bufs=1, align_bytes=64)
         quantise_slots(1, 0)
         quantise_w(6, 4)
@@ -256,8 +263,8 @@ def tile_moe_shr_lin_bias_kernel(tc, xT, w, b, gate, offs, pos1, pos2, out):
         quantise_w(E, 1)
         quantise_tokens(late[0], 1, 0, 1024)
         quantise_tokens(late[1], 1, 1024, 512)
-        expert_bank(range(16, 20), True)
-        expert_bank(range(20, 24), True)
+        expert_bank(range(16, 20))
+        expert_bank(range(20, 24))
         gates = []
         cuts = ((0, 1024), (1024, 1536))
         for t0, t1 in cuts:

@@ -244,7 +244,7 @@ def tile_moe_shr_lin_bias_kernel(tc, xT, w, b, gate, offs, pos1, pos2, out):
         interleave(1, 3, t=raws[16][:, 0, :].bitcast(BF16))
         load_and_cast_w(18, 2, 2)
         load_and_cast_w(20, 2, 2)
-        load_and_cast_w(22, 2, 1, raw[:, 0, :].bitcast(BF16).rearrange("p (e m) -> p e m", e=2), (23,))
+        load_and_cast_w(22, 2, 2, raw[:, 0, :].bitcast(BF16).rearrange("p (e m) -> p e m", e=2), (22,))
         y = ring.tile([P, S], F32, name="y", tag="table0", bufs=1, align_bytes=64)
         quantise_slots(1, 0)
         quantise_w(6, 4)

@@ -117,15 +117,25 @@ def tile_moe_shr_lin_bias_kernel(tc, xT, w, b, gate, offs, pos1, pos2, out):
                 )
             return halves
 
-        def load_and_cast_w(e0, n, split, t=None, on_vector=()):
+        def load_and_cast_w(e0, n, split, t=None, on_vector=(), on_gpsimd=()):
             halves = load_w(e0, n, n)
             if t is None:
                 t = ring.tile([P, n, G * 4 * N], BF16, name="wgrouped", tag="wgrouped", bufs=3, align_bytes=64)[:]
             for k in range(0, n, split):
-                dst = t[:, k : k + split, :].rearrange("p e (a c i t) -> p (e a) c t i", c=N // 2, i=2, t=4)
-                src = halves[:, k : k + split].rearrange("p e g (t c i) -> p (e g) c t i", t=4, i=2)
+                run = 4 if e0 + k in on_vector else 2
+                dst = t[:, k : k + split, :].rearrange("p e (a c i t) -> p (e a) c t i", c=N // run, i=run, t=4)
+                src = halves[:, k : k + split].rearrange("p e g (t c i) -> p (e g) c t i", t=4, i=run)
                 if e0 + k in on_vector:
                     nc.vector.tensor_copy(dst, src)
+                elif e0 + k in on_gpsimd:
+                    nc.gpsimd.tensor_scalar(
+                        t[:, k : k + split, :].rearrange("p e (a n t) -> p (e a) n t", n=N, t=4),
+                        halves[:, k : k + split].rearrange("p e g (t n) -> p (e g) n t", t=4),
+                        1.0,
+                        0.0,
+                        MULT,
+                        ADD,
+                    )
                 else:
                     nc.scalar.copy(dst, src)
             for k in range(n):
@@ -207,7 +217,7 @@ def tile_moe_shr_lin_bias_kernel(tc, xT, w, b, gate, offs, pos1, pos2, out):
         joint = ring.tile([P, 6, G * 4 * N], BF16, name="joint", tag="joint", bufs=1, align_bytes=64)
         wa = ring.tile([P, 4, G * 4 * N], BF16, name="wa", tag="wa", bufs=1, align_bytes=64)
         load_and_cast_w_gpsimd(0, 2, None, wa[:], 1)
-        load_and_cast_w_gpsimd(2, 2, None, wa[:, 2:4, :])
+        load_and_cast_w_gpsimd(2, 2, None, wa[:, 2:4, :], 1)
         load_and_cast_w_gpsimd(4, 2, None, joint[:, 4:6, :])
         token_steps(0)
         interleave(0, 0)
@@ -217,9 +227,6 @@ def tile_moe_shr_lin_bias_kernel(tc, xT, w, b, gate, offs, pos1, pos2, out):
         load_and_cast_x(1, 1, 0, 1024, 1024, "S")
         raw = load_and_cast_x(1, 1, 1024, 512, 512, "S", "held", 1, 1024)
         interleave(0, 2, t=raw[:].rearrange("p a b -> p (a b)").bitcast(BF16))
-        nc.sync.dma_start(b_t[:], b)
-        nc.sync.dma_start(pos1_t[:], pos1)
-        nc.sync.dma_start(pos2_t[:], pos2)
         quantise_w(0, 4)
         quantise_slots(0, 0)
         quantise_slots(0, 1)
@@ -229,13 +236,15 @@ def tile_moe_shr_lin_bias_kernel(tc, xT, w, b, gate, offs, pos1, pos2, out):
             gather(1, 1, q)
         quantise_slots(0, 2)
         middle = ring.tile([P, 8, G * 4 * N], BF16, name="middle", tag="joint", bufs=1, align_bytes=64)
-        load_and_cast_w_gpsimd(6, 6, None, middle[:])
+        load_and_cast_w_gpsimd(6, 2, None, middle[:], 1)
+        load_and_cast_w_gpsimd(8, 4, None, middle[:, 2:6, :])
+        nc.sync.dma_start(b_t[:], b)
+        nc.sync.dma_start(pos1_t[:], pos1)
+        nc.sync.dma_start(pos2_t[:], pos2)
         late = [group_tokens(1, 0, 1024, "wa", 1), group_tokens(1, 1024, 512, "tokens", 1)]
         interleave(1, 0)
-        load_and_cast_w(12, 2, 2, middle[:, 6:8, :])
+        load_and_cast_w(12, 2, 1, middle[:, 6:8, :], (), (12,))
         wgrouped[10] = (middle[:], 4)
-        last = ring.tile([P, 2, G * 4 * N], BF16, name="last", tag="wgrouped", bufs=3, align_bytes=64)
-        load_and_cast_w_gpsimd(E, 1, None, last[:], 1)
         later = ring.tile([P, 4, G * 4 * N], BF16, name="later", tag="planes2", bufs=1, align_bytes=64)
         load_and_cast_w_gpsimd(14, 2, None, later[:])
         interleave(1, 1)
@@ -244,7 +253,7 @@ def tile_moe_shr_lin_bias_kernel(tc, xT, w, b, gate, offs, pos1, pos2, out):
         interleave(1, 3, t=raws[16][:, 0, :].bitcast(BF16))
         load_and_cast_w(18, 2, 2)
         load_and_cast_w(20, 2, 2)
-        load_and_cast_w(22, 2, 2, raw[:, 0, :].bitcast(BF16).rearrange("p (e m) -> p e m", e=2), (22,))
+        load_and_cast_w(22, 2, 1, raw[:, 0, :].bitcast(BF16).rearrange("p (e m) -> p e m", e=2), (23,))
         y = ring.tile([P, S], F32, name="y", tag="table0", bufs=1, align_bytes=64)
         quantise_slots(1, 0)
         quantise_w(6, 4)
@@ -260,15 +269,16 @@ def tile_moe_shr_lin_bias_kernel(tc, xT, w, b, gate, offs, pos1, pos2, out):
         xs_pass.append(ring.tile([P, T], U8, name="xs1", tag="planes1", bufs=1, align_bytes=64))
         for e0 in range(0, 16, 4):
             expert_bank(range(e0, e0 + 4))
-        quantise_w(E, 1)
+        load_and_cast_w(E, 1, 1, None, (E,))
         quantise_tokens(late[0], 1, 0, 1024)
+        quantise_w(E, 1)
         quantise_tokens(late[1], 1, 1024, 512)
         expert_bank(range(16, 20))
         expert_bank(range(20, 24))
         gates = []
         cuts = ((0, 1024), (1024, 1536))
         for t0, t1 in cuts:
-            t = raw_tile("gates", t1 - t0)
+            t = raw_tile("gates", t1 - t0, "grouped", 2)
             nc.sync.dma_start(t[:], gate_view[:, :, t0:t1])
             gates.append(t)
         shared = []

@@ -7,8 +7,7 @@ P = 128
 K, T, E, C, N = 1024, 1536, 24, 128, 128
 S = E * C
 G = 2
-Q = 3
-SQ = S // Q
+GROUPED_W = G * 4 * N
 
 F32 = mybir.dt.float32
 BF16 = mybir.dt.bfloat16
@@ -21,9 +20,14 @@ MULT = mybir.AluOpType.mult
 IDENTITY = mybir.ActivationFunctionType.Identity
 
 PIECES = (((0, 1024), (1024, 1024), (2048, 1024)), ((0, 1024), (1024, 1024), (2048, 512), (2560, 512)))
-PLANE_SLOTS = (("planes0", "planes1", "planes2"), ("planes1", "planes0", "planes3", "table0"))
+PLANE_PLACES = (("planes0", "planes1", "planes2"), ("planes1", "planes0", "planes3", "table0"))
 
 SCALAR_HEAD_TOKENS = 160
+
+RAW_PLACES = 6
+BANK_RING = 5
+
+TENSOR_TOKENS = 512
 
 FLOPS = 2 * K * N * (S + T)
 
@@ -39,38 +43,33 @@ def tile_moe_shr_lin_bias_kernel(tc, xT, w, b, gate, offs, pos1, pos2, out):
         pos1_t = held.tile([P, T // 16], U16, name="pos1_t")
         pos2_t = held.tile([P, T // 16], U16, name="pos2_t")
         b_t = held.tile([P, E + 1], F32, name="b_t")
-        sc = held.tile([P, G, S], U32, name="sc", align_bytes=64)
-        ss = held.tile([P, G, S], U8, name="ss", align_bytes=64)
+        slot_codes = held.tile([P, G, S], U32, name="slot_codes", align_bytes=64)
+        slot_scales = held.tile([P, G, S], U8, name="slot_scales", align_bytes=64)
         ident = held.tile([P, P], F32, name="ident")
-        wc = held.tile([P, E + 1, G, N], U32, name="wc", align_bytes=64)
-        ws = held.tile([P, E + 1, G, N], U8, name="ws", align_bytes=64)
+        w_codes = held.tile([P, E + 1, G, N], U32, name="w_codes", align_bytes=64)
+        w_scales = held.tile([P, E + 1, G, N], U8, name="w_scales", align_bytes=64)
+        token_codes = [held.tile([P, T], U32, name="token_codes0", align_bytes=64)]
+        token_scales = [held.tile([P, T], U8, name="token_scales0", align_bytes=64)]
 
         x_view = xT.rearrange("(g p j) t -> g p j t", g=G, j=4)
         w_view = w.rearrange("e (g p j) n -> p e g j n", g=G, j=4)
         gate_view = gate.rearrange("r p t -> p r t")
 
         make_identity(nc, ident[:])
-        sc_pass = [sc[:, g, :] for g in range(G)]
-        ss_pass = [ss[:, g, :] for g in range(G)]
-        xc_pass = [held.tile([P, T], U32, name="xc0", align_bytes=64)]
-        xs_pass = [held.tile([P, T], U8, name="xs0", align_bytes=64)]
 
-        tables = []
-        for g in range(G):
-            table = ring.tile([P, 2, 2 * T], BF16, name="table%d" % g, tag="table%d" % g, bufs=1, align_bytes=64)
-            tables.append(table)
+        def place(name, shape, dtype, tag, bufs=1):
+            return ring.tile(shape, dtype, name=name, tag=tag, bufs=bufs, align_bytes=64)
 
-        def raw_tile(name, width, tag="raw", bufs=6):
-            return ring.tile([P, 2, width], F32, name=name, tag=tag, bufs=bufs, align_bytes=64)
+        tables = [place("table%d" % g, [P, 2, 2 * T], BF16, "table%d" % g) for g in range(G)]
 
-        def load_and_cast_x(g, u, t0, width, cut, engine, tag="raw", bufs=6, room=None):
-            raw = raw_tile("xraw", room or width, tag, bufs)
+        def load_and_cast_x(g, u, t0, width, cut, with_vector=False, tag="raw", bufs=RAW_PLACES, room=None):
+            raw = place("xraw", [P, 2, room or width], F32, tag, bufs)
             for c in range(0, width, cut):
                 nc.sync.dma_start(raw[:, :, c : c + cut], x_view[g, :, 2 * u : 2 * u + 2, t0 + c : t0 + c + cut])
                 dst = tables[g][:, u, 2 * (t0 + c) : 2 * (t0 + c + cut)].rearrange("p (n e) -> p n e", e=2)
                 src = raw[:, :, c : c + cut].rearrange("p e n -> p n e")
-                if engine == "V":
-                    share = cut - SCALAR_HEAD_TOKENS
+                if with_vector:
+                    share = cut - min(SCALAR_HEAD_TOKENS, cut * 5 // 16)
                     nc.vector.tensor_copy(dst[:, :share, :], src[:, :share, :])
                     nc.scalar.copy(dst[:, share:, :], src[:, share:, :])
                 else:
@@ -82,248 +81,245 @@ def tile_moe_shr_lin_bias_kernel(tc, xT, w, b, gate, offs, pos1, pos2, out):
         def gather(g, u, q):
             s0, n = PIECES[g][q]
             if u == 0:
-                planes[g, q] = ring.tile([P, 2, 2 * n], BF16, name="planes", tag=PLANE_SLOTS[g][q], bufs=1, align_bytes=64)
+                planes[g, q] = place("planes", [P, 2, 2 * n], BF16, PLANE_PLACES[g][q])
             window = tables[g][:].rearrange("p u m -> p (u m)") if (g, u) == (1, 0) else tables[g][:, u, :]
             nc.vector.tensor_copy(
                 planes[g, q][:, u, :].bitcast(U32),
                 window.bitcast(U32).indirect(offs_t[:, s0 // 16 : (s0 + n) // 16]),
             )
 
-        grouped = {}
+        def weave(dst, halves):
+            words = halves.rearrange("p u m -> p (u m)").bitcast(F32).rearrange("p (u n) -> p n u", u=2)
+            return dst.bitcast(F32).rearrange("p (n u) -> p n u", u=2), words
 
-        def interleave(g, q, tag="grouped", bufs=2, t=None):
-            if t is None:
-                t = ring.tile([P, 4 * PIECES[g][q][1]], BF16, name="grouped", tag=tag, bufs=bufs, align_bytes=64)[:]
-            dst = t.bitcast(F32).rearrange("p (n u) -> p n u", u=2)
-            src = planes[g, q][:].rearrange("p u m -> p (u m)").bitcast(F32).rearrange("p (u n) -> p n u", u=2)
-            nc.scalar.copy(dst, src)
-            grouped[g, q] = t
+        grouped_slots = {}
+
+        def group_slots(g, q, dst=None):
+            if dst is None:
+                dst = place("grouped", [P, 4 * PIECES[g][q][1]], BF16, "grouped", 2)[:]
+            nc.scalar.copy(*weave(dst, planes[g, q][:]))
+            grouped_slots[g, q] = dst
 
         def quantise_slots(g, q):
             s0, n = PIECES[g][q]
             cols = slice(s0, s0 + n)
-            nc.vector.quantize_mx(out=sc[:, g, cols].bitcast(FP8X4), scales=ss[:, g, cols], in_=grouped[g, q])
+            nc.vector.quantize_mx(
+                out=slot_codes[:, g, cols].bitcast(FP8X4), scales=slot_scales[:, g, cols], in_=grouped_slots[g, q]
+            )
 
-        wgrouped = {}
-        raws = {}
+        def group_tokens(g, t0, n, tag, bufs=1):
+            t = place("xgrouped", [P, 4 * n], BF16, tag, bufs)
+            dst, words = weave(t[:], tables[g][:])
+            nc.scalar.copy(dst, words[:, t0 : t0 + n, :])
+            return t
 
-        def load_w(e0, n, cut):
-            raw = raw_tile("wraw", n * 4 * N)
-            raws[e0] = raw
-            halves = raw[:].rearrange("p a b -> p (a b)").rearrange("p (e g m) -> p e g m", g=G, m=4 * N)
+        def quantise_tokens(t, g, t0, n):
+            cols = slice(t0, t0 + n)
+            nc.vector.quantize_mx(out=token_codes[g][:, cols].bitcast(FP8X4), scales=token_scales[g][:, cols], in_=t[:])
+
+        def load_and_cast_w(e0, engines, dst=None, single_loads=False):
+            n = len(engines)
+            raw = place("wraw", [P, 2, n * 4 * N], F32, "raw", RAW_PLACES)
+            rows = raw[:].rearrange("p a b -> p (a b)").rearrange("p (e g m) -> p e g m", g=G, m=4 * N)
+            cut = 1 if single_loads else n
             for k in range(0, n, cut):
                 nc.sync.dma_start(
-                    halves[:, k : k + cut].rearrange("p e g (j n) -> p e g j n", j=4), w_view[:, e0 + k : e0 + k + cut]
+                    rows[:, k : k + cut].rearrange("p e g (j n) -> p e g j n", j=4), w_view[:, e0 + k : e0 + k + cut]
                 )
-            return halves
-
-        def load_and_cast_w(e0, n, split, t=None, on_vector=(), on_gpsimd=()):
-            halves = load_w(e0, n, n)
-            if t is None:
-                t = ring.tile([P, n, G * 4 * N], BF16, name="wgrouped", tag="wgrouped", bufs=3, align_bytes=64)[:]
-            for k in range(0, n, split):
-                run = 4 if e0 + k in on_vector else 2
-                dst = t[:, k : k + split, :].rearrange("p e (a c i t) -> p (e a) c t i", c=N // run, i=run, t=4)
-                src = halves[:, k : k + split].rearrange("p e g (t c i) -> p (e g) c t i", t=4, i=run)
-                if e0 + k in on_vector:
-                    nc.vector.tensor_copy(dst, src)
-                elif e0 + k in on_gpsimd:
+            if dst is None:
+                dst = place("wgrouped", [P, n, GROUPED_W], BF16, "wgrouped", 3)[:]
+            step = n if len(set(engines)) == 1 and not single_loads else 1
+            for k in range(0, n, step):
+                if engines[k] == "G":
                     nc.gpsimd.tensor_scalar(
-                        t[:, k : k + split, :].rearrange("p e (a n t) -> p (e a) n t", n=N, t=4),
-                        halves[:, k : k + split].rearrange("p e g (t n) -> p (e g) n t", t=4),
+                        dst[:, k : k + step, :].rearrange("p e (a n t) -> p (e a) n t", n=N, t=4),
+                        rows[:, k : k + step].rearrange("p e g (t n) -> p (e g) n t", t=4),
                         1.0,
                         0.0,
                         MULT,
                         ADD,
                     )
                 else:
-                    nc.scalar.copy(dst, src)
-            for k in range(n):
-                wgrouped[e0 + k] = (t, k)
+                    run = 4 if engines[k] == "V" else 2
+                    to = dst[:, k : k + step, :].rearrange("p e (a c i t) -> p (e a) c t i", c=N // run, i=run, t=4)
+                    src = rows[:, k : k + step].rearrange("p e g (t c i) -> p (e g) c t i", t=4, i=run)
+                    if engines[k] == "V":
+                        nc.vector.tensor_copy(to, src)
+                    else:
+                        nc.scalar.copy(to, src)
+            return raw, dst
 
-        def load_and_cast_w_gpsimd(e0, n, tag, t=None, step=2):
-            if t is None:
-                t = ring.tile([P, n, G * 4 * N], BF16, name=tag, tag=tag, bufs=1, align_bytes=64)[:]
-            for k in range(0, n, 2):
-                halves = load_w(e0 + k, min(2, n), step)
-                for m in range(0, min(2, n), step):
-                    dst = t[:, k + m : k + m + step, :].rearrange("p e (a n t) -> p (e a) n t", n=N, t=4)
-                    src = halves[:, m : m + step].rearrange("p e g (t n) -> p (e g) n t", t=4)
-                    nc.gpsimd.tensor_scalar(dst, src, 1.0, 0.0, MULT, ADD)
-            for k in range(n):
-                wgrouped[e0 + k] = (t, k)
-
-        def quantise_w(e0, n):
-            t, k = wgrouped[e0]
+        def quantise_w(e0, grouped):
+            n = grouped.shape[1]
             nc.vector.quantize_mx(
-                out=wc[:, e0 : e0 + n].rearrange("p e g n -> p (e g n)").bitcast(FP8X4),
-                scales=ws[:, e0 : e0 + n].rearrange("p e g n -> p (e g n)"),
-                in_=t[:, k : k + n, :].rearrange("p e m -> p (e m)"),
+                out=w_codes[:, e0 : e0 + n].rearrange("p e g n -> p (e g n)").bitcast(FP8X4),
+                scales=w_scales[:, e0 : e0 + n].rearrange("p e g n -> p (e g n)"),
+                in_=grouped.rearrange("p e m -> p (e m)"),
             )
 
-        def multiply(bank, e, codes, scales, cols):
-            for g in range(G):
-                nc.tensor.matmul_mx(
-                    out=bank,
-                    lhsT=wc[:, e, g, :].bitcast(FP8X4),
-                    lhsT_scale=ws[:, e, g, :],
-                    rhs=codes[g][:, cols].bitcast(FP8X4),
-                    rhs_scale=scales[g][:, cols],
-                    start=(g == 0),
-                    stop=(g == G - 1),
-                )
+        def expert_bank(e0):
+            bank = psum.tile([P, 4, C], F32, name="bank", tag="bank", bufs=BANK_RING)
+            for k in range(4):
+                cols = slice((e0 + k) * C, (e0 + k + 1) * C)
+                for g in range(G):
+                    nc.tensor.matmul_mx(
+                        out=bank[:, k, :],
+                        lhsT=w_codes[:, e0 + k, g, :].bitcast(FP8X4),
+                        lhsT_scale=w_scales[:, e0 + k, g, :],
+                        rhs=slot_codes[:, g, cols].bitcast(FP8X4),
+                        rhs_scale=slot_scales[:, g, cols],
+                        start=(g == 0),
+                        stop=(g == G - 1),
+                    )
+            for k in range(4):
+                e = e0 + k
+                nc.scalar.activation(y[:, e * C : (e + 1) * C], bank[:, k, :], IDENTITY, bias=b_t[:, e : e + 1])
 
-        def group_tokens(g, t0, n, tag="grouped", bufs=2):
-            t = ring.tile([P, 4 * n], BF16, name="xgrouped", tag=tag, bufs=bufs, align_bytes=64)
-            dst = t[:].bitcast(F32).rearrange("p (n u) -> p n u", u=2)
-            words = tables[g][:].rearrange("p u m -> p (u m)").bitcast(F32).rearrange("p (u n) -> p n u", u=2)
-            nc.scalar.copy(dst, words[:, t0 : t0 + n, :])
-            return t
-
-        def quantise_tokens(t, g, t0, n):
-            cols = slice(t0, t0 + n)
-            nc.vector.quantize_mx(out=xc_pass[g][:, cols].bitcast(FP8X4), scales=xs_pass[g][:, cols], in_=t[:])
-
-        def token_steps(g):
-            a = group_tokens(g, 0, 1024)
-            c = group_tokens(g, 1024, 512, "tokens", 1)
-            quantise_tokens(a, g, 0, 1024)
-            quantise_tokens(c, g, 1024, 512)
-
-        def expert_bank(experts, on_vector=False):
-            e0, n = experts[0], len(experts)
-            bank = psum.tile([P, n, C], F32, name="bank", tag="bank", bufs=5)
-            for k, e in enumerate(experts):
-                multiply(bank[:, k, :], e, sc_pass, ss_pass, slice(e * C, (e + 1) * C))
-            if on_vector:
-                nc.vector.tensor_tensor(
-                    y[:, e0 * C : (e0 + n) * C].rearrange("p (e c) -> p e c", c=C),
-                    bank[:],
-                    b_t[:, e0 : e0 + n].unsqueeze(2).broadcast_to([P, n, C]),
-                    ADD,
-                )
-            else:
-                for k, e in enumerate(experts):
-                    nc.scalar.activation(y[:, e * C : (e + 1) * C], bank[:, k, :], IDENTITY, bias=b_t[:, e : e + 1])
-
-        load_and_cast_x(0, 0, 0, 1024, 1024, "V")
-        load_and_cast_x(0, 0, 1024, 512, 512, "V")
+        load_and_cast_x(0, 0, 0, 1024, 1024, with_vector=True)
+        load_and_cast_x(0, 0, 1024, 512, 256, with_vector=True)
         nc.sync.dma_start(offs_t[:], offs)
-        load_and_cast_x(0, 1, 0, 1024, 512, "S", "held", 1)
-        load_and_cast_x(0, 1, 1024, 512, 512, "S", "planes2", 1)
-        for q in range(Q):
+        load_and_cast_x(0, 1, 0, 1024, 512, tag="held", bufs=1)
+        load_and_cast_x(0, 1, 1024, 512, 512, tag="planes2", bufs=1)
+        for q in range(len(PIECES[0])):
             gather(0, 0, q)
             gather(0, 1, q)
-        joint = ring.tile([P, 6, G * 4 * N], BF16, name="joint", tag="joint", bufs=1, align_bytes=64)
-        wa = ring.tile([P, 4, G * 4 * N], BF16, name="wa", tag="wa", bufs=1, align_bytes=64)
-        load_and_cast_w_gpsimd(0, 2, None, wa[:], 1)
-        load_and_cast_w_gpsimd(2, 2, None, wa[:, 2:4, :], 1)
-        load_and_cast_w_gpsimd(4, 2, None, joint[:, 4:6, :])
-        token_steps(0)
-        interleave(0, 0)
-        interleave(0, 1, t=joint[:, 0:4, :].rearrange("p e m -> p (e m)"))
-        load_and_cast_x(1, 0, 0, 1024, 1024, "S")
-        load_and_cast_x(1, 0, 1024, 512, 512, "S")
-        load_and_cast_x(1, 1, 0, 1024, 1024, "S")
-        raw = load_and_cast_x(1, 1, 1024, 512, 512, "S", "held", 1, 1024)
-        interleave(0, 2, t=raw[:].rearrange("p a b -> p (a b)").bitcast(BF16))
-        quantise_w(0, 4)
+
+        joint = place("joint", [P, 6, GROUPED_W], BF16, "joint")
+        early = place("early", [P, 4, GROUPED_W], BF16, "wa")
+        load_and_cast_w(0, "GG", early[:, 0:2, :], single_loads=True)
+        load_and_cast_w(2, "GG", early[:, 2:4, :], single_loads=True)
+        load_and_cast_w(4, "GG", joint[:, 4:6, :])
+        tokens_a = group_tokens(0, 0, 1024, "grouped", 2)
+        tokens_b = group_tokens(0, 1024, 512, "tokens")
+        quantise_tokens(tokens_a, 0, 0, 1024)
+        quantise_tokens(tokens_b, 0, 1024, 512)
+        group_slots(0, 0)
+        group_slots(0, 1, joint[:, 0:4, :].rearrange("p e m -> p (e m)"))
+        load_and_cast_x(1, 0, 0, 1024, 1024)
+        load_and_cast_x(1, 0, 1024, 512, 512)
+        load_and_cast_x(1, 1, 0, 1024, 1024)
+        reused = load_and_cast_x(1, 1, 1024, 512, 512, tag="held", bufs=1, room=1024)
+        group_slots(0, 2, reused[:].rearrange("p a b -> p (a b)").bitcast(BF16))
+
+        quantise_w(0, early[:])
         quantise_slots(0, 0)
         quantise_slots(0, 1)
-        quantise_w(4, 2)
-        for q in range(4):
+        quantise_w(4, joint[:, 4:6, :])
+
+        for q in range(len(PIECES[1])):
             gather(1, 0, q)
             gather(1, 1, q)
         quantise_slots(0, 2)
-        middle = ring.tile([P, 8, G * 4 * N], BF16, name="middle", tag="joint", bufs=1, align_bytes=64)
-        load_and_cast_w_gpsimd(6, 2, None, middle[:], 1)
-        load_and_cast_w_gpsimd(8, 4, None, middle[:, 2:6, :])
+        middle = place("middle", [P, 8, GROUPED_W], BF16, "joint")
+        load_and_cast_w(6, "GG", middle[:, 0:2, :], single_loads=True)
+        load_and_cast_w(8, "GG", middle[:, 2:4, :])
+        load_and_cast_w(10, "GG", middle[:, 4:6, :])
         nc.sync.dma_start(b_t[:], b)
         nc.sync.dma_start(pos1_t[:], pos1)
         nc.sync.dma_start(pos2_t[:], pos2)
-        late = [group_tokens(1, 0, 1024, "wa", 1), group_tokens(1, 1024, 512, "tokens", 1)]
-        interleave(1, 0)
-        load_and_cast_w(12, 2, 1, middle[:, 6:8, :], (), (12,))
-        wgrouped[10] = (middle[:], 4)
-        later = ring.tile([P, 4, G * 4 * N], BF16, name="later", tag="planes2", bufs=1, align_bytes=64)
-        load_and_cast_w_gpsimd(14, 2, None, later[:])
-        interleave(1, 1)
-        interleave(1, 2, "half", 1)
-        load_and_cast_w(16, 2, 2, later[:, 2:4, :])
-        interleave(1, 3, t=raws[16][:, 0, :].bitcast(BF16))
-        load_and_cast_w(18, 2, 2)
-        load_and_cast_w(20, 2, 2)
-        load_and_cast_w(22, 2, 1, raw[:, 0, :].bitcast(BF16).rearrange("p (e m) -> p e m", e=2), (23,))
-        y = ring.tile([P, S], F32, name="y", tag="table0", bufs=1, align_bytes=64)
+        late_a = group_tokens(1, 0, 1024, "wa")
+        late_b = group_tokens(1, 1024, 512, "tokens")
+        group_slots(1, 0)
+        load_and_cast_w(12, "GS", middle[:, 6:8, :])
+        later = place("later", [P, 4, GROUPED_W], BF16, "planes2")
+        load_and_cast_w(14, "GG", later[:, 0:2, :])
+        group_slots(1, 1)
+        group_slots(1, 2, place("grouped", [P, 4 * PIECES[1][2][1]], BF16, "half")[:])
+        raw16 = load_and_cast_w(16, "SS", later[:, 2:4, :])[0]
+        group_slots(1, 3, raw16[:, 0, :].bitcast(BF16))
+        grouped18 = load_and_cast_w(18, "SS")[1]
+        grouped20 = load_and_cast_w(20, "SS")[1]
+        grouped22 = load_and_cast_w(22, "SV", reused[:, 0, :].bitcast(BF16).rearrange("p (e m) -> p e m", e=2))[1]
+
+        y = place("y", [P, S], F32, "table0")
         quantise_slots(1, 0)
-        quantise_w(6, 4)
+        quantise_w(6, middle[:, 0:4, :])
         quantise_slots(1, 1)
-        quantise_w(10, 4)
-        quantise_w(14, 4)
+        quantise_w(10, middle[:, 4:8, :])
+        quantise_w(14, later[:])
         quantise_slots(1, 2)
         quantise_slots(1, 3)
-        quantise_w(18, 2)
-        quantise_w(20, 2)
-        quantise_w(22, 2)
-        xc_pass.append(ring.tile([P, T], U32, name="xc1", tag="held", bufs=1, align_bytes=64))
-        xs_pass.append(ring.tile([P, T], U8, name="xs1", tag="planes1", bufs=1, align_bytes=64))
+        quantise_w(18, grouped18)
+        quantise_w(20, grouped20)
+        quantise_w(22, grouped22)
+        token_codes.append(place("token_codes1", [P, T], U32, "held"))
+        token_scales.append(place("token_scales1", [P, T], U8, "planes1"))
         for e0 in range(0, 16, 4):
-            expert_bank(range(e0, e0 + 4))
-        load_and_cast_w(E, 1, 1, None, (E,))
-        quantise_tokens(late[0], 1, 0, 1024)
-        quantise_w(E, 1)
-        quantise_tokens(late[1], 1, 1024, 512)
-        expert_bank(range(16, 20))
-        expert_bank(range(20, 24))
+            expert_bank(e0)
+        grouped_shared = load_and_cast_w(E, "V")[1]
+        quantise_tokens(late_a, 1, 0, 1024)
+        quantise_w(E, grouped_shared)
+        quantise_tokens(late_b, 1, 1024, 512)
+        expert_bank(16)
+        expert_bank(20)
+
         gates = []
-        cuts = ((0, 1024), (1024, 1536))
-        for t0, t1 in cuts:
-            t = raw_tile("gates", t1 - t0, "grouped", 2)
+        for t0, t1 in ((0, 1024), (1024, T)):
+            t = place("gates", [P, 2, t1 - t0], F32, "grouped", 2)
             nc.sync.dma_start(t[:], gate_view[:, :, t0:t1])
             gates.append(t)
-        shared = []
-        for c in range(3):
-            bank = psum.tile([P, 512], F32, name="shared", tag="shared%d" % c, bufs=1)
-            multiply(bank[:], E, xc_pass, xs_pass, slice(c * 512, (c + 1) * 512))
-            shared.append(bank)
+        first = place("first", [P, T], F32, "planes0")
+        second = place("second", [P, T], F32, "planes1")
+        total = place("total", [P, T], F32, "wa")
+        shared_turned = place("shared_turned", [P, T], F32, "joint")
+        routed_turned = place("routed_turned", [P, T], F32, "planes2")
 
-        first = ring.tile([P, T], F32, name="first", tag="planes0", bufs=1, align_bytes=64)
-        second = ring.tile([P, T], F32, name="second", tag="planes1", bufs=1, align_bytes=64)
-        total = ring.tile([P, T], F32, name="total", tag="wa", bufs=1, align_bytes=64)
-        biased = ring.tile([P, T], F32, name="biased", tag="joint", bufs=1, align_bytes=64)
-        turned = ring.tile([P, T], F32, name="turned", tag="planes2", bufs=1, align_bytes=64)
+        for c in (1, 2, 0):
+            bank = psum.tile([P, 4, N], F32, name="shared", tag="shared%d" % c, bufs=1)
+            for j in range(4):
+                cols = slice(512 * c + P * j, 512 * c + P * (j + 1))
+                for g in range(G):
+                    nc.tensor.matmul_mx(
+                        out=bank[:, j, :],
+                        lhsT=token_codes[g][:, cols].bitcast(FP8X4),
+                        lhsT_scale=token_scales[g][:, cols],
+                        rhs=w_codes[:, E, g, :].bitcast(FP8X4),
+                        rhs_scale=w_scales[:, E, g, :],
+                        start=(g == 0),
+                        stop=(g == G - 1),
+                    )
+            nc.scalar.copy(shared_turned[:, 512 * c : 512 * (c + 1)], bank[:].rearrange("p j n -> p (j n)"))
 
-        def fetch(dst, pos, r, t0, t1):
+        def fetch(r, t0, t1):
             k = t0 // 1024
             nc.vector.tensor_tensor(
-                dst[:, t0:t1], y[:].indirect(pos[:, t0 // 16 : t1 // 16]), gates[k][:, r, t0 - 1024 * k : t1 - 1024 * k], MULT
+                (first, second)[r][:, t0:t1],
+                y[:].indirect((pos1_t, pos2_t)[r][:, t0 // 16 : t1 // 16]),
+                gates[k][:, r, t0 - 1024 * k : t1 - 1024 * k],
+                MULT,
             )
 
-        sums = []
-        for c in range(3):
-            cols = slice(512 * c, 512 * (c + 1))
-            nc.scalar.activation(biased[:, cols], shared[c][:], IDENTITY, bias=b_t[:, E : E + 1])
-        for t0, t1 in ((0, 256), (256, 512), (512, 1024), (1024, 1536)):
-            fetch(first, pos1_t, 0, t0, t1)
-        ends = ((0, 512), (512, 1024), (1024, 1280), (1280, 1536))
-        for t0, t1 in ends:
-            blocks = (t1 - t0) // P
-            across = psum.tile([P, blocks, P], F32, name="across", tag="bank", bufs=5)
-            for j in range(blocks):
-                block = slice(t0 + P * j, t0 + P * (j + 1))
-                nc.tensor.matmul(across[:, j, :], biased[:, block], ident[:], start=True, stop=False, is_transpose=True)
-                nc.tensor.matmul(across[:, j, :], first[:, block], ident[:], start=False, stop=True, is_transpose=True)
-            nc.scalar.copy(turned[:, t0:t1], across[:].rearrange("p j n -> p (j n)"))
-            if t0 % 512 == 0:
-                back = psum.tile([P, blocks, P], F32, name="back", tag="shared%d" % (t0 // 512), bufs=1)
-            else:
-                back = psum.tile([P, blocks, P], F32, name="back", tag="bank", bufs=5)
-            for j in range(blocks):
-                nc.tensor.transpose(back[:, j, :], turned[:, t0 + P * j : t0 + P * (j + 1)], ident[:])
-            sums.append(back[:].rearrange("p j n -> p (j n)"))
+        for t0, t1 in ((TENSOR_TOKENS, 768), (768, 1024), (1024, T), (0, TENSOR_TOKENS)):
+            fetch(0, t0, t1)
+        for t0, t1 in ((0, 256), (256, TENSOR_TOKENS), (TENSOR_TOKENS, 1024), (1024, T)):
+            fetch(1, t0, t1)
 
-        fetch(second, pos2_t, 1, 0, 1024)
-        fetch(second, pos2_t, 1, 1024, 1536)
-        for (t0, t1), summed in zip(ends, sums):
-            nc.vector.tensor_tensor(total[:, t0:t1], summed, second[:, t0:t1], ADD)
+        def turn(dst, terms):
+            for k, term in enumerate(terms):
+                nc.tensor.matmul(dst, term, ident[:], start=(k == 0), stop=(k == len(terms) - 1), is_transpose=True)
+
+        for_vector = []
+        for t0, t1 in ((TENSOR_TOKENS, 1024), (1024, 1280), (1280, T), (0, 256), (256, TENSOR_TOKENS)):
+            blocks = (t1 - t0) // P
+            on_tensor = t1 <= TENSOR_TOKENS
+            across = psum.tile([P, blocks, P], F32, name="across", tag="bank", bufs=BANK_RING)
+            for j in range(blocks):
+                cols = slice(t0 + P * j, t0 + P * (j + 1))
+                turn(across[:, j, :], [first[:, cols]] + ([second[:, cols]] if on_tensor else []))
+            nc.scalar.copy(routed_turned[:, t0:t1], across[:].rearrange("p j n -> p (j n)"))
+            if on_tensor:
+                back = psum.tile([P, blocks, P], F32, name="back", tag="bank", bufs=BANK_RING)
+            else:
+                back = psum.tile([P, blocks, P], F32, name="back", tag="shared%d" % ((len(for_vector) + 1) % 3), bufs=1)
+            for j in range(blocks):
+                cols = slice(t0 + P * j, t0 + P * (j + 1))
+                turn(back[:, j, :], [shared_turned[:, cols], routed_turned[:, cols]])
+            summed = back[:].rearrange("p j n -> p (j n)")
+            if on_tensor:
+                nc.scalar.activation(total[:, t0:t1], summed, IDENTITY, bias=b_t[:, E : E + 1])
+                nc.scalar.dma_start(out[:, t0:t1], total[:, t0:t1])
+            else:
+                for_vector.append((t0, t1, summed))
+        for t0, t1, summed in for_vector:
+            nc.vector.scalar_tensor_tensor(total[:, t0:t1], summed, b_t[:, E : E + 1], second[:, t0:t1], ADD, ADD)
             nc.sync.dma_start(out[:, t0:t1], total[:, t0:t1])

@@ -7,7 +7,8 @@ P = 128
 K, T, E, C, N = 1024, 1536, 24, 128, 128
 S = E * C
 G = 2
-GROUPED_W = G * 4 * N
+PIECE = 1024
+KB = 1024
 
 F32 = mybir.dt.float32
 BF16 = mybir.dt.bfloat16
@@ -18,16 +19,20 @@ FP8X4 = mybir.dt.float8_e4m3fn_x4
 ADD = mybir.AluOpType.add
 MULT = mybir.AluOpType.mult
 IDENTITY = mybir.ActivationFunctionType.Identity
+COPY = mybir.ActivationFunctionType.Copy
 
-PIECES = (((0, 1024), (1024, 1024), (2048, 1024)), ((0, 1024), (1024, 1024), (2048, 512), (2560, 512)))
-PLANE_PLACES = (("planes0", "planes1", "planes2"), ("planes1", "planes0", "planes3", "table0"))
+TABLES = 0
+PLANES = 24
+SLOT_CELLS = 48
+RESULT = 88
+WEIGHT_CELLS = 96
+TOKEN_CELLS = 146
+RAW = 170
+RAW_SLOTS = 16
 
 SCALAR_HEAD_TOKENS = 160
-
-RAW_PLACES = 6
-BANK_RING = 5
-
-TENSOR_TOKENS = 512
+GPSIMD_EXPERTS = 11
+SCALAR_EXPERTS_END = 21
 
 FLOPS = 2 * K * N * (S + T)
 
@@ -36,290 +41,280 @@ def tile_moe_shr_lin_bias_kernel(tc, xT, w, b, gate, offs, pos1, pos2, out):
     nc = tc.nc
     with ExitStack() as ctx:
         held = ctx.enter_context(tc.tile_pool(name="held", bufs=1))
-        ring = ctx.enter_context(tc.tile_pool(name="ring", bufs=1))
+        room = ctx.enter_context(tc.tile_pool(name="room", bufs=1))
         psum = ctx.enter_context(tc.psum_pool(name="psum", bufs=1))
 
         offs_t = held.tile([P, S // 16], U16, name="offs_t")
         pos1_t = held.tile([P, T // 16], U16, name="pos1_t")
         pos2_t = held.tile([P, T // 16], U16, name="pos2_t")
         b_t = held.tile([P, E + 1], F32, name="b_t")
-        slot_codes = held.tile([P, G, S], U32, name="slot_codes", align_bytes=64)
-        slot_scales = held.tile([P, G, S], U8, name="slot_scales", align_bytes=64)
+
         ident = held.tile([P, P], F32, name="ident")
-        w_codes = held.tile([P, E + 1, G, N], U32, name="w_codes", align_bytes=64)
-        w_scales = held.tile([P, E + 1, G, N], U8, name="w_scales", align_bytes=64)
-        token_codes = [held.tile([P, T], U32, name="token_codes0", align_bytes=64)]
-        token_scales = [held.tile([P, T], U8, name="token_scales0", align_bytes=64)]
+        gate_columns = held.tile([P, T // P], F32, name="gate_columns")
+        make_identity(nc, ident[:])
 
         x_view = xT.rearrange("(g p j) t -> g p j t", g=G, j=4)
         w_view = w.rearrange("e (g p j) n -> p e g j n", g=G, j=4)
-        gate_view = gate.rearrange("r p t -> p r t")
 
-        make_identity(nc, ident[:])
+        def at(name, shape, dtype, kib):
+            return room.tile(shape, dtype, name=name, offset=kib * KB, align_bytes=64)
 
-        def place(name, shape, dtype, tag, bufs=1):
-            return ring.tile(shape, dtype, name=name, tag=tag, bufs=bufs, align_bytes=64)
+        def raw_at(slot):
+            return RAW + 4 * (slot % RAW_SLOTS)
 
-        tables = [place("table%d" % g, [P, 2, 2 * T], BF16, "table%d" % g) for g in range(G)]
+        tables = [at("table%d" % g, [P, 2 * 2 * T], BF16, TABLES + 12 * g) for g in range(G)]
 
-        def load_and_cast_x(g, u, t0, width, cut, with_vector=False, tag="raw", bufs=RAW_PLACES, room=None):
-            raw = place("xraw", [P, 2, room or width], F32, tag, bufs)
+        def cast(engine, dst, src):
+            if engine == "V":
+                nc.vector.tensor_copy(dst, src)
+            elif engine == "S":
+                nc.scalar.copy(dst, src)
+            else:
+                nc.gpsimd.tensor_scalar(dst, src, 1.0, 0.0, MULT, ADD)
+
+        def load_x(g, u, t0, width, kib, shares, cut=None):
+            raw = at("x%d%d_%d" % (g, u, t0), [P, 2, width], F32, kib)
+            cut = cut or width
             for c in range(0, width, cut):
                 nc.sync.dma_start(raw[:, :, c : c + cut], x_view[g, :, 2 * u : 2 * u + 2, t0 + c : t0 + c + cut])
-                dst = tables[g][:, u, 2 * (t0 + c) : 2 * (t0 + c + cut)].rearrange("p (n e) -> p n e", e=2)
+                first = 2 * (u * T + t0 + c)
+                dst = tables[g][:, first : first + 2 * cut].rearrange("p (n e) -> p n e", e=2)
                 src = raw[:, :, c : c + cut].rearrange("p e n -> p n e")
-                if with_vector:
-                    share = cut - min(SCALAR_HEAD_TOKENS, cut * 5 // 16)
-                    nc.vector.tensor_copy(dst[:, :share, :], src[:, :share, :])
-                    nc.scalar.copy(dst[:, share:, :], src[:, share:, :])
-                else:
-                    nc.scalar.copy(dst, src)
-            return raw
+                a = 0
+                for engine, tokens in shares:
+                    cast(engine, dst[:, a : a + tokens, :], src[:, a : a + tokens, :])
+                    a = a + tokens
 
         planes = {}
 
         def gather(g, u, q):
-            s0, n = PIECES[g][q]
             if u == 0:
-                planes[g, q] = place("planes", [P, 2, 2 * n], BF16, PLANE_PLACES[g][q])
-            window = tables[g][:].rearrange("p u m -> p (u m)") if (g, u) == (1, 0) else tables[g][:, u, :]
+                planes[g, q] = at("planes%d%d" % (g, q), [P, 2, 2 * PIECE], BF16, PLANES + 8 * q)
+            words = tables[g][:].bitcast(U32)
+            window = words if (g, u) == (1, 0) else words[:, u * T : (u + 1) * T]
             nc.vector.tensor_copy(
                 planes[g, q][:, u, :].bitcast(U32),
-                window.bitcast(U32).indirect(offs_t[:, s0 // 16 : (s0 + n) // 16]),
+                window.indirect(offs_t[:, q * PIECE // 16 : (q + 1) * PIECE // 16]),
             )
 
-        def weave(dst, halves):
-            words = halves.rearrange("p u m -> p (u m)").bitcast(F32).rearrange("p (u n) -> p n u", u=2)
-            return dst.bitcast(F32).rearrange("p (n u) -> p n u", u=2), words
+        def weave(dst, halves, t0, n):
+            words = halves.bitcast(F32).rearrange("p (u n) -> p n u", u=2)[:, t0 : t0 + n, :]
+            nc.scalar.copy(dst.bitcast(F32).rearrange("p (n u) -> p n u", u=2), words)
 
-        grouped_slots = {}
+        grouped = {}
 
-        def group_slots(g, q, dst=None):
-            if dst is None:
-                dst = place("grouped", [P, 4 * PIECES[g][q][1]], BF16, "grouped", 2)[:]
-            nc.scalar.copy(*weave(dst, planes[g, q][:]))
-            grouped_slots[g, q] = dst
+        def group_slots(g, q, kib):
+            t = at("slots%d%d" % (g, q), [P, 4 * PIECE], BF16, kib)
+            weave(t[:], planes[g, q][:].rearrange("p u m -> p (u m)"), 0, PIECE)
+            grouped["s", g, q] = (t, kib)
 
-        def quantise_slots(g, q):
-            s0, n = PIECES[g][q]
-            cols = slice(s0, s0 + n)
-            nc.vector.quantize_mx(
-                out=slot_codes[:, g, cols].bitcast(FP8X4), scales=slot_scales[:, g, cols], in_=grouped_slots[g, q]
-            )
+        token_cells = [at("tokens%d" % c, [P, 4 * PIECE], BF16, TOKEN_CELLS + 8 * c) for c in range(3)]
 
-        def group_tokens(g, t0, n, tag, bufs=1):
-            t = place("xgrouped", [P, 4 * n], BF16, tag, bufs)
-            dst, words = weave(t[:], tables[g][:])
-            nc.scalar.copy(dst, words[:, t0 : t0 + n, :])
-            return t
+        def group_tokens(g):
+            weave(token_cells[g][:], tables[g][:], 0, 1024)
+            weave(token_cells[2][:, 2048 * g : 2048 * (g + 1)], tables[g][:], 1024, 512)
 
-        def quantise_tokens(t, g, t0, n):
-            cols = slice(t0, t0 + n)
-            nc.vector.quantize_mx(out=token_codes[g][:, cols].bitcast(FP8X4), scales=token_scales[g][:, cols], in_=t[:])
+        for c in range(3):
+            grouped["t", c] = (token_cells[c], TOKEN_CELLS + 8 * c)
+        for c in range(6):
+            grouped["w", c] = (at("weights%d" % c, [P, 4 * PIECE], BF16, WEIGHT_CELLS + 8 * c), WEIGHT_CELLS + 8 * c)
+        grouped["w", 6] = (at("weights6", [P, PIECE], BF16, WEIGHT_CELLS + 48), WEIGHT_CELLS + 48)
 
-        def load_and_cast_w(e0, engines, dst=None, single_loads=False):
-            n = len(engines)
-            raw = place("wraw", [P, 2, n * 4 * N], F32, "raw", RAW_PLACES)
-            rows = raw[:].rearrange("p a b -> p (a b)").rearrange("p (e g m) -> p e g m", g=G, m=4 * N)
-            cut = 1 if single_loads else n
-            for k in range(0, n, cut):
-                nc.sync.dma_start(
-                    rows[:, k : k + cut].rearrange("p e g (j n) -> p e g j n", j=4), w_view[:, e0 + k : e0 + k + cut]
+        def w_slot(e):
+            return 11 + e
+
+        def load_w(e):
+            raw = at("w%d" % e, [P, G, 4, N], F32, raw_at(w_slot(e)))
+            nc.sync.dma_start(raw[:], w_view[:, e])
+            return raw
+
+        def cast_w(e, raw, engine):
+            dst = grouped["w", e // 4][0][:, (e % 4) * 1024 : (e % 4 + 1) * 1024]
+            if engine == "G":
+                cast("G", dst.rearrange("p (g n j) -> p g n j", g=G, j=4), raw[:].rearrange("p g j n -> p g n j"))
+            else:
+                run = 4 if engine == "V" else 2
+                to = dst.rearrange("p (g c i j) -> p g c j i", g=G, i=run, j=4)
+                cast(engine, to, raw[:].rearrange("p g j (c i) -> p g c j i", i=run))
+
+        codes = {}
+
+        def quantise(key, codes_kib, scales_kib):
+            src = grouped[key][0]
+            n = src.shape[1] // 4
+            name = "".join(str(k) for k in key)
+            c = at("codes_" + name, [P, n], U32, codes_kib)
+            s = at("scales_" + name, [P, n], U8, scales_kib)
+            nc.vector.quantize_mx(out=c[:].bitcast(FP8X4), scales=s[:], in_=src[:])
+            codes[key] = (c, s)
+
+        def quantise_over(key, earlier):
+            kib = grouped[earlier][1]
+            quantise(key, kib, kib + 4)
+
+        def multiply(dst, w_key, w_col, x_keys, x_cols, width):
+            for g in range(G):
+                wc = slice(w_col + g * N, w_col + (g + 1) * N)
+                xc = slice(x_cols[g], x_cols[g] + width)
+                nc.tensor.matmul_mx(
+                    out=dst,
+                    lhsT=codes[w_key][0][:, wc].bitcast(FP8X4),
+                    lhsT_scale=codes[w_key][1][:, wc],
+                    rhs=codes[x_keys[g]][0][:, xc].bitcast(FP8X4),
+                    rhs_scale=codes[x_keys[g]][1][:, xc],
+                    start=(g == 0),
+                    stop=(g == G - 1),
                 )
-            if dst is None:
-                dst = place("wgrouped", [P, n, GROUPED_W], BF16, "wgrouped", 3)[:]
-            step = n if len(set(engines)) == 1 and not single_loads else 1
-            for k in range(0, n, step):
-                if engines[k] == "G":
-                    nc.gpsimd.tensor_scalar(
-                        dst[:, k : k + step, :].rearrange("p e (a n t) -> p (e a) n t", n=N, t=4),
-                        rows[:, k : k + step].rearrange("p e g (t n) -> p (e g) n t", t=4),
-                        1.0,
-                        0.0,
-                        MULT,
-                        ADD,
-                    )
-                else:
-                    run = 4 if engines[k] == "V" else 2
-                    to = dst[:, k : k + step, :].rearrange("p e (a c i t) -> p (e a) c t i", c=N // run, i=run, t=4)
-                    src = rows[:, k : k + step].rearrange("p e g (t c i) -> p (e g) c t i", t=4, i=run)
-                    if engines[k] == "V":
-                        nc.vector.tensor_copy(to, src)
-                    else:
-                        nc.scalar.copy(to, src)
-            return raw, dst
 
-        def quantise_w(e0, grouped):
-            n = grouped.shape[1]
-            nc.vector.quantize_mx(
-                out=w_codes[:, e0 : e0 + n].rearrange("p e g n -> p (e g n)").bitcast(FP8X4),
-                scales=w_scales[:, e0 : e0 + n].rearrange("p e g n -> p (e g n)"),
-                in_=grouped.rearrange("p e m -> p (e m)"),
-            )
-
-        def expert_bank(e0):
-            bank = psum.tile([P, 4, C], F32, name="bank", tag="bank", bufs=BANK_RING)
+        def expert_bank(c):
+            bank = psum.tile([P, 4, C], F32, name="bank", tag="bank", bufs=5)
             for k in range(4):
-                cols = slice((e0 + k) * C, (e0 + k + 1) * C)
-                for g in range(G):
-                    nc.tensor.matmul_mx(
-                        out=bank[:, k, :],
-                        lhsT=w_codes[:, e0 + k, g, :].bitcast(FP8X4),
-                        lhsT_scale=w_scales[:, e0 + k, g, :],
-                        rhs=slot_codes[:, g, cols].bitcast(FP8X4),
-                        rhs_scale=slot_scales[:, g, cols],
-                        start=(g == 0),
-                        stop=(g == G - 1),
-                    )
+                e = 4 * c + k
+                q, col = divmod(e * C, PIECE)
+                multiply(bank[:, k, :], ("w", c), k * G * N, (("s", 0, q), ("s", 1, q)), (col, col), C)
             for k in range(4):
-                e = e0 + k
+                e = 4 * c + k
                 nc.scalar.activation(y[:, e * C : (e + 1) * C], bank[:, k, :], IDENTITY, bias=b_t[:, e : e + 1])
 
-        load_and_cast_x(0, 0, 0, 1024, 1024, with_vector=True)
-        load_and_cast_x(0, 0, 1024, 512, 256, with_vector=True)
+        head = SCALAR_HEAD_TOKENS
+        load_x(0, 0, 0, 1024, raw_at(0), (("V", 1024 - head), ("S", head)))
+        load_x(0, 0, 1024, 512, raw_at(2), (("V", 256 - head // 2), ("S", head // 2)), cut=256)
         nc.sync.dma_start(offs_t[:], offs)
-        load_and_cast_x(0, 1, 0, 1024, 512, tag="held", bufs=1)
-        load_and_cast_x(0, 1, 1024, 512, 512, tag="planes2", bufs=1)
-        for q in range(len(PIECES[0])):
-            gather(0, 0, q)
-            gather(0, 1, q)
-
-        joint = place("joint", [P, 6, GROUPED_W], BF16, "joint")
-        early = place("early", [P, 4, GROUPED_W], BF16, "wa")
-        load_and_cast_w(0, "GG", early[:, 0:2, :], single_loads=True)
-        load_and_cast_w(2, "GG", early[:, 2:4, :], single_loads=True)
-        load_and_cast_w(4, "GG", joint[:, 4:6, :])
-        tokens_a = group_tokens(0, 0, 1024, "grouped", 2)
-        tokens_b = group_tokens(0, 1024, 512, "tokens")
-        quantise_tokens(tokens_a, 0, 0, 1024)
-        quantise_tokens(tokens_b, 0, 1024, 512)
-        group_slots(0, 0)
-        group_slots(0, 1, joint[:, 0:4, :].rearrange("p e m -> p (e m)"))
-        load_and_cast_x(1, 0, 0, 1024, 1024)
-        load_and_cast_x(1, 0, 1024, 512, 512)
-        load_and_cast_x(1, 1, 0, 1024, 1024)
-        reused = load_and_cast_x(1, 1, 1024, 512, 512, tag="held", bufs=1, room=1024)
-        group_slots(0, 2, reused[:].rearrange("p a b -> p (a b)").bitcast(BF16))
-
-        quantise_w(0, early[:])
-        quantise_slots(0, 0)
-        quantise_slots(0, 1)
-        quantise_w(4, joint[:, 4:6, :])
-
-        for q in range(len(PIECES[1])):
+        load_x(0, 1, 0, 512, raw_at(3), (("G", 512),))
+        load_x(0, 1, 512, 512, raw_at(4), (("S", 512),))
+        load_x(0, 1, 1024, 512, PLANES + 16, (("G", 256), ("S", 256)))
+        for u in range(2):
+            for c in range(3):
+                load_x(1, u, 512 * c, 512, raw_at(5 + 3 * u + c), (("G", 512),))
+        for u, q in ((0, 0), (0, 1), (1, 0), (1, 1), (0, 2), (1, 2)):
+            gather(0, u, q)
+        group_tokens(0)
+        group_slots(0, 0, SLOT_CELLS)
+        group_slots(0, 1, SLOT_CELLS + 8)
+        group_tokens(1)
+        group_slots(0, 2, SLOT_CELLS + 16)
+        for q in range(3):
             gather(1, 0, q)
             gather(1, 1, q)
-        quantise_slots(0, 2)
-        middle = place("middle", [P, 8, GROUPED_W], BF16, "joint")
-        load_and_cast_w(6, "GG", middle[:, 0:2, :], single_loads=True)
-        load_and_cast_w(8, "GG", middle[:, 2:4, :])
-        load_and_cast_w(10, "GG", middle[:, 4:6, :])
-        nc.sync.dma_start(b_t[:], b)
-        nc.sync.dma_start(pos1_t[:], pos1)
-        nc.sync.dma_start(pos2_t[:], pos2)
-        late_a = group_tokens(1, 0, 1024, "wa")
-        late_b = group_tokens(1, 1024, 512, "tokens")
-        group_slots(1, 0)
-        load_and_cast_w(12, "GS", middle[:, 6:8, :])
-        later = place("later", [P, 4, GROUPED_W], BF16, "planes2")
-        load_and_cast_w(14, "GG", later[:, 0:2, :])
-        group_slots(1, 1)
-        group_slots(1, 2, place("grouped", [P, 4 * PIECES[1][2][1]], BF16, "half")[:])
-        raw16 = load_and_cast_w(16, "SS", later[:, 2:4, :])[0]
-        group_slots(1, 3, raw16[:, 0, :].bitcast(BF16))
-        grouped18 = load_and_cast_w(18, "SS")[1]
-        grouped20 = load_and_cast_w(20, "SS")[1]
-        grouped22 = load_and_cast_w(22, "SV", reused[:, 0, :].bitcast(BF16).rearrange("p (e m) -> p e m", e=2))[1]
+        group_slots(1, 0, SLOT_CELLS + 24)
+        group_slots(1, 1, SLOT_CELLS + 32)
 
-        y = place("y", [P, S], F32, "table0")
-        quantise_slots(1, 0)
-        quantise_w(6, middle[:, 0:4, :])
-        quantise_slots(1, 1)
-        quantise_w(10, middle[:, 4:8, :])
-        quantise_w(14, later[:])
-        quantise_slots(1, 2)
-        quantise_slots(1, 3)
-        quantise_w(18, grouped18)
-        quantise_w(20, grouped20)
-        quantise_w(22, grouped22)
-        token_codes.append(place("token_codes1", [P, T], U32, "held"))
-        token_scales.append(place("token_scales1", [P, T], U8, "planes1"))
-        for e0 in range(0, 16, 4):
-            expert_bank(e0)
-        grouped_shared = load_and_cast_w(E, "V")[1]
-        quantise_tokens(late_a, 1, 0, 1024)
-        quantise_w(E, grouped_shared)
-        quantise_tokens(late_b, 1, 1024, 512)
-        expert_bank(16)
-        expert_bank(20)
+        for e in range(GPSIMD_EXPERTS):
+            cast_w(e, load_w(e), "G")
+            if e == 0:
+                nc.sync.dma_start(b_t[:], b)
+                nc.sync.dma_start(pos1_t[:], pos1)
+                nc.sync.dma_start(pos2_t[:], pos2)
+        for e in range(GPSIMD_EXPERTS, 14):
+            cast_w(e, load_w(e), "S")
+        group_slots(1, 2, raw_at(w_slot(12)))
+        for e in range(14, 16):
+            cast_w(e, load_w(e), "S")
 
-        gates = []
-        for t0, t1 in ((0, 1024), (1024, T)):
-            t = place("gates", [P, 2, t1 - t0], F32, "grouped", 2)
-            nc.sync.dma_start(t[:], gate_view[:, :, t0:t1])
-            gates.append(t)
-        first = place("first", [P, T], F32, "planes0")
-        second = place("second", [P, T], F32, "planes1")
-        total = place("total", [P, T], F32, "wa")
-        shared_turned = place("shared_turned", [P, T], F32, "joint")
-        routed_turned = place("routed_turned", [P, T], F32, "planes2")
+        y = at("y", [P, S], F32, TABLES + 8)
+        last = raw_at(w_slot(GPSIMD_EXPERTS - 1))
+        quantise(("s", 0, 0), TABLES, last)
+        quantise(("s", 1, 0), TABLES + 4, last + 1)
+        quantise_over(("w", 0), ("s", 0, 0))
+        quantise_over(("w", 1), ("s", 1, 0))
+        expert_bank(0)
+        expert_bank(1)
+        quantise_over(("s", 0, 1), ("w", 0))
+        quantise_over(("s", 1, 1), ("w", 1))
+        quantise_over(("w", 2), ("s", 0, 1))
+        quantise_over(("w", 3), ("s", 1, 1))
+        for e in range(16, 18):
+            cast_w(e, load_w(e), "S")
+        expert_bank(2)
+        expert_bank(3)
+        for e in range(18, SCALAR_EXPERTS_END):
+            cast_w(e, load_w(e), "S")
+        quantise_over(("s", 0, 2), ("w", 2))
+        quantise_over(("s", 1, 2), ("w", 3))
+        for e in range(SCALAR_EXPERTS_END, E):
+            cast_w(e, load_w(e), "V")
+        quantise_over(("w", 4), ("s", 0, 2))
+        quantise_over(("w", 5), ("s", 1, 2))
+        expert_bank(4)
+        expert_bank(5)
+        cast_w(E, load_w(E), "V")
+        quantise(("t", 0), grouped["w", 4][1], grouped["w", 5][1] + 7)
+        quantise(("w", 6), grouped["w", 5][1], grouped["w", 5][1] + 1)
+        quantise_over(("t", 1), ("t", 0))
+        quantise(("t", 2), grouped["w", 5][1] + 2, grouped["w", 5][1] + 6)
 
-        for c in (1, 2, 0):
-            bank = psum.tile([P, 4, N], F32, name="shared", tag="shared%d" % c, bufs=1)
-            for j in range(4):
-                cols = slice(512 * c + P * j, 512 * c + P * (j + 1))
-                for g in range(G):
-                    nc.tensor.matmul_mx(
-                        out=bank[:, j, :],
-                        lhsT=token_codes[g][:, cols].bitcast(FP8X4),
-                        lhsT_scale=token_scales[g][:, cols],
-                        rhs=w_codes[:, E, g, :].bitcast(FP8X4),
-                        rhs_scale=w_scales[:, E, g, :],
-                        start=(g == 0),
-                        stop=(g == G - 1),
-                    )
-            nc.scalar.copy(shared_turned[:, 512 * c : 512 * (c + 1)], bank[:].rearrange("p j n -> p (j n)"))
-
-        def fetch(r, t0, t1):
-            k = t0 // 1024
-            nc.vector.tensor_tensor(
-                (first, second)[r][:, t0:t1],
-                y[:].indirect((pos1_t, pos2_t)[r][:, t0 // 16 : t1 // 16]),
-                gates[k][:, r, t0 - 1024 * k : t1 - 1024 * k],
-                MULT,
-            )
-
-        for t0, t1 in ((TENSOR_TOKENS, 768), (768, 1024), (1024, T), (0, TENSOR_TOKENS)):
-            fetch(0, t0, t1)
-        for t0, t1 in ((0, 256), (256, TENSOR_TOKENS), (TENSOR_TOKENS, 1024), (1024, T)):
-            fetch(1, t0, t1)
+        gate_rows = at("gate_rows", [P, P], F32, raw_at(11))
+        nc.sync.dma_start(gate_rows[:], gate[0].rearrange("n (c t) -> (n c) t", t=P)[:P])
+        second_gate = at("second_gate", [P, T], F32, raw_at(9))
+        nc.sync.dma_start(second_gate[:], gate[1])
 
         def turn(dst, terms):
             for k, term in enumerate(terms):
                 nc.tensor.matmul(dst, term, ident[:], start=(k == 0), stop=(k == len(terms) - 1), is_transpose=True)
 
-        for_vector = []
-        for t0, t1 in ((TENSOR_TOKENS, 1024), (1024, 1280), (1280, T), (0, 256), (256, TENSOR_TOKENS)):
-            blocks = (t1 - t0) // P
-            on_tensor = t1 <= TENSOR_TOKENS
-            across = psum.tile([P, blocks, P], F32, name="across", tag="bank", bufs=BANK_RING)
+        bank = psum.tile([P, 4, C], F32, name="gate_bank", tag="shared0", bufs=1)
+        turn(bank[:, 0, :], [gate_rows[:]])
+        nc.scalar.copy(gate_columns[:], bank[:, 0, : T // P])
+
+        shared_turned = at("shared_turned", [P, T], F32, PLANES)
+        first_turned = at("first_turned", [P, T], F32, PLANES + 6)
+        second = at("second", [P, T], F32, PLANES + 12)
+        total = at("total", [P, T], F32, RESULT)
+        shared = []
+        for c in range(3):
+            bank = psum.tile([P, 4, N], F32, name="shared", tag="shared%d" % c, bufs=1)
+            for j in range(4):
+                for g in range(G):
+                    key, col = (("t", g), 512 * c + P * j) if c < 2 else (("t", 2), 512 * g + P * j)
+                    nc.tensor.matmul_mx(
+                        out=bank[:, j, :],
+                        lhsT=codes[key][0][:, col : col + P].bitcast(FP8X4),
+                        lhsT_scale=codes[key][1][:, col : col + P],
+                        rhs=codes["w", 6][0][:, g * N : (g + 1) * N].bitcast(FP8X4),
+                        rhs_scale=codes["w", 6][1][:, g * N : (g + 1) * N],
+                        start=(g == 0),
+                        stop=(g == G - 1),
+                    )
+            shared.append(bank)
+
+        across = {}
+
+        def fetch_first(c):
+            t = at("first%d" % c, [P, 512], F32, PLANES + 18 + 2 * c)
+            nc.scalar.activation(t[:], y[:].indirect(pos1_t[:, 32 * c : 32 * (c + 1)]), COPY)
+            across[c] = psum.tile([P, 4, P], F32, name="across", tag="bank", bufs=5)
+            for j in range(4):
+                turn(across[c][:, j, :], [t[:, P * j : P * (j + 1)]])
+
+        backs = []
+
+        def empty_shared(c):
+            nc.scalar.copy(shared_turned[:, 512 * c : 512 * (c + 1)], shared[c][:].rearrange("p j n -> p (j n)"))
+
+        def scale_and_turn_back(first_block, blocks, tag, bufs):
+            back = psum.tile([P, blocks, P], F32, name="back", tag=tag, bufs=bufs)
             for j in range(blocks):
-                cols = slice(t0 + P * j, t0 + P * (j + 1))
-                turn(across[:, j, :], [first[:, cols]] + ([second[:, cols]] if on_tensor else []))
-            nc.scalar.copy(routed_turned[:, t0:t1], across[:].rearrange("p j n -> p (j n)"))
-            if on_tensor:
-                back = psum.tile([P, blocks, P], F32, name="back", tag="bank", bufs=BANK_RING)
-            else:
-                back = psum.tile([P, blocks, P], F32, name="back", tag="shared%d" % ((len(for_vector) + 1) % 3), bufs=1)
-            for j in range(blocks):
-                cols = slice(t0 + P * j, t0 + P * (j + 1))
-                turn(back[:, j, :], [shared_turned[:, cols], routed_turned[:, cols]])
+                block = first_block + j
+                cols = slice(P * block, P * (block + 1))
+                scale = gate_columns[:, block : block + 1]
+                nc.scalar.activation(first_turned[:, cols], across[block // 4][:, block % 4, :], COPY, scale=scale)
+                turn(back[:, j, :], [shared_turned[:, cols], first_turned[:, cols]])
+            backs.append((P * first_block, P * (first_block + blocks), back))
+
+        fetch_first(0)
+        fetch_first(1)
+        empty_shared(0)
+        scale_and_turn_back(0, 4, "shared0", 1)
+        fetch_first(2)
+        empty_shared(1)
+        scale_and_turn_back(4, 4, "shared1", 1)
+        empty_shared(2)
+        scale_and_turn_back(8, 3, "shared2", 1)
+        scale_and_turn_back(11, 1, "bank", 5)
+        for c in range(3):
+            cols = slice(512 * c, 512 * (c + 1))
+            nc.vector.tensor_tensor(second[:, cols], y[:].indirect(pos2_t[:, 32 * c : 32 * (c + 1)]), second_gate[:, cols], MULT)
+        for t0, t1, back in backs:
             summed = back[:].rearrange("p j n -> p (j n)")
-            if on_tensor:
-                nc.scalar.activation(total[:, t0:t1], summed, IDENTITY, bias=b_t[:, E : E + 1])
-                nc.scalar.dma_start(out[:, t0:t1], total[:, t0:t1])
-            else:
-                for_vector.append((t0, t1, summed))
-        for t0, t1, summed in for_vector:
             nc.vector.scalar_tensor_tensor(total[:, t0:t1], summed, b_t[:, E : E + 1], second[:, t0:t1], ADD, ADD)
             nc.sync.dma_start(out[:, t0:t1], total[:, t0:t1])

@@ -22,17 +22,17 @@ IDENTITY = mybir.ActivationFunctionType.Identity
 COPY = mybir.ActivationFunctionType.Copy
 
 TABLES = 0
-PLANES = 24
-SLOT_CELLS = 48
-RESULT = 88
-WEIGHT_CELLS = 96
-TOKEN_CELLS = 146
-RAW = 170
-RAW_SLOTS = 16
+PLANE_A, PLANE_B, PLANE_C = 24, 32, 40
+TOKENS_0, TOKENS_0_END, TOKENS_1_END = 48, 56, 60
+SLOTS_0 = 64
+W_4 = 88
+W_0, W_12, W_16, W_20, W_SHARED = 92, 100, 108, 116, 124
+TOKENS_1 = 126
+SLOTS_1 = 134
+RAW = 160
 
 SCALAR_HEAD_TOKENS = 160
-GPSIMD_EXPERTS = 11
-SCALAR_EXPERTS_END = 21
+TURNED_TOKENS = 1024
 
 FLOPS = 2 * K * N * (S + T)
 
@@ -50,6 +50,7 @@ def tile_moe_shr_lin_bias_kernel(tc, xT, w, b, gate, offs, pos1, pos2, out):
         b_t = held.tile([P, E + 1], F32, name="b_t")
 
         ident = held.tile([P, P], F32, name="ident")
+        gate_rows = held.tile([P, P], F32, name="gate_rows")
         gate_columns = held.tile([P, T // P], F32, name="gate_columns")
         make_identity(nc, ident[:])
 
@@ -60,7 +61,7 @@ def tile_moe_shr_lin_bias_kernel(tc, xT, w, b, gate, offs, pos1, pos2, out):
             return room.tile(shape, dtype, name=name, offset=kib * KB, align_bytes=64)
 
         def raw_at(slot):
-            return RAW + 4 * (slot % RAW_SLOTS)
+            return RAW + 4 * slot
 
         tables = [at("table%d" % g, [P, 2 * 2 * T], BF16, TABLES + 12 * g) for g in range(G)]
 
@@ -87,93 +88,80 @@ def tile_moe_shr_lin_bias_kernel(tc, xT, w, b, gate, offs, pos1, pos2, out):
 
         planes = {}
 
-        def gather(g, u, q):
+        def gather(g, u, q, kib=None):
             if u == 0:
-                planes[g, q] = at("planes%d%d" % (g, q), [P, 2, 2 * PIECE], BF16, PLANES + 8 * q)
-            words = tables[g][:].bitcast(U32)
-            window = words if (g, u) == (1, 0) else words[:, u * T : (u + 1) * T]
+                planes[g, q] = at("planes%d%d" % (g, q), [P, 2, 2 * PIECE], BF16, kib)
+            window = tables[g][:].bitcast(U32)[:, u * T : (u + 1) * T]
             nc.vector.tensor_copy(
                 planes[g, q][:, u, :].bitcast(U32),
                 window.indirect(offs_t[:, q * PIECE // 16 : (q + 1) * PIECE // 16]),
             )
 
-        def weave(dst, halves, t0, n):
+        def weave(name, halves, t0, n, kib):
+            t = at(name, [P, 4 * n], BF16, kib)
             words = halves.bitcast(F32).rearrange("p (u n) -> p n u", u=2)[:, t0 : t0 + n, :]
-            nc.scalar.copy(dst.bitcast(F32).rearrange("p (n u) -> p n u", u=2), words)
+            nc.scalar.copy(t[:].bitcast(F32).rearrange("p (n u) -> p n u", u=2), words)
+            return t
 
-        grouped = {}
-
-        def group_slots(g, q, kib):
-            t = at("slots%d%d" % (g, q), [P, 4 * PIECE], BF16, kib)
-            weave(t[:], planes[g, q][:].rearrange("p u m -> p (u m)"), 0, PIECE)
-            grouped["s", g, q] = (t, kib)
-
-        token_cells = [at("tokens%d" % c, [P, 4 * PIECE], BF16, TOKEN_CELLS + 8 * c) for c in range(3)]
-
-        def group_tokens(g):
-            weave(token_cells[g][:], tables[g][:], 0, 1024)
-            weave(token_cells[2][:, 2048 * g : 2048 * (g + 1)], tables[g][:], 1024, 512)
-
-        for c in range(3):
-            grouped["t", c] = (token_cells[c], TOKEN_CELLS + 8 * c)
-        for c in range(6):
-            grouped["w", c] = (at("weights%d" % c, [P, 4 * PIECE], BF16, WEIGHT_CELLS + 8 * c), WEIGHT_CELLS + 8 * c)
-        grouped["w", 6] = (at("weights6", [P, PIECE], BF16, WEIGHT_CELLS + 48), WEIGHT_CELLS + 48)
+        def group_slots(g, q, kib=None):
+            halves = planes[g, q][:].rearrange("p u m -> p (u m)")
+            return weave("slots%d%d" % (g, q), halves, 0, PIECE, kib or (SLOTS_0, SLOTS_1)[g] + 8 * q)
 
         def w_slot(e):
-            return 11 + e
+            return 5 + e if e < 6 else e - 6 if e < 16 else 7 if e == 19 else e - 5 if e < 21 else e - 21
 
-        def load_w(e):
+        def load_and_cast_w(e, engine, cell, first):
             raw = at("w%d" % e, [P, G, 4, N], F32, raw_at(w_slot(e)))
             nc.sync.dma_start(raw[:], w_view[:, e])
-            return raw
-
-        def cast_w(e, raw, engine):
-            dst = grouped["w", e // 4][0][:, (e % 4) * 1024 : (e % 4 + 1) * 1024]
+            dst = cell[:, (e - first) * 1024 : (e - first + 1) * 1024]
             if engine == "G":
                 cast("G", dst.rearrange("p (g n j) -> p g n j", g=G, j=4), raw[:].rearrange("p g j n -> p g n j"))
             else:
-                run = 4 if engine == "V" else 2
-                to = dst.rearrange("p (g c i j) -> p g c j i", g=G, i=run, j=4)
-                cast(engine, to, raw[:].rearrange("p g j (c i) -> p g c j i", i=run))
+                to = dst.rearrange("p (g c i j) -> p g c j i", g=G, i=4, j=4)
+                cast(engine, to, raw[:].rearrange("p g j (c i) -> p g c j i", i=4))
 
-        codes = {}
-
-        def quantise(key, codes_kib, scales_kib):
-            src = grouped[key][0]
+        def quantise(name, src, codes_kib, scales_kib):
             n = src.shape[1] // 4
-            name = "".join(str(k) for k in key)
             c = at("codes_" + name, [P, n], U32, codes_kib)
             s = at("scales_" + name, [P, n], U8, scales_kib)
-            nc.vector.quantize_mx(out=c[:].bitcast(FP8X4), scales=s[:], in_=src[:])
-            codes[key] = (c, s)
+            nc.vector.quantize_mx(out=c[:].bitcast(FP8X4), scales=s[:], in_=src)
+            return c, s
 
-        def quantise_over(key, earlier):
-            kib = grouped[earlier][1]
-            quantise(key, kib, kib + 4)
+        w_codes = {}
 
-        def multiply(dst, w_key, w_col, x_keys, x_cols, width):
+        def quantise_w(cell, first, e0, n, codes_kib, scales_kib):
+            src = cell[:, (e0 - first) * 1024 : (e0 - first + n) * 1024]
+            pair = quantise("w%d" % e0, src, codes_kib, scales_kib)
+            for k in range(n):
+                w_codes[e0 + k] = (pair, k * G * N)
+
+        def multiply(dst, e, moving, width):
+            (c, s), col = w_codes[e]
             for g in range(G):
-                wc = slice(w_col + g * N, w_col + (g + 1) * N)
-                xc = slice(x_cols[g], x_cols[g] + width)
+                (xc, xs), x0 = moving[g]
                 nc.tensor.matmul_mx(
                     out=dst,
-                    lhsT=codes[w_key][0][:, wc].bitcast(FP8X4),
-                    lhsT_scale=codes[w_key][1][:, wc],
-                    rhs=codes[x_keys[g]][0][:, xc].bitcast(FP8X4),
-                    rhs_scale=codes[x_keys[g]][1][:, xc],
+                    lhsT=c[:, col + g * N : col + (g + 1) * N].bitcast(FP8X4),
+                    lhsT_scale=s[:, col + g * N : col + (g + 1) * N],
+                    rhs=xc[:, x0 : x0 + width].bitcast(FP8X4),
+                    rhs_scale=xs[:, x0 : x0 + width],
                     start=(g == 0),
                     stop=(g == G - 1),
                 )
 
-        def expert_bank(c):
-            bank = psum.tile([P, 4, C], F32, name="bank", tag="bank", bufs=5)
-            for k in range(4):
-                e = 4 * c + k
-                q, col = divmod(e * C, PIECE)
-                multiply(bank[:, k, :], ("w", c), k * G * N, (("s", 0, q), ("s", 1, q)), (col, col), C)
-            for k in range(4):
-                e = 4 * c + k
+        def turn(dst, terms):
+            for k, term in enumerate(terms):
+                nc.tensor.matmul(dst, term, ident[:], start=(k == 0), stop=(k == len(terms) - 1), is_transpose=True)
+
+        slot_codes = {}
+
+        def expert_bank(e0, n):
+            bank = psum.tile([P, n, C], F32, name="bank", tag="bank", bufs=5)
+            for k in range(n):
+                q, col = divmod((e0 + k) * C, PIECE)
+                multiply(bank[:, k, :], e0 + k, [(slot_codes[g, q], col) for g in range(G)], C)
+            for k in range(n):
+                e = e0 + k
                 nc.scalar.activation(y[:, e * C : (e + 1) * C], bank[:, k, :], IDENTITY, bias=b_t[:, e : e + 1])
 
         head = SCALAR_HEAD_TOKENS
@@ -182,139 +170,153 @@ def tile_moe_shr_lin_bias_kernel(tc, xT, w, b, gate, offs, pos1, pos2, out):
         nc.sync.dma_start(offs_t[:], offs)
         load_x(0, 1, 0, 512, raw_at(3), (("G", 512),))
         load_x(0, 1, 512, 512, raw_at(4), (("S", 512),))
-        load_x(0, 1, 1024, 512, PLANES + 16, (("G", 256), ("S", 256)))
-        for u in range(2):
-            for c in range(3):
-                load_x(1, u, 512 * c, 512, raw_at(5 + 3 * u + c), (("G", 512),))
+        load_x(0, 1, 1024, 512, PLANE_C, (("S", 512),))
         for u, q in ((0, 0), (0, 1), (1, 0), (1, 1), (0, 2), (1, 2)):
-            gather(0, u, q)
-        group_tokens(0)
-        group_slots(0, 0, SLOT_CELLS)
-        group_slots(0, 1, SLOT_CELLS + 8)
-        group_tokens(1)
-        group_slots(0, 2, SLOT_CELLS + 16)
-        for q in range(3):
-            gather(1, 0, q)
-            gather(1, 1, q)
-        group_slots(1, 0, SLOT_CELLS + 24)
-        group_slots(1, 1, SLOT_CELLS + 32)
+            gather(0, u, q, PLANE_A + 8 * q)
+        w0 = at("w_cell0", [P, 4 * 1024], BF16, W_0)
+        w4 = at("w_cell4", [P, 2 * 1024], BF16, W_4)
+        for e in range(4):
+            load_and_cast_w(e, "G", w0, 0)
+        for e in (4, 5):
+            load_and_cast_w(e, "G", w4, 4)
+        tokens0 = weave("tokens0", tables[0][:], 0, 1024, TOKENS_0)
+        tokens0_end = weave("tokens0_end", tables[0][:], 1024, 512, TOKENS_0_END)
+        slots0 = [group_slots(0, 0), group_slots(0, 1)]
+        load_x(1, 0, 0, 512, raw_at(11), (("S", 512),))
+        load_x(1, 0, 512, 512, raw_at(12), (("S", 512),))
+        slots0.append(group_slots(0, 2))
+        load_x(1, 0, 1024, 512, raw_at(13), (("S", 512),))
+        load_x(1, 1, 0, 1024, raw_at(14), (("S", 1024),))
+        load_x(1, 1, 1024, 512, PLANE_A, (("S", 512),))
 
-        for e in range(GPSIMD_EXPERTS):
-            cast_w(e, load_w(e), "G")
-            if e == 0:
-                nc.sync.dma_start(b_t[:], b)
-                nc.sync.dma_start(pos1_t[:], pos1)
-                nc.sync.dma_start(pos2_t[:], pos2)
-        for e in range(GPSIMD_EXPERTS, 14):
-            cast_w(e, load_w(e), "S")
-        group_slots(1, 2, raw_at(w_slot(12)))
-        for e in range(14, 16):
-            cast_w(e, load_w(e), "S")
+        held_by_gpsimd = raw_at(w_slot(5))
+        token_codes0 = quantise("t0", tokens0[:], TABLES, held_by_gpsimd)
+        quantise_w(w0, 0, 0, 4, TABLES + 4, held_by_gpsimd + 1)
+        slot_codes[0, 0] = quantise("s00", slots0[0][:], TOKENS_0, TOKENS_0 + 4)
+        token_codes0_end = quantise("t0e", tokens0_end[:], W_0, W_0 + 4)
+        slot_codes[0, 1] = quantise("s01", slots0[1][:], SLOTS_0, SLOTS_0 + 4)
+        slot_codes[0, 2] = quantise("s02", slots0[2][:], TOKENS_0_END, TABLES + 8)
+        quantise_w(w4, 4, 4, 2, TABLES + 9, TABLES + 11)
 
-        y = at("y", [P, S], F32, TABLES + 8)
-        last = raw_at(w_slot(GPSIMD_EXPERTS - 1))
-        quantise(("s", 0, 0), TABLES, last)
-        quantise(("s", 1, 0), TABLES + 4, last + 1)
-        quantise_over(("w", 0), ("s", 0, 0))
-        quantise_over(("w", 1), ("s", 1, 0))
-        expert_bank(0)
-        expert_bank(1)
-        quantise_over(("s", 0, 1), ("w", 0))
-        quantise_over(("s", 1, 1), ("w", 1))
-        quantise_over(("w", 2), ("s", 0, 1))
-        quantise_over(("w", 3), ("s", 1, 1))
-        for e in range(16, 18):
-            cast_w(e, load_w(e), "S")
-        expert_bank(2)
-        expert_bank(3)
-        for e in range(18, SCALAR_EXPERTS_END):
-            cast_w(e, load_w(e), "S")
-        quantise_over(("s", 0, 2), ("w", 2))
-        quantise_over(("s", 1, 2), ("w", 3))
-        for e in range(SCALAR_EXPERTS_END, E):
-            cast_w(e, load_w(e), "V")
-        quantise_over(("w", 4), ("s", 0, 2))
-        quantise_over(("w", 5), ("s", 1, 2))
-        expert_bank(4)
-        expert_bank(5)
-        cast_w(E, load_w(E), "V")
-        quantise(("t", 0), grouped["w", 4][1], grouped["w", 5][1] + 7)
-        quantise(("w", 6), grouped["w", 5][1], grouped["w", 5][1] + 1)
-        quantise_over(("t", 1), ("t", 0))
-        quantise(("t", 2), grouped["w", 5][1] + 2, grouped["w", 5][1] + 6)
-
-        gate_rows = at("gate_rows", [P, P], F32, raw_at(11))
+        gather(1, 0, 0, SLOTS_0 + 8)
+        gather(1, 0, 1, PLANE_B)
+        gather(1, 1, 0)
+        gather(1, 1, 1)
+        gather(1, 0, 2, PLANE_A)
+        gather(1, 1, 2)
+        w6 = at("w_cell6", [P, 6 * 1024], BF16, SLOTS_0 + 16)
+        w12 = at("w_cell12", [P, 4 * 1024], BF16, W_12)
+        w16 = at("w_cell16", [P, 4 * 1024], BF16, W_16)
+        w20 = at("w_cell20", [P, 4 * 1024], BF16, W_20)
+        load_and_cast_w(6, "G", w6, 6)
+        load_and_cast_w(7, "G", w6, 6)
+        tokens1 = weave("tokens1", tables[1][:], 0, 1024, TOKENS_1)
+        tokens1_end = weave("tokens1_end", tables[1][:], 1024, 512, TOKENS_1_END)
+        load_and_cast_w(8, "S", w6, 6)
+        load_and_cast_w(9, "S", w6, 6)
+        load_and_cast_w(10, "G", w6, 6)
+        load_and_cast_w(11, "G", w6, 6)
+        nc.sync.dma_start(b_t[:], b)
+        nc.sync.dma_start(pos1_t[:], pos1)
+        nc.sync.dma_start(pos2_t[:], pos2)
         nc.sync.dma_start(gate_rows[:], gate[0].rearrange("n (c t) -> (n c) t", t=P)[:P])
-        second_gate = at("second_gate", [P, T], F32, raw_at(9))
+        gate_bank = psum.tile([P, P], F32, name="gate_bank", tag="shared0", bufs=1)
+        turn(gate_bank[:], [gate_rows[:]])
+        nc.scalar.copy(gate_columns[:], gate_bank[:, : T // P])
+        slots1 = [group_slots(1, 0), group_slots(1, 1)]
+        for e in (12, 13, 14):
+            load_and_cast_w(e, "G", w12, 12)
+        load_and_cast_w(15, "S", w12, 12)
+        load_and_cast_w(16, "G", w16, 16)
+        load_and_cast_w(17, "G", w16, 16)
+        load_and_cast_w(18, "S", w16, 16)
+        slots1.append(group_slots(1, 2, raw_at(w_slot(18))))
+        load_and_cast_w(19, "S", w16, 16)
+
+        y = at("y", [P, S], F32, PLANE_B + 4)
+        held_by_gpsimd = raw_at(w_slot(17))
+        slot_codes[1, 0] = quantise("s10", slots1[0][:], TABLES + 12, held_by_gpsimd)
+        quantise_w(w6, 6, 6, 2, TABLES + 16, held_by_gpsimd + 1)
+        quantise_w(w6, 6, 8, 4, SLOTS_1, SLOTS_1 + 4)
+        slot_codes[1, 1] = quantise("s11", slots1[1][:], TABLES + 18, held_by_gpsimd + 2)
+        quantise_w(w12, 12, 12, 4, SLOTS_0 + 16, SLOTS_0 + 20)
+        slot_codes[1, 2] = quantise("s12", slots1[2][:], SLOTS_1 + 8, SLOTS_1 + 12)
+        quantise_w(w16, 16, 16, 4, W_12, W_12 + 4)
+        expert_bank(0, 4)
+        expert_bank(4, 4)
+        load_and_cast_w(20, "S", w20, 20)
+        load_and_cast_w(21, "S", w20, 20)
+        quantise_w(w20, 20, 20, 2, raw_at(13), raw_at(13) + 2)
+        expert_bank(8, 4)
+        expert_bank(12, 4)
+        load_and_cast_w(22, "S", w20, 20)
+        load_and_cast_w(23, "S", w20, 20)
+        token_codes1 = quantise("t1", tokens1[:], W_16, W_16 + 4)
+        quantise_w(w20, 20, 22, 2, raw_at(14), raw_at(14) + 2)
+        expert_bank(16, 4)
+        expert_bank(20, 4)
+        w24 = at("w_cell24", [P, 1024], BF16, W_SHARED)
+        load_and_cast_w(E, "V", w24, E)
+        token_codes1_end = quantise("t1e", tokens1_end[:], W_20, W_20 + 2)
+        quantise_w(w24, E, E, 1, W_20 + 4, W_20 + 5)
+
+        second_gate = at("second_gate", [P, T], F32, raw_at(4))
         nc.sync.dma_start(second_gate[:], gate[1])
-
-        def turn(dst, terms):
-            for k, term in enumerate(terms):
-                nc.tensor.matmul(dst, term, ident[:], start=(k == 0), stop=(k == len(terms) - 1), is_transpose=True)
-
-        bank = psum.tile([P, 4, C], F32, name="gate_bank", tag="shared0", bufs=1)
-        turn(bank[:, 0, :], [gate_rows[:]])
-        nc.scalar.copy(gate_columns[:], bank[:, 0, : T // P])
-
-        shared_turned = at("shared_turned", [P, T], F32, PLANES)
-        first_turned = at("first_turned", [P, T], F32, PLANES + 6)
-        second = at("second", [P, T], F32, PLANES + 12)
-        total = at("total", [P, T], F32, RESULT)
-        shared = []
-        for c in range(3):
+        first_gate = at("first_gate", [P, T - TURNED_TOKENS], F32, raw_at(6))
+        nc.sync.dma_start(first_gate[:], gate[0, :, TURNED_TOKENS:])
+        wc, ws = w_codes[E][0]
+        shared_turned = at("shared_turned", [P, TURNED_TOKENS], F32, raw_at(7))
+        first_turned = at("first_turned", [P, TURNED_TOKENS], F32, raw_at(8))
+        second = at("second", [P, T], F32, raw_at(13))
+        last_first = at("last_first", [P, T - TURNED_TOKENS], F32, raw_at(15))
+        total = at("total", [P, T], F32, PLANE_A)
+        for c in range(2):
             bank = psum.tile([P, 4, N], F32, name="shared", tag="shared%d" % c, bufs=1)
             for j in range(4):
-                for g in range(G):
-                    key, col = (("t", g), 512 * c + P * j) if c < 2 else (("t", 2), 512 * g + P * j)
+                cols = slice(512 * c + P * j, 512 * c + P * (j + 1))
+                for g, (xc, xs) in enumerate((token_codes0, token_codes1)):
                     nc.tensor.matmul_mx(
                         out=bank[:, j, :],
-                        lhsT=codes[key][0][:, col : col + P].bitcast(FP8X4),
-                        lhsT_scale=codes[key][1][:, col : col + P],
-                        rhs=codes["w", 6][0][:, g * N : (g + 1) * N].bitcast(FP8X4),
-                        rhs_scale=codes["w", 6][1][:, g * N : (g + 1) * N],
+                        lhsT=xc[:, cols].bitcast(FP8X4),
+                        lhsT_scale=xs[:, cols],
+                        rhs=wc[:, g * N : (g + 1) * N].bitcast(FP8X4),
+                        rhs_scale=ws[:, g * N : (g + 1) * N],
                         start=(g == 0),
                         stop=(g == G - 1),
                     )
-            shared.append(bank)
+            nc.scalar.copy(shared_turned[:, 512 * c : 512 * (c + 1)], bank[:].rearrange("p j n -> p (j n)"))
+        shared_end = psum.tile([P, 512], F32, name="shared_end", tag="shared2", bufs=1)
+        multiply(shared_end[:], E, [(token_codes0_end, 0), (token_codes1_end, 0)], 512)
 
-        across = {}
-
-        def fetch_first(c):
-            t = at("first%d" % c, [P, 512], F32, PLANES + 18 + 2 * c)
+        across = []
+        for c in range(2):
+            t = at("first%d" % c, [P, 512], F32, raw_at(9) + 2 * c)
             nc.scalar.activation(t[:], y[:].indirect(pos1_t[:, 32 * c : 32 * (c + 1)]), COPY)
-            across[c] = psum.tile([P, 4, P], F32, name="across", tag="bank", bufs=5)
+            across.append(psum.tile([P, 4, P], F32, name="across", tag="bank", bufs=5))
             for j in range(4):
                 turn(across[c][:, j, :], [t[:, P * j : P * (j + 1)]])
-
         backs = []
-
-        def empty_shared(c):
-            nc.scalar.copy(shared_turned[:, 512 * c : 512 * (c + 1)], shared[c][:].rearrange("p j n -> p (j n)"))
-
-        def scale_and_turn_back(first_block, blocks, tag, bufs):
-            back = psum.tile([P, blocks, P], F32, name="back", tag=tag, bufs=bufs)
-            for j in range(blocks):
-                block = first_block + j
+        for c in range(2):
+            backs.append(psum.tile([P, 4, P], F32, name="back", tag="shared%d" % c, bufs=1))
+            for j in range(4):
+                block = 4 * c + j
                 cols = slice(P * block, P * (block + 1))
                 scale = gate_columns[:, block : block + 1]
-                nc.scalar.activation(first_turned[:, cols], across[block // 4][:, block % 4, :], COPY, scale=scale)
-                turn(back[:, j, :], [shared_turned[:, cols], first_turned[:, cols]])
-            backs.append((P * first_block, P * (first_block + blocks), back))
+                nc.scalar.activation(first_turned[:, cols], across[c][:, j, :], COPY, scale=scale)
+                turn(backs[c][:, j, :], [shared_turned[:, cols], first_turned[:, cols]])
 
-        fetch_first(0)
-        fetch_first(1)
-        empty_shared(0)
-        scale_and_turn_back(0, 4, "shared0", 1)
-        fetch_first(2)
-        empty_shared(1)
-        scale_and_turn_back(4, 4, "shared1", 1)
-        empty_shared(2)
-        scale_and_turn_back(8, 3, "shared2", 1)
-        scale_and_turn_back(11, 1, "bank", 5)
-        for c in range(3):
-            cols = slice(512 * c, 512 * (c + 1))
-            nc.vector.tensor_tensor(second[:, cols], y[:].indirect(pos2_t[:, 32 * c : 32 * (c + 1)]), second_gate[:, cols], MULT)
-        for t0, t1, back in backs:
-            summed = back[:].rearrange("p j n -> p (j n)")
-            nc.vector.scalar_tensor_tensor(total[:, t0:t1], summed, b_t[:, E : E + 1], second[:, t0:t1], ADD, ADD)
+        def fetch(dst, pos, t0, t1, gates):
+            nc.vector.tensor_tensor(dst, y[:].indirect(pos[:, t0 // 16 : t1 // 16]), gates, MULT)
+
+        def close(t0, t1, summed, term):
+            nc.vector.scalar_tensor_tensor(total[:, t0:t1], summed, b_t[:, E : E + 1], term, ADD, ADD)
             nc.sync.dma_start(out[:, t0:t1], total[:, t0:t1])
+
+        fetch(last_first[:], pos1_t, TURNED_TOKENS, T, first_gate[:])
+        fetch(second[:, 1024:], pos2_t, 1024, T, second_gate[:, 1024:])
+        fetch(second[:, :512], pos2_t, 0, 512, second_gate[:, :512])
+        nc.vector.tensor_tensor(last_first[:], last_first[:], second[:, 1024:], ADD)
+        fetch(second[:, 512:1024], pos2_t, 512, 1024, second_gate[:, 512:1024])
+        close(1024, T, shared_end[:], last_first[:])
+        close(0, 512, backs[0][:].rearrange("p j n -> p (j n)"), second[:, :512])
+        close(512, 1024, backs[1][:].rearrange("p j n -> p (j n)"), second[:, 512:1024])

@@ -30,9 +30,10 @@ W_0, W_12, W_16, W_20, W_SHARED = 92, 100, 108, 116, 124
 TOKENS_1 = 126
 SLOTS_1 = 134
 RAW = 160
+SPARE = 224
 
 SCALAR_HEAD_TOKENS = 160
-TURNED_TOKENS = 1024
+TURNED_TOKENS = 1280
 
 FLOPS = 2 * K * N * (S + T)
 
@@ -190,7 +191,7 @@ def tile_moe_shr_lin_bias_kernel(tc, xT, w, b, gate, offs, pos1, pos2, out):
         load_x(1, 1, 1024, 512, PLANE_A, (("S", 512),))
 
         held_by_gpsimd = raw_at(w_slot(5))
-        token_codes0 = quantise("t0", tokens0[:], TABLES, held_by_gpsimd)
+        token_codes0 = quantise("t0", tokens0[:], SPARE, held_by_gpsimd)
         quantise_w(w0, 0, 0, 4, TABLES + 4, held_by_gpsimd + 1)
         slot_codes[0, 0] = quantise("s00", slots0[0][:], TOKENS_0, TOKENS_0 + 4)
         token_codes0_end = quantise("t0e", tokens0_end[:], W_0, W_0 + 4)
@@ -235,7 +236,7 @@ def tile_moe_shr_lin_bias_kernel(tc, xT, w, b, gate, offs, pos1, pos2, out):
 
         y = at("y", [P, S], F32, PLANE_B + 4)
         held_by_gpsimd = raw_at(w_slot(17))
-        slot_codes[1, 0] = quantise("s10", slots1[0][:], TABLES + 12, held_by_gpsimd)
+        slot_codes[1, 0] = quantise("s10", slots1[0][:], SPARE + 4, held_by_gpsimd)
         quantise_w(w6, 6, 6, 2, TABLES + 16, held_by_gpsimd + 1)
         quantise_w(w6, 6, 8, 4, SLOTS_1, SLOTS_1 + 4)
         slot_codes[1, 1] = quantise("s11", slots1[1][:], TABLES + 18, held_by_gpsimd + 2)
@@ -250,60 +251,80 @@ def tile_moe_shr_lin_bias_kernel(tc, xT, w, b, gate, offs, pos1, pos2, out):
         expert_bank(8, 4)
         expert_bank(12, 4)
         load_and_cast_w(22, "S", w20, 20)
-        load_and_cast_w(23, "S", w20, 20)
-        token_codes1 = quantise("t1", tokens1[:], W_16, W_16 + 4)
+        load_and_cast_w(23, "V", w20, 20)
         quantise_w(w20, 20, 22, 2, raw_at(14), raw_at(14) + 2)
         expert_bank(16, 4)
         expert_bank(20, 4)
         w24 = at("w_cell24", [P, 1024], BF16, W_SHARED)
         load_and_cast_w(E, "V", w24, E)
-        token_codes1_end = quantise("t1e", tokens1_end[:], W_20, W_20 + 2)
+        token_codes1 = quantise("t1", tokens1[:], W_16, W_20 + 6)
         quantise_w(w24, E, E, 1, W_20 + 4, W_20 + 5)
+        token_codes1_end = quantise("t1e", tokens1_end[:], W_20, W_20 + 2)
 
         second_gate = at("second_gate", [P, T], F32, raw_at(4))
         nc.sync.dma_start(second_gate[:], gate[1])
         first_gate = at("first_gate", [P, T - TURNED_TOKENS], F32, raw_at(6))
         nc.sync.dma_start(first_gate[:], gate[0, :, TURNED_TOKENS:])
         wc, ws = w_codes[E][0]
-        shared_turned = at("shared_turned", [P, TURNED_TOKENS], F32, raw_at(7))
-        first_turned = at("first_turned", [P, TURNED_TOKENS], F32, raw_at(8))
+        shared_turned = at("shared_turned", [P, TURNED_TOKENS], F32, SLOTS_0 + 8)
+        first_turned = at("first_turned", [P, TURNED_TOKENS], F32, raw_at(7))
         second = at("second", [P, T], F32, raw_at(13))
         last_first = at("last_first", [P, T - TURNED_TOKENS], F32, raw_at(15))
         total = at("total", [P, T], F32, PLANE_A)
-        for c in range(2):
-            bank = psum.tile([P, 4, N], F32, name="shared", tag="shared%d" % c, bufs=1)
-            for j in range(4):
-                cols = slice(512 * c + P * j, 512 * c + P * (j + 1))
-                for g, (xc, xs) in enumerate((token_codes0, token_codes1)):
+        turned = [(t0, min(t0 + 512, TURNED_TOKENS)) for t0 in range(0, TURNED_TOKENS, 512)]
+
+        def token_operand(g, t0):
+            if t0 < 1024:
+                return (token_codes0, token_codes1)[g], t0
+            return (token_codes0_end, token_codes1_end)[g], t0 - 1024
+
+        def shared_product(c):
+            t0, t1 = turned[c]
+            bank = psum.tile([P, (t1 - t0) // P, N], F32, name="shared", tag="shared%d" % c, bufs=1)
+            for j in range((t1 - t0) // P):
+                for g in range(G):
+                    (xc, xs), x0 = token_operand(g, t0 + P * j)
                     nc.tensor.matmul_mx(
                         out=bank[:, j, :],
-                        lhsT=xc[:, cols].bitcast(FP8X4),
-                        lhsT_scale=xs[:, cols],
+                        lhsT=xc[:, x0 : x0 + P].bitcast(FP8X4),
+                        lhsT_scale=xs[:, x0 : x0 + P],
                         rhs=wc[:, g * N : (g + 1) * N].bitcast(FP8X4),
                         rhs_scale=ws[:, g * N : (g + 1) * N],
                         start=(g == 0),
                         stop=(g == G - 1),
                     )
-            nc.scalar.copy(shared_turned[:, 512 * c : 512 * (c + 1)], bank[:].rearrange("p j n -> p (j n)"))
-        shared_end = psum.tile([P, 512], F32, name="shared_end", tag="shared2", bufs=1)
-        multiply(shared_end[:], E, [(token_codes0_end, 0), (token_codes1_end, 0)], 512)
+            return bank
+
+        shared = [shared_product(c) for c in range(len(turned))]
+        shared_end = psum.tile([P, T - TURNED_TOKENS], F32, name="shared_end", tag="bank", bufs=5)
+        multiply(shared_end[:], E, [token_operand(g, TURNED_TOKENS) for g in range(G)], T - TURNED_TOKENS)
 
         across = []
-        for c in range(2):
-            t = at("first%d" % c, [P, 512], F32, raw_at(9) + 2 * c)
-            nc.scalar.activation(t[:], y[:].indirect(pos1_t[:, 32 * c : 32 * (c + 1)]), COPY)
-            across.append(psum.tile([P, 4, P], F32, name="across", tag="bank", bufs=5))
-            for j in range(4):
-                turn(across[c][:, j, :], [t[:, P * j : P * (j + 1)]])
         backs = []
-        for c in range(2):
-            backs.append(psum.tile([P, 4, P], F32, name="back", tag="shared%d" % c, bufs=1))
-            for j in range(4):
-                block = 4 * c + j
+
+        def fetch_first(c):
+            t0, t1 = turned[c]
+            t = at("first%d" % c, [P, t1 - t0], F32, raw_at(9) + 2 * c)
+            nc.scalar.activation(t[:], y[:].indirect(pos1_t[:, t0 // 16 : t1 // 16]), COPY)
+            across.append(psum.tile([P, (t1 - t0) // P, P], F32, name="across", tag="bank", bufs=5))
+            for j in range((t1 - t0) // P):
+                turn(across[c][:, j, :], [t[:, P * j : P * (j + 1)]])
+
+        def scale_and_turn_back(c):
+            t0, t1 = turned[c]
+            nc.scalar.copy(shared_turned[:, t0:t1], shared[c][:].rearrange("p j n -> p (j n)"))
+            backs.append(psum.tile([P, (t1 - t0) // P, P], F32, name="back", tag="shared%d" % c, bufs=1))
+            for j in range((t1 - t0) // P):
+                block = t0 // P + j
                 cols = slice(P * block, P * (block + 1))
                 scale = gate_columns[:, block : block + 1]
                 nc.scalar.activation(first_turned[:, cols], across[c][:, j, :], COPY, scale=scale)
                 turn(backs[c][:, j, :], [shared_turned[:, cols], first_turned[:, cols]])
+
+        for c in range(len(turned)):
+            fetch_first(c)
+        for c in range(len(turned)):
+            scale_and_turn_back(c)
 
         def fetch(dst, pos, t0, t1, gates):
             nc.vector.tensor_tensor(dst, y[:].indirect(pos[:, t0 // 16 : t1 // 16]), gates, MULT)
@@ -315,8 +336,8 @@ def tile_moe_shr_lin_bias_kernel(tc, xT, w, b, gate, offs, pos1, pos2, out):
         fetch(last_first[:], pos1_t, TURNED_TOKENS, T, first_gate[:])
         fetch(second[:, 1024:], pos2_t, 1024, T, second_gate[:, 1024:])
         fetch(second[:, :512], pos2_t, 0, 512, second_gate[:, :512])
-        nc.vector.tensor_tensor(last_first[:], last_first[:], second[:, 1024:], ADD)
+        nc.vector.tensor_tensor(last_first[:], last_first[:], second[:, TURNED_TOKENS:], ADD)
         fetch(second[:, 512:1024], pos2_t, 512, 1024, second_gate[:, 512:1024])
-        close(1024, T, shared_end[:], last_first[:])
-        close(0, 512, backs[0][:].rearrange("p j n -> p (j n)"), second[:, :512])
-        close(512, 1024, backs[1][:].rearrange("p j n -> p (j n)"), second[:, 512:1024])
+        close(TURNED_TOKENS, T, shared_end[:], last_first[:])
+        for c, (t0, t1) in enumerate(turned):
+            close(t0, t1, backs[c][:].rearrange("p j n -> p (j n)"), second[:, t0:t1])

@@ -109,16 +109,18 @@ def tile_moe_shr_lin_bias_kernel(tc, xT, w, b, gate, offs, pos1, pos2, out):
             return weave("slots%d%d" % (g, q), halves, 0, PIECE, kib or (SLOTS_0, SLOTS_1)[g] + 8 * q)
 
         def w_slot(e):
-            return 5 + e if e < 6 else e - 6 if e < 16 else 7 if e == 19 else e - 5 if e < 21 else e - 21
+            return 5 + e if e < 6 else e - 6 if e < 16 else e - 5 if e < 21 else e - 21
 
-        def load_and_cast_w(e, engine, cell, first):
-            raw = at("w%d" % e, [P, G, 4, N], F32, raw_at(w_slot(e)))
-            nc.sync.dma_start(raw[:], w_view[:, e])
-            dst = cell[:, (e - first) * 1024 : (e - first + 1) * 1024]
+        def load_and_cast_w(e, engine, cell, first, n=1):
+            kib = PLANE_C + 4 * (e - 19) if e in (19, 20) else raw_at(w_slot(e))
+            raw = at("w%d" % e, [P, n * G, 4, N], F32, kib)
+            for k in range(n):
+                nc.sync.dma_start(raw[:, k * G : (k + 1) * G], w_view[:, e + k])
+            dst = cell[:, (e - first) * 1024 : (e - first + n) * 1024]
             if engine == "G":
-                cast("G", dst.rearrange("p (g n j) -> p g n j", g=G, j=4), raw[:].rearrange("p g j n -> p g n j"))
+                cast("G", dst.rearrange("p (g n j) -> p g n j", n=N, j=4), raw[:].rearrange("p g j n -> p g n j"))
             else:
-                to = dst.rearrange("p (g c i j) -> p g c j i", g=G, i=4, j=4)
+                to = dst.rearrange("p (g c i j) -> p g c j i", c=N // 4, i=4, j=4)
                 cast(engine, to, raw[:].rearrange("p g j (c i) -> p g c j i", i=4))
 
         def quantise(name, src, codes_kib, scales_kib):
@@ -178,8 +180,7 @@ def tile_moe_shr_lin_bias_kernel(tc, xT, w, b, gate, offs, pos1, pos2, out):
         w4 = at("w_cell4", [P, 2 * 1024], BF16, W_4)
         for e in range(4):
             load_and_cast_w(e, "G", w0, 0)
-        for e in (4, 5):
-            load_and_cast_w(e, "G", w4, 4)
+        load_and_cast_w(4, "G", w4, 4, 2)
         tokens0 = weave("tokens0", tables[0][:], 0, 1024, TOKENS_0)
         tokens0_end = weave("tokens0_end", tables[0][:], 1024, 512, TOKENS_0_END)
         slots0 = [group_slots(0, 0), group_slots(0, 1)]
@@ -209,39 +210,34 @@ def tile_moe_shr_lin_bias_kernel(tc, xT, w, b, gate, offs, pos1, pos2, out):
         w12 = at("w_cell12", [P, 4 * 1024], BF16, W_12)
         w16 = at("w_cell16", [P, 4 * 1024], BF16, W_16)
         w20 = at("w_cell20", [P, 4 * 1024], BF16, W_20)
-        load_and_cast_w(6, "G", w6, 6)
-        load_and_cast_w(7, "G", w6, 6)
+        load_and_cast_w(6, "G", w6, 6, 2)
+        load_and_cast_w(8, "G", w6, 6, 2)
         tokens1 = weave("tokens1", tables[1][:], 0, 1024, TOKENS_1)
         tokens1_end = weave("tokens1_end", tables[1][:], 1024, 512, TOKENS_1_END)
-        load_and_cast_w(8, "S", w6, 6)
-        load_and_cast_w(9, "S", w6, 6)
-        load_and_cast_w(10, "G", w6, 6)
-        load_and_cast_w(11, "G", w6, 6)
+        load_and_cast_w(10, "S", w6, 6)
+        load_and_cast_w(11, "S", w6, 6)
         nc.sync.dma_start(b_t[:], b)
-        nc.sync.dma_start(pos1_t[:], pos1)
-        nc.sync.dma_start(pos2_t[:], pos2)
         nc.sync.dma_start(gate_rows[:], gate[0].rearrange("n (c t) -> (n c) t", t=P)[:P])
         gate_bank = psum.tile([P, P], F32, name="gate_bank", tag="shared0", bufs=1)
         turn(gate_bank[:], [gate_rows[:]])
         nc.scalar.copy(gate_columns[:], gate_bank[:, : T // P])
-        slots1 = [group_slots(1, 0), group_slots(1, 1)]
-        for e in (12, 13, 14):
-            load_and_cast_w(e, "G", w12, 12)
-        load_and_cast_w(15, "S", w12, 12)
-        load_and_cast_w(16, "G", w16, 16)
+        slots1 = [group_slots(1, 0, raw_at(w_slot(10))), group_slots(1, 1, SLOTS_0 + 8)]
+        load_and_cast_w(12, "G", w12, 12, 2)
+        load_and_cast_w(14, "G", w12, 12, 2)
+        load_and_cast_w(16, "S", w16, 16)
         load_and_cast_w(17, "G", w16, 16)
         load_and_cast_w(18, "S", w16, 16)
         slots1.append(group_slots(1, 2, raw_at(w_slot(18))))
         load_and_cast_w(19, "S", w16, 16)
 
-        y = at("y", [P, S], F32, PLANE_B + 4)
+        y = at("y", [P, S], F32, PLANE_A + 4)
         held_by_gpsimd = raw_at(w_slot(17))
         slot_codes[1, 0] = quantise("s10", slots1[0][:], SPARE + 4, held_by_gpsimd)
         quantise_w(w6, 6, 6, 2, TABLES + 16, held_by_gpsimd + 1)
-        quantise_w(w6, 6, 8, 4, SLOTS_1, SLOTS_1 + 4)
+        quantise_w(w6, 6, 8, 4, raw_at(w_slot(10)), raw_at(w_slot(11)))
         slot_codes[1, 1] = quantise("s11", slots1[1][:], TABLES + 18, held_by_gpsimd + 2)
         quantise_w(w12, 12, 12, 4, SLOTS_0 + 16, SLOTS_0 + 20)
-        slot_codes[1, 2] = quantise("s12", slots1[2][:], SLOTS_1 + 8, SLOTS_1 + 12)
+        slot_codes[1, 2] = quantise("s12", slots1[2][:], SLOTS_0 + 8, SLOTS_0 + 12)
         quantise_w(w16, 16, 16, 4, W_12, W_12 + 4)
         expert_bank(0, 4)
         expert_bank(4, 4)
@@ -254,23 +250,26 @@ def tile_moe_shr_lin_bias_kernel(tc, xT, w, b, gate, offs, pos1, pos2, out):
         load_and_cast_w(23, "V", w20, 20)
         quantise_w(w20, 20, 22, 2, raw_at(14), raw_at(14) + 2)
         expert_bank(16, 4)
-        expert_bank(20, 4)
+        expert_bank(20, 2)
+        expert_bank(22, 2)
         w24 = at("w_cell24", [P, 1024], BF16, W_SHARED)
         load_and_cast_w(E, "V", w24, E)
+        nc.sync.dma_start(pos1_t[:], pos1)
+        nc.sync.dma_start(pos2_t[:], pos2)
         token_codes1 = quantise("t1", tokens1[:], W_16, W_20 + 6)
         quantise_w(w24, E, E, 1, W_20 + 4, W_20 + 5)
         token_codes1_end = quantise("t1e", tokens1_end[:], W_20, W_20 + 2)
 
-        second_gate = at("second_gate", [P, T], F32, raw_at(4))
+        second_gate = at("second_gate", [P, T], F32, SLOTS_1)
         nc.sync.dma_start(second_gate[:], gate[1])
         first_gate = at("first_gate", [P, T - TURNED_TOKENS], F32, raw_at(6))
         nc.sync.dma_start(first_gate[:], gate[0, :, TURNED_TOKENS:])
         wc, ws = w_codes[E][0]
-        shared_turned = at("shared_turned", [P, TURNED_TOKENS], F32, SLOTS_0 + 8)
+        shared_turned = at("shared_turned", [P, TURNED_TOKENS], F32, SLOTS_1 + 8)
         first_turned = at("first_turned", [P, TURNED_TOKENS], F32, raw_at(7))
         second = at("second", [P, T], F32, raw_at(13))
         last_first = at("last_first", [P, T - TURNED_TOKENS], F32, raw_at(15))
-        total = at("total", [P, T], F32, PLANE_A)
+        total = at("total", [P, T], F32, PLANE_C)
         turned = [(t0, min(t0 + 512, TURNED_TOKENS)) for t0 in range(0, TURNED_TOKENS, 512)]
 
         def token_operand(g, t0):

@@ -52,11 +52,10 @@ def tile_moe_shr_lin_bias_kernel(tc, xT, w, b, gate, offs, pos1, pos2, out):
 
         ident = held.tile([P, P], F32, name="ident")
         gate_rows = held.tile([P, P], F32, name="gate_rows")
-        gate_columns = held.tile([P, T // P], F32, name="gate_columns")
         make_identity(nc, ident[:])
 
         x_view = xT.rearrange("(g p j) t -> g p j t", g=G, j=4)
-        w_view = w.rearrange("e (g p j) n -> p e g j n", g=G, j=4)
+        w_view = w.rearrange("e (g p j) n -> p (e g) j n", g=G, j=4)
 
         def at(name, shape, dtype, kib):
             return room.tile(shape, dtype, name=name, offset=kib * KB, align_bytes=64)
@@ -114,8 +113,7 @@ def tile_moe_shr_lin_bias_kernel(tc, xT, w, b, gate, offs, pos1, pos2, out):
         def load_and_cast_w(e, engine, cell, first, n=1):
             kib = PLANE_C + 4 * (e - 19) if e in (19, 20) else raw_at(w_slot(e))
             raw = at("w%d" % e, [P, n * G, 4, N], F32, kib)
-            for k in range(n):
-                nc.sync.dma_start(raw[:, k * G : (k + 1) * G], w_view[:, e + k])
+            nc.sync.dma_start(raw[:], w_view[:, G * e : G * (e + n)])
             dst = cell[:, (e - first) * 1024 : (e - first + n) * 1024]
             if engine == "G":
                 cast("G", dst.rearrange("p (g n j) -> p g n j", n=N, j=4), raw[:].rearrange("p g j n -> p g n j"))
@@ -171,8 +169,7 @@ def tile_moe_shr_lin_bias_kernel(tc, xT, w, b, gate, offs, pos1, pos2, out):
         load_x(0, 0, 0, 1024, raw_at(0), (("V", 1024 - head), ("S", head)))
         load_x(0, 0, 1024, 512, raw_at(2), (("V", 256 - head // 2), ("S", head // 2)), cut=256)
         nc.sync.dma_start(offs_t[:], offs)
-        load_x(0, 1, 0, 512, raw_at(3), (("G", 512),))
-        load_x(0, 1, 512, 512, raw_at(4), (("S", 512),))
+        load_x(0, 1, 0, 1024, raw_at(3), (("G", 512), ("S", 512)))
         load_x(0, 1, 1024, 512, PLANE_C, (("S", 512),))
         for u, q in ((0, 0), (0, 1), (1, 0), (1, 1), (0, 2), (1, 2)):
             gather(0, u, q, PLANE_A + 8 * q)
@@ -185,9 +182,8 @@ def tile_moe_shr_lin_bias_kernel(tc, xT, w, b, gate, offs, pos1, pos2, out):
         tokens0_end = weave("tokens0_end", tables[0][:], 1024, 512, TOKENS_0_END)
         slots0 = [group_slots(0, 0), group_slots(0, 1)]
         load_x(1, 0, 0, 512, raw_at(11), (("S", 512),))
-        load_x(1, 0, 512, 512, raw_at(12), (("S", 512),))
         slots0.append(group_slots(0, 2))
-        load_x(1, 0, 1024, 512, raw_at(13), (("S", 512),))
+        load_x(1, 0, 512, 1024, raw_at(12), (("S", 1024),))
         load_x(1, 1, 0, 1024, raw_at(14), (("S", 1024),))
         load_x(1, 1, 1024, 512, PLANE_A, (("S", 512),))
 
@@ -216,11 +212,6 @@ def tile_moe_shr_lin_bias_kernel(tc, xT, w, b, gate, offs, pos1, pos2, out):
         tokens1_end = weave("tokens1_end", tables[1][:], 1024, 512, TOKENS_1_END)
         load_and_cast_w(10, "S", w6, 6)
         load_and_cast_w(11, "S", w6, 6)
-        nc.sync.dma_start(b_t[:], b)
-        nc.sync.dma_start(gate_rows[:], gate[0].rearrange("n (c t) -> (n c) t", t=P)[:P])
-        gate_bank = psum.tile([P, P], F32, name="gate_bank", tag="shared0", bufs=1)
-        turn(gate_bank[:], [gate_rows[:]])
-        nc.scalar.copy(gate_columns[:], gate_bank[:, : T // P])
         slots1 = [group_slots(1, 0, raw_at(w_slot(10))), group_slots(1, 1, SLOTS_0 + 8)]
         load_and_cast_w(12, "G", w12, 12, 2)
         load_and_cast_w(14, "G", w12, 12, 2)
@@ -229,6 +220,7 @@ def tile_moe_shr_lin_bias_kernel(tc, xT, w, b, gate, offs, pos1, pos2, out):
         load_and_cast_w(18, "S", w16, 16)
         slots1.append(group_slots(1, 2, raw_at(w_slot(18))))
         load_and_cast_w(19, "S", w16, 16)
+        nc.sync.dma_start(b_t[:], b)
 
         y = at("y", [P, S], F32, PLANE_A + 4)
         held_by_gpsimd = raw_at(w_slot(17))
@@ -254,6 +246,11 @@ def tile_moe_shr_lin_bias_kernel(tc, xT, w, b, gate, offs, pos1, pos2, out):
         expert_bank(22, 2)
         w24 = at("w_cell24", [P, 1024], BF16, W_SHARED)
         load_and_cast_w(E, "V", w24, E)
+        nc.sync.dma_start(gate_rows[:], gate[0].rearrange("n (c t) -> (n c) t", t=P)[:P])
+        gate_bank = psum.tile([P, P], F32, name="gate_bank", tag="shared0", bufs=1)
+        turn(gate_bank[:], [gate_rows[:]])
+        gate_columns = at("gate_columns", [P, T // P], F32, raw_at(w_slot(22)))
+        nc.scalar.copy(gate_columns[:], gate_bank[:, : T // P])
         nc.sync.dma_start(pos1_t[:], pos1)
         nc.sync.dma_start(pos2_t[:], pos2)
         token_codes1 = quantise("t1", tokens1[:], W_16, W_20 + 6)
@@ -303,7 +300,7 @@ def tile_moe_shr_lin_bias_kernel(tc, xT, w, b, gate, offs, pos1, pos2, out):
 
         def fetch_first(c):
             t0, t1 = turned[c]
-            t = at("first%d" % c, [P, t1 - t0], F32, raw_at(9) + 2 * c)
+            t = at("first%d" % c, [P, t1 - t0], F32, SLOTS_1 + 16 + 2 * c)
             nc.scalar.activation(t[:], y[:].indirect(pos1_t[:, t0 // 16 : t1 // 16]), COPY)
             across.append(psum.tile([P, (t1 - t0) // P, P], F32, name="across", tag="bank", bufs=5))
             for j in range((t1 - t0) // P):

@@ -22,18 +22,19 @@ IDENTITY = mybir.ActivationFunctionType.Identity
 COPY = mybir.ActivationFunctionType.Copy
 
 TABLES = 0
-PLANE_A, PLANE_B, PLANE_C = 24, 32, 40
-TOKENS_0, TOKENS_0_END, TOKENS_1_END = 48, 56, 60
-SLOTS_0 = 64
-W_4 = 88
-W_0, W_12, W_16, W_20, W_SHARED = 92, 100, 108, 116, 124
-TOKENS_1 = 126
-SLOTS_1 = 134
-RAW = 160
-SPARE = 224
+PLANES_0 = 24
+CODES_2 = 24
+SLOTS_0 = 48
+Y = 52
+TOKENS_0, TOKENS_0_END, TOKENS_1 = 56, 64, 68
+PLANES_11 = 60
+CELLS = 80
+RAW = 124
+SPARE = 192
+CELL_6, CELL_0, PLANES_10 = 208, 214, 216
 
 SCALAR_HEAD_TOKENS = 160
-TURNED_TOKENS = 1280
+TURNED_TOKENS = 1152
 
 FLOPS = 2 * K * N * (S + T)
 
@@ -51,17 +52,19 @@ def tile_moe_shr_lin_bias_kernel(tc, xT, w, b, gate, offs, pos1, pos2, out):
         b_t = held.tile([P, E + 1], F32, name="b_t")
 
         ident = held.tile([P, P], F32, name="ident")
-        gate_rows = held.tile([P, P], F32, name="gate_rows")
         make_identity(nc, ident[:])
 
         x_view = xT.rearrange("(g p j) t -> g p j t", g=G, j=4)
         w_view = w.rearrange("e (g p j) n -> p (e g) j n", g=G, j=4)
 
         def at(name, shape, dtype, kib):
-            return room.tile(shape, dtype, name=name, offset=kib * KB, align_bytes=64)
+            return room.tile(shape, dtype, name=name, offset=int(kib * KB), align_bytes=64)
 
         def raw_at(slot):
             return RAW + 4 * slot
+
+        def cell_at(e):
+            return CELLS + 2 * e
 
         tables = [at("table%d" % g, [P, 2 * 2 * T], BF16, TABLES + 12 * g) for g in range(G)]
 
@@ -86,35 +89,40 @@ def tile_moe_shr_lin_bias_kernel(tc, xT, w, b, gate, offs, pos1, pos2, out):
                     cast(engine, dst[:, a : a + tokens, :], src[:, a : a + tokens, :])
                     a = a + tokens
 
-        planes = {}
+        def planes_at(g, s0, n, kib):
+            return (at("planes%d_%d" % (g, s0), [P, 2, 2 * n], BF16, kib), g, s0, n)
 
-        def gather(g, u, q, kib=None):
-            if u == 0:
-                planes[g, q] = at("planes%d%d" % (g, q), [P, 2, 2 * PIECE], BF16, kib)
+        def gather(piece, u):
+            planes, g, s0, n = piece
             window = tables[g][:].bitcast(U32)[:, u * T : (u + 1) * T]
-            nc.vector.tensor_copy(
-                planes[g, q][:, u, :].bitcast(U32),
-                window.indirect(offs_t[:, q * PIECE // 16 : (q + 1) * PIECE // 16]),
-            )
+            nc.vector.tensor_copy(planes[:, u, :].bitcast(U32), window.indirect(offs_t[:, s0 // 16 : (s0 + n) // 16]))
 
-        def weave(name, halves, t0, n, kib):
+        def weave(engine, name, halves, t0, n, kib):
             t = at(name, [P, 4 * n], BF16, kib)
-            words = halves.bitcast(F32).rearrange("p (u n) -> p n u", u=2)[:, t0 : t0 + n, :]
-            nc.scalar.copy(t[:].bitcast(F32).rearrange("p (n u) -> p n u", u=2), words)
+            words = halves.bitcast(U32).rearrange("p (u n) -> p n u", u=2)[:, t0 : t0 + n, :]
+            to = t[:].bitcast(U32).rearrange("p (n u) -> p n u", u=2)
+            if engine == "S":
+                nc.scalar.copy(to, words)
+            else:
+                nc.gpsimd.tensor_copy(to, words)
             return t
 
-        def group_slots(g, q, kib=None):
-            halves = planes[g, q][:].rearrange("p u m -> p (u m)")
-            return weave("slots%d%d" % (g, q), halves, 0, PIECE, kib or (SLOTS_0, SLOTS_1)[g] + 8 * q)
+        def group_slots(engine, piece, kib):
+            planes, g, s0, n = piece
+            return weave(engine, "slots%d_%d" % (g, s0), planes[:].rearrange("p u m -> p (u m)"), 0, n, kib)
 
-        def w_slot(e):
-            return 5 + e if e < 6 else e - 6 if e < 16 else e - 5 if e < 21 else e - 21
+        cells = {}
 
-        def load_and_cast_w(e, engine, cell, first, n=1):
-            kib = PLANE_C + 4 * (e - 19) if e in (19, 20) else raw_at(w_slot(e))
+        def cell(first, n, kib=None):
+            t = at("cell%d" % first, [P, n * 1024], BF16, kib or cell_at(first))
+            for k in range(n):
+                cells[first + k] = (t, k)
+
+        def load_and_cast_w(e, engine, kib, n=1):
             raw = at("w%d" % e, [P, n * G, 4, N], F32, kib)
             nc.sync.dma_start(raw[:], w_view[:, G * e : G * (e + n)])
-            dst = cell[:, (e - first) * 1024 : (e - first + n) * 1024]
+            t, k = cells[e]
+            dst = t[:, k * 1024 : (k + n) * 1024]
             if engine == "G":
                 cast("G", dst.rearrange("p (g n j) -> p g n j", n=N, j=4), raw[:].rearrange("p g j n -> p g n j"))
             else:
@@ -130,11 +138,18 @@ def tile_moe_shr_lin_bias_kernel(tc, xT, w, b, gate, offs, pos1, pos2, out):
 
         w_codes = {}
 
-        def quantise_w(cell, first, e0, n, codes_kib, scales_kib):
-            src = cell[:, (e0 - first) * 1024 : (e0 - first + n) * 1024]
-            pair = quantise("w%d" % e0, src, codes_kib, scales_kib)
+        def quantise_w(e0, n, codes_kib, scales_kib):
+            t, k0 = cells[e0]
+            pair = quantise("w%d" % e0, t[:, k0 * 1024 : (k0 + n) * 1024], codes_kib, scales_kib)
             for k in range(n):
                 w_codes[e0 + k] = (pair, k * G * N)
+
+        slot_codes = {}
+
+        def quantise_slots(g, s0, src, codes_kib, scales_kib):
+            pair = quantise("s%d_%d" % (g, s0), src, codes_kib, scales_kib)
+            for k in range(src.shape[1] // 4 // C):
+                slot_codes[g, s0 // C + k] = (pair, k * C)
 
         def multiply(dst, e, moving, width):
             (c, s), col = w_codes[e]
@@ -154,13 +169,16 @@ def tile_moe_shr_lin_bias_kernel(tc, xT, w, b, gate, offs, pos1, pos2, out):
             for k, term in enumerate(terms):
                 nc.tensor.matmul(dst, term, ident[:], start=(k == 0), stop=(k == len(terms) - 1), is_transpose=True)
 
-        slot_codes = {}
+        def turn_onto(dst, term, start, stop):
+            nc.tensor.matmul(dst, term, ident[:], start=start, stop=stop, is_transpose=True)
 
-        def expert_bank(e0, n):
-            bank = psum.tile([P, n, C], F32, name="bank", tag="bank", bufs=5)
+        def bank_at(name, shape, number):
+            return psum.tile(shape, F32, name=name, offset=number * 2 * KB)
+
+        def expert_bank(e0, n, number):
+            bank = bank_at("bank%d" % e0, [P, n, C], number)
             for k in range(n):
-                q, col = divmod((e0 + k) * C, PIECE)
-                multiply(bank[:, k, :], e0 + k, [(slot_codes[g, q], col) for g in range(G)], C)
+                multiply(bank[:, k, :], e0 + k, [slot_codes[g, e0 + k] for g in range(G)], C)
             for k in range(n):
                 e = e0 + k
                 nc.scalar.activation(y[:, e * C : (e + 1) * C], bank[:, k, :], IDENTITY, bias=b_t[:, e : e + 1])
@@ -170,118 +188,115 @@ def tile_moe_shr_lin_bias_kernel(tc, xT, w, b, gate, offs, pos1, pos2, out):
         load_x(0, 0, 1024, 512, raw_at(2), (("V", 256 - head // 2), ("S", head // 2)), cut=256)
         nc.sync.dma_start(offs_t[:], offs)
         load_x(0, 1, 0, 1024, raw_at(3), (("G", 512), ("S", 512)))
-        load_x(0, 1, 1024, 512, PLANE_C, (("S", 512),))
+        load_x(0, 1, 1024, 512, PLANES_0 + 16, (("S", 512),))
+        pieces0 = [planes_at(0, PIECE * q, PIECE, PLANES_0 + 8 * q) for q in range(3)]
         for u, q in ((0, 0), (0, 1), (1, 0), (1, 1), (0, 2), (1, 2)):
-            gather(0, u, q, PLANE_A + 8 * q)
-        w0 = at("w_cell0", [P, 4 * 1024], BF16, W_0)
-        w4 = at("w_cell4", [P, 2 * 1024], BF16, W_4)
+            gather(pieces0[q], u)
+        cell(0, 4)
+        cell(4, 2, 72)
         for e in range(4):
-            load_and_cast_w(e, "G", w0, 0)
-        load_and_cast_w(4, "G", w4, 4, 2)
-        tokens0 = weave("tokens0", tables[0][:], 0, 1024, TOKENS_0)
-        tokens0_end = weave("tokens0_end", tables[0][:], 1024, 512, TOKENS_0_END)
-        slots0 = [group_slots(0, 0), group_slots(0, 1)]
+            load_and_cast_w(e, "G", raw_at(5 + e))
+        load_and_cast_w(4, "G", raw_at(9), 2)
+        tokens0 = weave("S", "tokens0", tables[0][:], 0, 1024, TOKENS_0)
+        tokens0_end = weave("S", "tokens0_end", tables[0][:], 1024, 512, TOKENS_0_END)
+        slots0 = [group_slots("S", pieces0[q], (SLOTS_0, SPARE + 20)[q]) for q in range(2)]
         load_x(1, 0, 0, 512, raw_at(11), (("S", 512),))
-        slots0.append(group_slots(0, 2))
-        load_x(1, 0, 512, 1024, raw_at(12), (("S", 1024),))
-        load_x(1, 1, 0, 1024, raw_at(14), (("S", 1024),))
-        load_x(1, 1, 1024, 512, PLANE_A, (("S", 512),))
+        slots0.append(group_slots("S", pieces0[2], raw_at(11)))
+        load_x(1, 0, 512, 1024, raw_at(13), (("S", 1024),))
+        load_x(1, 1, 0, 1024, raw_at(15), (("S", 1024),))
+        load_x(1, 1, 1024, 512, SPARE + 28, (("S", 512),))
 
-        held_by_gpsimd = raw_at(w_slot(5))
-        token_codes0 = quantise("t0", tokens0[:], SPARE, held_by_gpsimd)
-        quantise_w(w0, 0, 0, 4, TABLES + 4, held_by_gpsimd + 1)
-        slot_codes[0, 0] = quantise("s00", slots0[0][:], TOKENS_0, TOKENS_0 + 4)
-        token_codes0_end = quantise("t0e", tokens0_end[:], W_0, W_0 + 4)
-        slot_codes[0, 1] = quantise("s01", slots0[1][:], SLOTS_0, SLOTS_0 + 4)
-        slot_codes[0, 2] = quantise("s02", slots0[2][:], TOKENS_0_END, TABLES + 8)
-        quantise_w(w4, 4, 4, 2, TABLES + 9, TABLES + 11)
+        token_codes = {}
+        token_codes[0, 0] = quantise("t0", tokens0[:], SPARE, SPARE + 39)
+        quantise_w(0, 4, SPARE + 16, TABLES + 3)
+        quantise_slots(0, 0, slots0[0][:], SPARE + 4, TABLES)
+        token_codes[0, 1024] = quantise("t0e", tokens0_end[:], TABLES + 4, TABLES + 6)
+        quantise_slots(0, 1024, slots0[1][:], SPARE + 8, TABLES + 1)
+        quantise_slots(0, 2048, slots0[2][:], SPARE + 12, TABLES + 2)
+        quantise_w(4, 2, TABLES + 7, PLANES_0 + 23.5)
 
-        gather(1, 0, 0, SLOTS_0 + 8)
-        gather(1, 0, 1, PLANE_B)
-        gather(1, 1, 0)
-        gather(1, 1, 1)
-        gather(1, 0, 2, PLANE_A)
-        gather(1, 1, 2)
-        w6 = at("w_cell6", [P, 6 * 1024], BF16, SLOTS_0 + 16)
-        w12 = at("w_cell12", [P, 4 * 1024], BF16, W_12)
-        w16 = at("w_cell16", [P, 4 * 1024], BF16, W_16)
-        w20 = at("w_cell20", [P, 4 * 1024], BF16, W_20)
-        load_and_cast_w(6, "G", w6, 6, 2)
-        load_and_cast_w(8, "G", w6, 6, 2)
-        tokens1 = weave("tokens1", tables[1][:], 0, 1024, TOKENS_1)
-        tokens1_end = weave("tokens1_end", tables[1][:], 1024, 512, TOKENS_1_END)
-        load_and_cast_w(10, "S", w6, 6)
-        load_and_cast_w(11, "S", w6, 6)
-        slots1 = [group_slots(1, 0, raw_at(w_slot(10))), group_slots(1, 1, SLOTS_0 + 8)]
-        load_and_cast_w(12, "G", w12, 12, 2)
-        load_and_cast_w(14, "G", w12, 12, 2)
-        load_and_cast_w(16, "S", w16, 16)
-        load_and_cast_w(17, "G", w16, 16)
-        load_and_cast_w(18, "S", w16, 16)
-        slots1.append(group_slots(1, 2, raw_at(w_slot(18))))
-        load_and_cast_w(19, "S", w16, 16)
+        piece10 = planes_at(1, 0, PIECE, raw_at(12) + 2)
+        piece11 = planes_at(1, PIECE, PIECE, SPARE + 22)
+        piece12 = planes_at(1, 2 * PIECE, PIECE, SPARE + 30)
+        for piece in (piece10, piece11, piece12):
+            gather(piece, 0)
+            gather(piece, 1)
+        cell(6, 4, raw_at(10) + 2)
+        cell(10, 2)
+        cell(12, 4)
+        cell(16, 4)
+        cell(20, 2)
+        load_and_cast_w(6, "G", raw_at(0), 2)
+        load_and_cast_w(8, "G", raw_at(2), 2)
+        tokens1 = weave("S", "tokens1", tables[1][:], 0, 1024, raw_at(15))
+        tokens1_end = weave("S", "tokens1_end", tables[1][:], 1024, 512, PLANES_0 + 8)
+        load_and_cast_w(10, "S", raw_at(4))
+        slots10 = group_slots("S", piece10, 84)
+        load_and_cast_w(11, "S", raw_at(5))
+        slots11 = group_slots("S", piece11, 92)
+        load_and_cast_w(12, "G", raw_at(6), 2)
+        load_and_cast_w(14, "G", PLANES_0, 2)
+        load_and_cast_w(16, "S", raw_at(8))
+        load_and_cast_w(17, "G", 76)
+        load_and_cast_w(18, "S", 68)
+        slots12 = group_slots("S", piece12, 68)
+        load_and_cast_w(19, "S", raw_at(9))
         nc.sync.dma_start(b_t[:], b)
+        load_and_cast_w(20, "S", TOKENS_0)
+        load_and_cast_w(21, "S", raw_at(0))
 
-        y = at("y", [P, S], F32, PLANE_A + 4)
-        held_by_gpsimd = raw_at(w_slot(17))
-        slot_codes[1, 0] = quantise("s10", slots1[0][:], SPARE + 4, held_by_gpsimd)
-        quantise_w(w6, 6, 6, 2, TABLES + 16, held_by_gpsimd + 1)
-        quantise_w(w6, 6, 8, 4, raw_at(w_slot(10)), raw_at(w_slot(11)))
-        slot_codes[1, 1] = quantise("s11", slots1[1][:], TABLES + 18, held_by_gpsimd + 2)
-        quantise_w(w12, 12, 12, 4, SLOTS_0 + 16, SLOTS_0 + 20)
-        slot_codes[1, 2] = quantise("s12", slots1[2][:], SLOTS_0 + 8, SLOTS_0 + 12)
-        quantise_w(w16, 16, 16, 4, W_12, W_12 + 4)
-        expert_bank(0, 4)
-        expert_bank(4, 4)
-        load_and_cast_w(20, "S", w20, 20)
-        load_and_cast_w(21, "S", w20, 20)
-        quantise_w(w20, 20, 20, 2, raw_at(13), raw_at(13) + 2)
-        expert_bank(8, 4)
-        expert_bank(12, 4)
-        load_and_cast_w(22, "S", w20, 20)
-        load_and_cast_w(23, "V", w20, 20)
-        quantise_w(w20, 20, 22, 2, raw_at(14), raw_at(14) + 2)
-        expert_bank(16, 4)
-        expert_bank(20, 2)
-        expert_bank(22, 2)
-        w24 = at("w_cell24", [P, 1024], BF16, W_SHARED)
-        load_and_cast_w(E, "V", w24, E)
+        y = at("y", [P, S], F32, SLOTS_0)
+        quantise_w(6, 4, 60, 64)
+        quantise_slots(1, 0, slots10[:], 36, 46)
+        quantise_w(10, 2, 44, 47)
+        quantise_slots(1, 1024, slots11[:], 40, 65)
+        quantise_w(12, 4, 76, TABLES + 9)
+        quantise_slots(1, 2048, slots12[:], SPARE + 34, TABLES + 10)
+        cell(22, 2, raw_at(5))
+        cell(24, 1, raw_at(0))
+        load_and_cast_w(22, "V", raw_at(2))
+        quantise_w(16, 4, SPARE + 20, TABLES + 11)
+        load_and_cast_w(23, "V", raw_at(3))
+        quantise_w(20, 2, 82, cell_at(10))
+        quantise_w(22, 2, cell_at(11), raw_at(0) + 3.5)
+        for e in range(0, 20, 4):
+            expert_bank(e, 4, e // 4)
+        expert_bank(20, 2, 0)
+        expert_bank(22, 2, 1)
+        load_and_cast_w(E, "V", raw_at(4))
+        gate_rows = held.tile([P, P], F32, name="gate_rows")
         nc.sync.dma_start(gate_rows[:], gate[0].rearrange("n (c t) -> (n c) t", t=P)[:P])
-        gate_bank = psum.tile([P, P], F32, name="gate_bank", tag="shared0", bufs=1)
+        gate_bank = bank_at("gate_bank", [P, P], 7)
         turn(gate_bank[:], [gate_rows[:]])
-        gate_columns = at("gate_columns", [P, T // P], F32, raw_at(w_slot(22)))
+        gate_columns = held.tile([P, T // P], F32, name="gate_columns")
         nc.scalar.copy(gate_columns[:], gate_bank[:, : T // P])
         nc.sync.dma_start(pos1_t[:], pos1)
         nc.sync.dma_start(pos2_t[:], pos2)
-        token_codes1 = quantise("t1", tokens1[:], W_16, W_20 + 6)
-        quantise_w(w24, E, E, 1, W_20 + 4, W_20 + 5)
-        token_codes1_end = quantise("t1e", tokens1_end[:], W_20, W_20 + 2)
+        token_codes[1, 0] = quantise("t1", tokens1[:, :2048], cell_at(13), raw_at(0) + 2)
+        quantise_w(E, 1, cell_at(10) + 1, cell_at(12))
+        token_codes[1, 512] = quantise("t1b", tokens1[:, 2048:], cell_at(14), raw_at(0) + 2.5)
+        token_codes[1, 1024] = quantise("t1e", tokens1_end[:], cell_at(15), raw_at(0) + 3)
 
-        second_gate = at("second_gate", [P, T], F32, SLOTS_1)
+        second_gate = at("second_gate", [P, T], F32, TABLES + 12)
         nc.sync.dma_start(second_gate[:], gate[1])
-        first_gate = at("first_gate", [P, T - TURNED_TOKENS], F32, raw_at(6))
+        first_gate = at("first_gate", [P, T - TURNED_TOKENS], F32, TABLES + 18)
         nc.sync.dma_start(first_gate[:], gate[0, :, TURNED_TOKENS:])
         wc, ws = w_codes[E][0]
-        shared_turned = at("shared_turned", [P, TURNED_TOKENS], F32, SLOTS_1 + 8)
-        first_turned = at("first_turned", [P, TURNED_TOKENS], F32, raw_at(7))
-        second = at("second", [P, T], F32, raw_at(13))
-        last_first = at("last_first", [P, T - TURNED_TOKENS], F32, raw_at(15))
-        total = at("total", [P, T], F32, PLANE_C)
+        second = at("second", [P, T], F32, raw_at(7))
+        last_first = at("last_first", [P, T - TURNED_TOKENS], F32, TABLES + 20)
+        total = at("total", [P, T], F32, PLANES_0)
         turned = [(t0, min(t0 + 512, TURNED_TOKENS)) for t0 in range(0, TURNED_TOKENS, 512)]
 
         def token_operand(g, t0):
-            if t0 < 1024:
-                return (token_codes0, token_codes1)[g], t0
-            return (token_codes0_end, token_codes1_end)[g], t0 - 1024
+            first = max(a for (h, a) in token_codes if h == g and a <= t0)
+            return token_codes[g, first], t0 - first
 
-        def shared_product(c):
-            t0, t1 = turned[c]
-            bank = psum.tile([P, (t1 - t0) // P, N], F32, name="shared", tag="shared%d" % c, bufs=1)
+        def shared_product(dst, t0, t1):
             for j in range((t1 - t0) // P):
                 for g in range(G):
                     (xc, xs), x0 = token_operand(g, t0 + P * j)
                     nc.tensor.matmul_mx(
-                        out=bank[:, j, :],
+                        out=dst[:, P * j : P * (j + 1)],
                         lhsT=xc[:, x0 : x0 + P].bitcast(FP8X4),
                         lhsT_scale=xs[:, x0 : x0 + P],
                         rhs=wc[:, g * N : (g + 1) * N].bitcast(FP8X4),
@@ -289,37 +304,41 @@ def tile_moe_shr_lin_bias_kernel(tc, xT, w, b, gate, offs, pos1, pos2, out):
                         start=(g == 0),
                         stop=(g == G - 1),
                     )
-            return bank
 
-        shared = [shared_product(c) for c in range(len(turned))]
-        shared_end = psum.tile([P, T - TURNED_TOKENS], F32, name="shared_end", tag="bank", bufs=5)
-        multiply(shared_end[:], E, [token_operand(g, TURNED_TOKENS) for g in range(G)], T - TURNED_TOKENS)
+        shared = [bank_at("shared%d" % c, [P, t1 - t0], (5, 6, 0)[c]) for c, (t0, t1) in enumerate(turned)]
+        for c in range(len(turned)):
+            shared_product(shared[c], *turned[c])
 
         across = []
-        backs = []
+        for c, (t0, t1) in enumerate(turned):
+            first = at("first%d" % c, [P, t1 - t0], F32, (raw_at(10) + 2, 66, 68)[c])
+            nc.scalar.activation(first[:], y[:].indirect(pos1_t[:, t0 // 16 : t1 // 16]), COPY)
+            across.append(bank_at("across%d" % c, [P, t1 - t0], 2 + c))
+            for a in range(0, t1 - t0, P):
+                turn(across[c][:, a : a + P], [first[:, a : a + P]])
 
-        def fetch_first(c):
-            t0, t1 = turned[c]
-            t = at("first%d" % c, [P, t1 - t0], F32, SLOTS_1 + 16 + 2 * c)
-            nc.scalar.activation(t[:], y[:].indirect(pos1_t[:, t0 // 16 : t1 // 16]), COPY)
-            across.append(psum.tile([P, (t1 - t0) // P, P], F32, name="across", tag="bank", bufs=5))
-            for j in range((t1 - t0) // P):
-                turn(across[c][:, j, :], [t[:, P * j : P * (j + 1)]])
+        shared_turned = at("shared_turned", [P, TURNED_TOKENS], F32, raw_at(10) + 2)
+        first_turned = at("first_turned", [P, TURNED_TOKENS], F32, raw_at(12) + 2)
+        backs = []
 
         def scale_and_turn_back(c):
             t0, t1 = turned[c]
-            nc.scalar.copy(shared_turned[:, t0:t1], shared[c][:].rearrange("p j n -> p (j n)"))
-            backs.append(psum.tile([P, (t1 - t0) // P, P], F32, name="back", tag="shared%d" % c, bufs=1))
-            for j in range((t1 - t0) // P):
-                block = t0 // P + j
-                cols = slice(P * block, P * (block + 1))
-                scale = gate_columns[:, block : block + 1]
-                nc.scalar.activation(first_turned[:, cols], across[c][:, j, :], COPY, scale=scale)
-                turn(backs[c][:, j, :], [shared_turned[:, cols], first_turned[:, cols]])
+            nc.scalar.copy(shared_turned[:, t0:t1], shared[c][:])
+            backs.append(bank_at("back%d" % c, [P, t1 - t0], 5 + c))
+            for a in range(t0, t1, P):
+                turn_onto(backs[c][:, a - t0 : a - t0 + P], shared_turned[:, a : a + P], a == t0, False)
+            for a in range(t0, t1, P):
+                scale = gate_columns[:, a // P : a // P + 1]
+                nc.scalar.activation(first_turned[:, a : a + P], across[c][:, a - t0 : a - t0 + P], COPY, scale=scale)
+                turn_onto(backs[c][:, a - t0 : a - t0 + P], first_turned[:, a : a + P], False, a == t1 - P)
 
-        for c in range(len(turned)):
-            fetch_first(c)
-        for c in range(len(turned)):
+        scale_and_turn_back(0)
+        shared_end = bank_at("shared_end", [P, T - TURNED_TOKENS], 2)
+        for t0, t1 in ((TURNED_TOKENS, T - 256), (T - 256, T)):
+            if t1 > t0:
+                cols = slice(t0 - TURNED_TOKENS, t1 - TURNED_TOKENS)
+                multiply(shared_end[:, cols], E, [token_operand(g, t0) for g in range(G)], t1 - t0)
+        for c in range(1, len(turned)):
             scale_and_turn_back(c)
 
         def fetch(dst, pos, t0, t1, gates):
@@ -334,6 +353,7 @@ def tile_moe_shr_lin_bias_kernel(tc, xT, w, b, gate, offs, pos1, pos2, out):
         fetch(second[:, :512], pos2_t, 0, 512, second_gate[:, :512])
         nc.vector.tensor_tensor(last_first[:], last_first[:], second[:, TURNED_TOKENS:], ADD)
         fetch(second[:, 512:1024], pos2_t, 512, 1024, second_gate[:, 512:1024])
+        close(0, 512, backs[0][:], second[:, :512])
         close(TURNED_TOKENS, T, shared_end[:], last_first[:])
-        for c, (t0, t1) in enumerate(turned):
-            close(t0, t1, backs[c][:].rearrange("p j n -> p (j n)"), second[:, t0:t1])
+        for c, (t0, t1) in list(enumerate(turned))[1:]:
+            close(t0, t1, backs[c][:], second[:, t0:t1])

@@ -34,7 +34,7 @@ SPARE = 192
 CELL_6, CELL_0, PLANES_10 = 208, 214, 216
 
 SCALAR_HEAD_TOKENS = 160
-TURNED_TOKENS = 1152
+TURNED_TOKENS = 1280
 
 FLOPS = 2 * K * N * (S + T)
 
@@ -125,9 +125,14 @@ def tile_moe_shr_lin_bias_kernel(tc, xT, w, b, gate, offs, pos1, pos2, out):
             dst = t[:, k * 1024 : (k + n) * 1024]
             if engine == "G":
                 cast("G", dst.rearrange("p (g n j) -> p g n j", n=N, j=4), raw[:].rearrange("p g j n -> p g n j"))
+                return
+            to = dst.rearrange("p (g c i j) -> p g c j i", c=N // 4, i=4, j=4)
+            rows = raw[:].rearrange("p g j (c i) -> p g c j i", i=4)
+            if len(engine) == 1:
+                cast(engine, to, rows)
             else:
-                to = dst.rearrange("p (g c i j) -> p g c j i", c=N // 4, i=4, j=4)
-                cast(engine, to, raw[:].rearrange("p g j (c i) -> p g c j i", i=4))
+                for g in range(G):
+                    cast(engine[g], to[:, g], rows[:, g])
 
         def quantise(name, src, codes_kib, scales_kib):
             n = src.shape[1] // 4
@@ -175,8 +180,8 @@ def tile_moe_shr_lin_bias_kernel(tc, xT, w, b, gate, offs, pos1, pos2, out):
         def bank_at(name, shape, number):
             return psum.tile(shape, F32, name=name, offset=number * 2 * KB)
 
-        def expert_bank(e0, n, number):
-            bank = bank_at("bank%d" % e0, [P, n, C], number)
+        def expert_bank(e0, n):
+            bank = psum.tile([P, n, C], F32, name="bank", tag="bank", bufs=4)
             for k in range(n):
                 multiply(bank[:, k, :], e0 + k, [slot_codes[g, e0 + k] for g in range(G)], C)
             for k in range(n):
@@ -207,11 +212,11 @@ def tile_moe_shr_lin_bias_kernel(tc, xT, w, b, gate, offs, pos1, pos2, out):
         load_x(1, 1, 1024, 512, SPARE + 28, (("S", 512),))
 
         token_codes = {}
-        token_codes[0, 0] = quantise("t0", tokens0[:], SPARE, SPARE + 39)
-        quantise_w(0, 4, SPARE + 16, TABLES + 3)
-        quantise_slots(0, 0, slots0[0][:], SPARE + 4, TABLES)
-        token_codes[0, 1024] = quantise("t0e", tokens0_end[:], TABLES + 4, TABLES + 6)
-        quantise_slots(0, 1024, slots0[1][:], SPARE + 8, TABLES + 1)
+        token_codes[0, 0] = quantise("t0", tokens0[:], SPARE, raw_at(10))
+        quantise_w(0, 4, SPARE + 16, raw_at(10) + 1)
+        quantise_slots(0, 0, slots0[0][:], SPARE + 4, TOKENS_0 + 7)
+        token_codes[0, 1024] = quantise("t0e", tokens0_end[:], TABLES + 4, cell_at(0))
+        quantise_slots(0, 1024, slots0[1][:], SPARE + 8, SLOTS_0)
         quantise_slots(0, 2048, slots0[2][:], SPARE + 12, TABLES + 2)
         quantise_w(4, 2, TABLES + 7, PLANES_0 + 23.5)
 
@@ -222,81 +227,86 @@ def tile_moe_shr_lin_bias_kernel(tc, xT, w, b, gate, offs, pos1, pos2, out):
             gather(piece, 0)
             gather(piece, 1)
         cell(6, 4, raw_at(10) + 2)
-        cell(10, 2)
-        cell(12, 4)
-        cell(16, 4)
-        cell(20, 2)
+        cell(10, 4, 100)
+        cell(14, 4, 108)
+        cell(18, 2, 116)
         load_and_cast_w(6, "G", raw_at(0), 2)
         load_and_cast_w(8, "G", raw_at(2), 2)
         tokens1 = weave("S", "tokens1", tables[1][:], 0, 1024, raw_at(15))
         tokens1_end = weave("S", "tokens1_end", tables[1][:], 1024, 512, PLANES_0 + 8)
         load_and_cast_w(10, "S", raw_at(4))
         slots10 = group_slots("S", piece10, 84)
-        load_and_cast_w(11, "S", raw_at(5))
+        load_and_cast_w(11, "G", raw_at(6), 2)
+        load_and_cast_w(13, "S", 92)
         slots11 = group_slots("S", piece11, 92)
-        load_and_cast_w(12, "G", raw_at(6), 2)
         load_and_cast_w(14, "G", PLANES_0, 2)
-        load_and_cast_w(16, "S", raw_at(8))
+        load_and_cast_w(16, "S", raw_at(5))
         load_and_cast_w(17, "G", 76)
-        load_and_cast_w(18, "S", 68)
-        slots12 = group_slots("S", piece12, 68)
-        load_and_cast_w(19, "S", raw_at(9))
+        load_and_cast_w(18, "S", raw_at(8))
+        slots12 = group_slots("S", piece12, raw_at(8))
+        load_and_cast_w(19, "S", 68)
         nc.sync.dma_start(b_t[:], b)
-        load_and_cast_w(20, "S", TOKENS_0)
-        load_and_cast_w(21, "S", raw_at(0))
+        cell(20, 3, SPARE + 28)
+        load_and_cast_w(20, "S", raw_at(0))
+        load_and_cast_w(21, "S", TOKENS_0)
+        load_and_cast_w(22, "S", raw_at(1))
 
-        y = at("y", [P, S], F32, SLOTS_0)
-        quantise_w(6, 4, 60, 64)
-        quantise_slots(1, 0, slots10[:], 36, 46)
-        quantise_w(10, 2, 44, 47)
-        quantise_slots(1, 1024, slots11[:], 40, 65)
-        quantise_w(12, 4, 76, TABLES + 9)
-        quantise_slots(1, 2048, slots12[:], SPARE + 34, TABLES + 10)
-        cell(22, 2, raw_at(5))
-        cell(24, 1, raw_at(0))
-        load_and_cast_w(22, "V", raw_at(2))
-        quantise_w(16, 4, SPARE + 20, TABLES + 11)
+        y = at("y", [P, S], F32, SLOTS_0 + 1)
+        quantise_w(6, 4, SPARE + 38, 76)
+        quantise_slots(1, 0, slots10[:], 36, 77)
+        quantise_w(10, 4, 120, 78)
+        quantise_slots(1, 1024, slots11[:], 40, raw_at(10) + 9)
+        quantise_w(14, 4, 84, TABLES + 10)
+        quantise_slots(1, 2048, slots12[:], SPARE + 34, TABLES + 11)
+        quantise_w(18, 2, SPARE + 20, 79)
+        cell(23, 1, 112)
         load_and_cast_w(23, "V", raw_at(3))
-        quantise_w(20, 2, 82, cell_at(10))
-        quantise_w(22, 2, cell_at(11), raw_at(0) + 3.5)
+        quantise_w(20, 2, 82, 100)
+        quantise_w(22, 1, 88, 100.5)
+        quantise_w(23, 1, 102, raw_at(1) + 1.75)
         for e in range(0, 20, 4):
-            expert_bank(e, 4, e // 4)
-        expert_bank(20, 2, 0)
-        expert_bank(22, 2, 1)
+            expert_bank(e, 4)
+        expert_bank(20, 2)
+        expert_bank(22, 2)
+        cell(24, 1, raw_at(1) + 2)
         load_and_cast_w(E, "V", raw_at(4))
         gate_rows = held.tile([P, P], F32, name="gate_rows")
         nc.sync.dma_start(gate_rows[:], gate[0].rearrange("n (c t) -> (n c) t", t=P)[:P])
-        gate_bank = bank_at("gate_bank", [P, P], 7)
+        gate_bank = psum.tile([P, P], F32, name="gate_bank", tag="shared0", bufs=1)
         turn(gate_bank[:], [gate_rows[:]])
-        gate_columns = held.tile([P, T // P], F32, name="gate_columns")
+        gate_columns = at("gate_columns", [P, T // P], F32, raw_at(1) + 1.5)
         nc.scalar.copy(gate_columns[:], gate_bank[:, : T // P])
         nc.sync.dma_start(pos1_t[:], pos1)
         nc.sync.dma_start(pos2_t[:], pos2)
-        token_codes[1, 0] = quantise("t1", tokens1[:, :2048], cell_at(13), raw_at(0) + 2)
-        quantise_w(E, 1, cell_at(10) + 1, cell_at(12))
-        token_codes[1, 512] = quantise("t1b", tokens1[:, 2048:], cell_at(14), raw_at(0) + 2.5)
-        token_codes[1, 1024] = quantise("t1e", tokens1_end[:], cell_at(15), raw_at(0) + 3)
+        token_codes[1, 0] = quantise("t1", tokens1[:, :2048], 104, raw_at(1))
+        quantise_w(E, 1, 101, 103)
+        token_codes[1, 512] = quantise("t1b", tokens1[:, 2048:], 106, raw_at(1) + 0.5)
+        token_codes[1, 1024] = quantise("t1e", tokens1_end[:], 108, raw_at(1) + 1)
 
         second_gate = at("second_gate", [P, T], F32, TABLES + 12)
         nc.sync.dma_start(second_gate[:], gate[1])
         first_gate = at("first_gate", [P, T - TURNED_TOKENS], F32, TABLES + 18)
         nc.sync.dma_start(first_gate[:], gate[0, :, TURNED_TOKENS:])
         wc, ws = w_codes[E][0]
-        second = at("second", [P, T], F32, raw_at(7))
-        last_first = at("last_first", [P, T - TURNED_TOKENS], F32, TABLES + 20)
-        total = at("total", [P, T], F32, PLANES_0)
+        shared_turned = at("shared_turned", [P, TURNED_TOKENS], F32, raw_at(10) + 2)
+        first_turned = at("first_turned", [P, TURNED_TOKENS], F32, 68)
+        second = at("second", [P, T], F32, raw_at(13))
+        last_first = at("last_first", [P, T - TURNED_TOKENS], F32, TABLES + 19)
+        total = at("total", [P, T], F32, raw_at(5))
         turned = [(t0, min(t0 + 512, TURNED_TOKENS)) for t0 in range(0, TURNED_TOKENS, 512)]
 
         def token_operand(g, t0):
             first = max(a for (h, a) in token_codes if h == g and a <= t0)
             return token_codes[g, first], t0 - first
 
-        def shared_product(dst, t0, t1):
+        def shared_product(c):
+            t0, t1 = turned[c]
+            bank = psum.tile([P, (t1 - t0) // P, N], F32, name="shared", tag="shared%d" % c, bufs=1)
             for j in range((t1 - t0) // P):
                 for g in range(G):
                     (xc, xs), x0 = token_operand(g, t0 + P * j)
                     nc.tensor.matmul_mx(
-                        out=dst[:, P * j : P * (j + 1)],
+                        out=bank[:, j, :],
                         lhsT=xc[:, x0 : x0 + P].bitcast(FP8X4),
                         lhsT_scale=xs[:, x0 : x0 + P],
                         rhs=wc[:, g * N : (g + 1) * N].bitcast(FP8X4),
@@ -304,41 +314,37 @@ def tile_moe_shr_lin_bias_kernel(tc, xT, w, b, gate, offs, pos1, pos2, out):
                         start=(g == 0),
                         stop=(g == G - 1),
                     )
+            return bank
 
-        shared = [bank_at("shared%d" % c, [P, t1 - t0], (5, 6, 0)[c]) for c, (t0, t1) in enumerate(turned)]
-        for c in range(len(turned)):
-            shared_product(shared[c], *turned[c])
+        shared = [shared_product(c) for c in range(len(turned))]
+        shared_end = psum.tile([P, T - TURNED_TOKENS], F32, name="shared_end", tag="shared_end", bufs=1)
+        multiply(shared_end[:], E, [token_operand(g, TURNED_TOKENS) for g in range(G)], T - TURNED_TOKENS)
 
         across = []
-        for c, (t0, t1) in enumerate(turned):
-            first = at("first%d" % c, [P, t1 - t0], F32, (raw_at(10) + 2, 66, 68)[c])
-            nc.scalar.activation(first[:], y[:].indirect(pos1_t[:, t0 // 16 : t1 // 16]), COPY)
-            across.append(bank_at("across%d" % c, [P, t1 - t0], 2 + c))
-            for a in range(0, t1 - t0, P):
-                turn(across[c][:, a : a + P], [first[:, a : a + P]])
-
-        shared_turned = at("shared_turned", [P, TURNED_TOKENS], F32, raw_at(10) + 2)
-        first_turned = at("first_turned", [P, TURNED_TOKENS], F32, raw_at(12) + 2)
         backs = []
+
+        def fetch_first(c):
+            t0, t1 = turned[c]
+            t = at("first%d" % c, [P, t1 - t0], F32, (raw_at(10) + 2, PLANES_0, PLANES_0 + 2)[c])
+            nc.scalar.activation(t[:], y[:].indirect(pos1_t[:, t0 // 16 : t1 // 16]), COPY)
+            across.append(psum.tile([P, (t1 - t0) // P, P], F32, name="across", tag="bank", bufs=4))
+            for j in range((t1 - t0) // P):
+                turn(across[c][:, j, :], [t[:, P * j : P * (j + 1)]])
 
         def scale_and_turn_back(c):
             t0, t1 = turned[c]
-            nc.scalar.copy(shared_turned[:, t0:t1], shared[c][:])
-            backs.append(bank_at("back%d" % c, [P, t1 - t0], 5 + c))
-            for a in range(t0, t1, P):
-                turn_onto(backs[c][:, a - t0 : a - t0 + P], shared_turned[:, a : a + P], a == t0, False)
-            for a in range(t0, t1, P):
-                scale = gate_columns[:, a // P : a // P + 1]
-                nc.scalar.activation(first_turned[:, a : a + P], across[c][:, a - t0 : a - t0 + P], COPY, scale=scale)
-                turn_onto(backs[c][:, a - t0 : a - t0 + P], first_turned[:, a : a + P], False, a == t1 - P)
+            nc.scalar.copy(shared_turned[:, t0:t1], shared[c][:].rearrange("p j n -> p (j n)"))
+            backs.append(psum.tile([P, (t1 - t0) // P, P], F32, name="back", tag="shared%d" % c, bufs=1))
+            for j in range((t1 - t0) // P):
+                block = t0 // P + j
+                cols = slice(P * block, P * (block + 1))
+                scale = gate_columns[:, block : block + 1]
+                nc.scalar.activation(first_turned[:, cols], across[c][:, j, :], COPY, scale=scale)
+                turn(backs[c][:, j, :], [shared_turned[:, cols], first_turned[:, cols]])
 
-        scale_and_turn_back(0)
-        shared_end = bank_at("shared_end", [P, T - TURNED_TOKENS], 2)
-        for t0, t1 in ((TURNED_TOKENS, T - 256), (T - 256, T)):
-            if t1 > t0:
-                cols = slice(t0 - TURNED_TOKENS, t1 - TURNED_TOKENS)
-                multiply(shared_end[:, cols], E, [token_operand(g, t0) for g in range(G)], t1 - t0)
-        for c in range(1, len(turned)):
+        for c in range(len(turned)):
+            fetch_first(c)
+        for c in range(len(turned)):
             scale_and_turn_back(c)
 
         def fetch(dst, pos, t0, t1, gates):
@@ -353,7 +359,6 @@ def tile_moe_shr_lin_bias_kernel(tc, xT, w, b, gate, offs, pos1, pos2, out):
         fetch(second[:, :512], pos2_t, 0, 512, second_gate[:, :512])
         nc.vector.tensor_tensor(last_first[:], last_first[:], second[:, TURNED_TOKENS:], ADD)
         fetch(second[:, 512:1024], pos2_t, 512, 1024, second_gate[:, 512:1024])
-        close(0, 512, backs[0][:], second[:, :512])
         close(TURNED_TOKENS, T, shared_end[:], last_first[:])
-        for c, (t0, t1) in list(enumerate(turned))[1:]:
-            close(t0, t1, backs[c][:], second[:, t0:t1])
+        for c, (t0, t1) in enumerate(turned):
+            close(t0, t1, backs[c][:].rearrange("p j n -> p (j n)"), second[:, t0:t1])

@@ -118,21 +118,23 @@ def tile_moe_shr_lin_bias_kernel(tc, xT, w, b, gate, offs, pos1, pos2, out):
             for k in range(n):
                 cells[first + k] = (t, k)
 
-        def load_and_cast_w(e, engine, kib, n=1):
+        def load_and_cast_w(e, engine, kib, n=1, scalar_passes=0):
             raw = at("w%d" % e, [P, n * G, 4, N], F32, kib)
             nc.sync.dma_start(raw[:], w_view[:, G * e : G * (e + n)])
             t, k = cells[e]
             dst = t[:, k * 1024 : (k + n) * 1024]
-            if engine == "G":
-                cast("G", dst.rearrange("p (g n j) -> p g n j", n=N, j=4), raw[:].rearrange("p g j n -> p g n j"))
-                return
+            passes = n * G - scalar_passes
             to = dst.rearrange("p (g c i j) -> p g c j i", c=N // 4, i=4, j=4)
             rows = raw[:].rearrange("p g j (c i) -> p g c j i", i=4)
-            if len(engine) == 1:
-                cast(engine, to, rows)
+            if engine == "G":
+                plain = dst.rearrange("p (g n j) -> p g n j", n=N, j=4)
+                cast("G", plain[:, :passes], raw[:, :passes].rearrange("p g j n -> p g n j"))
+            elif passes == 1:
+                cast(engine, to[:, 0], rows[:, 0])
             else:
-                for g in range(G):
-                    cast(engine[g], to[:, g], rows[:, g])
+                cast(engine, to[:, :passes], rows[:, :passes])
+            if scalar_passes:
+                cast("S", to[:, passes:], rows[:, passes:])
 
         def quantise(name, src, codes_kib, scales_kib):
             n = src.shape[1] // 4
@@ -201,10 +203,10 @@ def tile_moe_shr_lin_bias_kernel(tc, xT, w, b, gate, offs, pos1, pos2, out):
         cell(4, 2, 72)
         for e in range(4):
             load_and_cast_w(e, "G", raw_at(5 + e))
-        load_and_cast_w(4, "G", raw_at(9), 2)
         tokens0 = weave("S", "tokens0", tables[0][:], 0, 1024, TOKENS_0)
         tokens0_end = weave("S", "tokens0_end", tables[0][:], 1024, 512, TOKENS_0_END)
         slots0 = [group_slots("S", pieces0[q], (SLOTS_0, SPARE + 20)[q]) for q in range(2)]
+        load_and_cast_w(4, "G", raw_at(9), 2, scalar_passes=1)
         load_x(1, 0, 0, 512, raw_at(11), (("S", 512),))
         slots0.append(group_slots("S", pieces0[2], raw_at(11)))
         load_x(1, 0, 512, 1024, raw_at(13), (("S", 1024),))
@@ -236,29 +238,29 @@ def tile_moe_shr_lin_bias_kernel(tc, xT, w, b, gate, offs, pos1, pos2, out):
         tokens1_end = weave("S", "tokens1_end", tables[1][:], 1024, 512, PLANES_0 + 8)
         load_and_cast_w(10, "S", raw_at(4))
         slots10 = group_slots("S", piece10, 84)
-        load_and_cast_w(11, "G", raw_at(6), 2)
+        load_and_cast_w(11, "G", raw_at(5), 2)
         load_and_cast_w(13, "S", 92)
+        load_and_cast_w(14, "S", raw_at(7))
         slots11 = group_slots("S", piece11, 92)
-        load_and_cast_w(14, "G", PLANES_0, 2)
-        load_and_cast_w(16, "S", raw_at(5))
-        load_and_cast_w(17, "G", 76)
+        load_and_cast_w(15, "G", 76)
+        load_and_cast_w(16, "G", PLANES_0, 2)
         load_and_cast_w(18, "S", raw_at(8))
-        slots12 = group_slots("S", piece12, raw_at(8))
-        load_and_cast_w(19, "S", 68)
+        load_and_cast_w(19, "S", raw_at(9))
+        slots12 = group_slots("S", piece12, raw_at(7))
         nc.sync.dma_start(b_t[:], b)
-        cell(20, 3, SPARE + 28)
+        cell(20, 3, 68)
         load_and_cast_w(20, "S", raw_at(0))
         load_and_cast_w(21, "S", TOKENS_0)
         load_and_cast_w(22, "S", raw_at(1))
 
         y = at("y", [P, S], F32, SLOTS_0 + 1)
-        quantise_w(6, 4, SPARE + 38, 76)
-        quantise_slots(1, 0, slots10[:], 36, 77)
-        quantise_w(10, 4, 120, 78)
+        quantise_w(6, 4, SPARE + 38, PLANES_0 + 4)
+        quantise_slots(1, 0, slots10[:], 36, PLANES_0 + 5)
+        quantise_w(10, 4, 120, PLANES_0 + 6)
         quantise_slots(1, 1024, slots11[:], 40, raw_at(10) + 9)
         quantise_w(14, 4, 84, TABLES + 10)
+        quantise_w(18, 2, SPARE + 20, PLANES_0 + 7)
         quantise_slots(1, 2048, slots12[:], SPARE + 34, TABLES + 11)
-        quantise_w(18, 2, SPARE + 20, 79)
         cell(23, 1, 112)
         load_and_cast_w(23, "V", raw_at(3))
         quantise_w(20, 2, 82, 100)
@@ -289,7 +291,7 @@ def tile_moe_shr_lin_bias_kernel(tc, xT, w, b, gate, offs, pos1, pos2, out):
         nc.sync.dma_start(first_gate[:], gate[0, :, TURNED_TOKENS:])
         wc, ws = w_codes[E][0]
         shared_turned = at("shared_turned", [P, TURNED_TOKENS], F32, raw_at(10) + 2)
-        first_turned = at("first_turned", [P, TURNED_TOKENS], F32, 68)
+        first_turned = at("first_turned", [P, TURNED_TOKENS], F32, raw_at(7))
         second = at("second", [P, T], F32, raw_at(13))
         last_first = at("last_first", [P, T - TURNED_TOKENS], F32, TABLES + 19)
         total = at("total", [P, T], F32, raw_at(5))

@@ -248,10 +248,11 @@ def tile_moe_shr_lin_bias_kernel(tc, xT, w, b, gate, offs, pos1, pos2, out):
         load_and_cast_w(19, "S", raw_at(9))
         slots12 = group_slots("S", piece12, raw_at(7))
         nc.sync.dma_start(b_t[:], b)
-        cell(20, 3, 68)
+        cell(20, 4, 68)
         load_and_cast_w(20, "S", raw_at(0))
-        load_and_cast_w(21, "S", TOKENS_0)
-        load_and_cast_w(22, "S", raw_at(1))
+        load_and_cast_w(21, "S", raw_at(1))
+        load_and_cast_w(22, "S", TOKENS_0)
+        load_and_cast_w(23, "S", raw_at(3))
 
         y = at("y", [P, S], F32, SLOTS_0 + 1)
         quantise_w(6, 4, SPARE + 38, PLANES_0 + 4)
@@ -261,29 +262,26 @@ def tile_moe_shr_lin_bias_kernel(tc, xT, w, b, gate, offs, pos1, pos2, out):
         quantise_w(14, 4, 84, TABLES + 10)
         quantise_w(18, 2, SPARE + 20, PLANES_0 + 7)
         quantise_slots(1, 2048, slots12[:], SPARE + 34, TABLES + 11)
-        cell(23, 1, 112)
-        load_and_cast_w(23, "V", raw_at(3))
         quantise_w(20, 2, 82, 100)
-        quantise_w(22, 1, 88, 100.5)
-        quantise_w(23, 1, 102, raw_at(1) + 1.75)
+        quantise_w(22, 2, 88, 100.5)
         for e in range(0, 20, 4):
             expert_bank(e, 4)
         expert_bank(20, 2)
         expert_bank(22, 2)
-        cell(24, 1, raw_at(1) + 2)
+        cell(24, 1, raw_at(3) + 2)
         load_and_cast_w(E, "V", raw_at(4))
         gate_rows = held.tile([P, P], F32, name="gate_rows")
         nc.sync.dma_start(gate_rows[:], gate[0].rearrange("n (c t) -> (n c) t", t=P)[:P])
         gate_bank = psum.tile([P, P], F32, name="gate_bank", tag="shared0", bufs=1)
         turn(gate_bank[:], [gate_rows[:]])
-        gate_columns = at("gate_columns", [P, T // P], F32, raw_at(1) + 1.5)
+        gate_columns = at("gate_columns", [P, T // P], F32, raw_at(3) + 1.5)
         nc.scalar.copy(gate_columns[:], gate_bank[:, : T // P])
         nc.sync.dma_start(pos1_t[:], pos1)
         nc.sync.dma_start(pos2_t[:], pos2)
-        token_codes[1, 0] = quantise("t1", tokens1[:, :2048], 104, raw_at(1))
+        token_codes[1, 0] = quantise("t1", tokens1[:, :2048], 104, raw_at(3))
         quantise_w(E, 1, 101, 103)
-        token_codes[1, 512] = quantise("t1b", tokens1[:, 2048:], 106, raw_at(1) + 0.5)
-        token_codes[1, 1024] = quantise("t1e", tokens1_end[:], 108, raw_at(1) + 1)
+        token_codes[1, 512] = quantise("t1b", tokens1[:, 2048:], 106, raw_at(3) + 0.5)
+        token_codes[1, 1024] = quantise("t1e", tokens1_end[:], 108, raw_at(3) + 1)
 
         second_gate = at("second_gate", [P, T], F32, TABLES + 12)
         nc.sync.dma_start(second_gate[:], gate[1])
@@ -337,12 +335,15 @@ def tile_moe_shr_lin_bias_kernel(tc, xT, w, b, gate, offs, pos1, pos2, out):
             t0, t1 = turned[c]
             nc.scalar.copy(shared_turned[:, t0:t1], shared[c][:].rearrange("p j n -> p (j n)"))
             backs.append(psum.tile([P, (t1 - t0) // P, P], F32, name="back", tag="shared%d" % c, bufs=1))
-            for j in range((t1 - t0) // P):
-                block = t0 // P + j
+            blocks = range(t0 // P, t1 // P)
+            for block in blocks:
+                cols = slice(P * block, P * (block + 1))
+                turn_onto(backs[c][:, block - blocks[0], :], shared_turned[:, cols], block == blocks[0], False)
+            for block in blocks:
                 cols = slice(P * block, P * (block + 1))
                 scale = gate_columns[:, block : block + 1]
-                nc.scalar.activation(first_turned[:, cols], across[c][:, j, :], COPY, scale=scale)
-                turn(backs[c][:, j, :], [shared_turned[:, cols], first_turned[:, cols]])
+                nc.scalar.activation(first_turned[:, cols], across[c][:, block - blocks[0], :], COPY, scale=scale)
+                turn_onto(backs[c][:, block - blocks[0], :], first_turned[:, cols], False, block == blocks[-1])
 
         for c in range(len(turned)):
             fetch_first(c)

@@ -118,23 +118,28 @@ def tile_moe_shr_lin_bias_kernel(tc, xT, w, b, gate, offs, pos1, pos2, out):
             for k in range(n):
                 cells[first + k] = (t, k)
 
-        def load_and_cast_w(e, engine, kib, n=1, scalar_passes=0):
+        def load_w(e, kib, n=1):
             raw = at("w%d" % e, [P, n * G, 4, N], F32, kib)
             nc.sync.dma_start(raw[:], w_view[:, G * e : G * (e + n)])
+            return raw
+
+        def cast_w(engine, e, raw, a, z):
             t, k = cells[e]
-            dst = t[:, k * 1024 : (k + n) * 1024]
-            passes = n * G - scalar_passes
-            to = dst.rearrange("p (g c i j) -> p g c j i", c=N // 4, i=4, j=4)
-            rows = raw[:].rearrange("p g j (c i) -> p g c j i", i=4)
+            dst = t[:, (k * G + a) * 512 : (k * G + z) * 512]
             if engine == "G":
-                plain = dst.rearrange("p (g n j) -> p g n j", n=N, j=4)
-                cast("G", plain[:, :passes], raw[:, :passes].rearrange("p g j n -> p g n j"))
-            elif passes == 1:
-                cast(engine, to[:, 0], rows[:, 0])
+                cast("G", dst.rearrange("p (g n j) -> p g n j", n=N, j=4), raw[:, a:z].rearrange("p g j n -> p g n j"))
+            elif z - a == 1:
+                to = dst.rearrange("p (c i j) -> p c j i", i=4, j=4)
+                cast(engine, to, raw[:, a].rearrange("p j (c i) -> p c j i", i=4))
             else:
-                cast(engine, to[:, :passes], rows[:, :passes])
+                to = dst.rearrange("p (g c i j) -> p g c j i", c=N // 4, i=4, j=4)
+                cast(engine, to, raw[:, a:z].rearrange("p g j (c i) -> p g c j i", i=4))
+
+        def load_and_cast_w(e, engine, kib, n=1, scalar_passes=0):
+            raw = load_w(e, kib, n)
+            cast_w(engine, e, raw, 0, n * G - scalar_passes)
             if scalar_passes:
-                cast("S", to[:, passes:], rows[:, passes:])
+                cast_w("S", e, raw, n * G - scalar_passes, n * G)
 
         def quantise(name, src, codes_kib, scales_kib):
             n = src.shape[1] // 4
@@ -248,11 +253,10 @@ def tile_moe_shr_lin_bias_kernel(tc, xT, w, b, gate, offs, pos1, pos2, out):
         load_and_cast_w(19, "S", raw_at(9))
         slots12 = group_slots("S", piece12, raw_at(7))
         nc.sync.dma_start(b_t[:], b)
-        cell(20, 4, 68)
+        cell(20, 3, 68)
         load_and_cast_w(20, "S", raw_at(0))
         load_and_cast_w(21, "S", raw_at(1))
         load_and_cast_w(22, "S", TOKENS_0)
-        load_and_cast_w(23, "S", raw_at(3))
 
         y = at("y", [P, S], F32, SLOTS_0 + 1)
         quantise_w(6, 4, SPARE + 38, PLANES_0 + 4)
@@ -262,8 +266,11 @@ def tile_moe_shr_lin_bias_kernel(tc, xT, w, b, gate, offs, pos1, pos2, out):
         quantise_w(14, 4, 84, TABLES + 10)
         quantise_w(18, 2, SPARE + 20, PLANES_0 + 7)
         quantise_slots(1, 2048, slots12[:], SPARE + 34, TABLES + 11)
+        cell(23, 1, 90)
+        load_and_cast_w(23, "V", raw_at(3), scalar_passes=1)
         quantise_w(20, 2, 82, 100)
-        quantise_w(22, 2, 88, 100.5)
+        quantise_w(22, 1, 88, 100.5)
+        quantise_w(23, 1, 89, 100.75)
         for e in range(0, 20, 4):
             expert_bank(e, 4)
         expert_bank(20, 2)

from contextlib import ExitStack

import concourse.mybir as mybir
from concourse.masks import make_identity

P = 128
K, T, E, C, N = 1024, 1536, 24, 128, 128
S = E * C
G = 2
PIECE = 1024
KB = 1024

F32 = mybir.dt.float32
BF16 = mybir.dt.bfloat16
U32 = mybir.dt.uint32
U16 = mybir.dt.uint16
U8 = mybir.dt.uint8
FP8X4 = mybir.dt.float8_e4m3fn_x4
ADD = mybir.AluOpType.add
MULT = mybir.AluOpType.mult
IDENTITY = mybir.ActivationFunctionType.Identity
COPY = mybir.ActivationFunctionType.Copy

TABLES = 0
PLANES_0 = 24
CODES_2 = 24
SLOTS_0 = 48
Y = 52
TOKENS_0, TOKENS_0_END, TOKENS_1 = 56, 64, 68
PLANES_11 = 60
CELLS = 80
RAW = 124
SPARE = 192
CELL_6, CELL_0, PLANES_10 = 208, 214, 216

SCALAR_HEAD_TOKENS = 160
TURNED_TOKENS = 1280

FLOPS = 2 * K * N * (S + T)


def tile_moe_shr_lin_bias_kernel(tc, xT, w, b, gate, offs, pos1, pos2, out):
    nc = tc.nc
    with ExitStack() as ctx:
        held = ctx.enter_context(tc.tile_pool(name="held", bufs=1))
        room = ctx.enter_context(tc.tile_pool(name="room", bufs=1))
        psum = ctx.enter_context(tc.psum_pool(name="psum", bufs=1))

        offs_t = held.tile([P, S // 16], U16, name="offs_t")
        pos1_t = held.tile([P, T // 16], U16, name="pos1_t")
        pos2_t = held.tile([P, T // 16], U16, name="pos2_t")
        b_t = held.tile([P, E + 1], F32, name="b_t")

        ident = held.tile([P, P], F32, name="ident")
        make_identity(nc, ident[:])

        x_view = xT.rearrange("(g p j) t -> g p j t", g=G, j=4)
        w_view = w.rearrange("e (g p j) n -> p (e g) j n", g=G, j=4)

        def at(name, shape, dtype, kib):
            return room.tile(shape, dtype, name=name, offset=int(kib * KB), align_bytes=64)

        def raw_at(slot):
            return RAW + 4 * slot

        def cell_at(e):
            return CELLS + 2 * e

        tables = [at("table%d" % g, [P, 2 * 2 * T], BF16, TABLES + 12 * g) for g in range(G)]

        def cast(engine, dst, src):
            if engine == "V":
                nc.vector.tensor_copy(dst, src)
            elif engine == "S":
                nc.scalar.copy(dst, src)
            else:
                nc.gpsimd.tensor_scalar(dst, src, 1.0, 0.0, MULT, ADD)

        def load_x(g, u, t0, width, kib, shares, cut=None):
            raw = at("x%d%d_%d" % (g, u, t0), [P, 2, width], F32, kib)
            cut = cut or width
            for c in range(0, width, cut):
                nc.sync.dma_start(raw[:, :, c : c + cut], x_view[g, :, 2 * u : 2 * u + 2, t0 + c : t0 + c + cut])
                first = 2 * (u * T + t0 + c)
                dst = tables[g][:, first : first + 2 * cut].rearrange("p (n e) -> p n e", e=2)
                src = raw[:, :, c : c + cut].rearrange("p e n -> p n e")
                a = 0
                for engine, tokens in shares:
                    cast(engine, dst[:, a : a + tokens, :], src[:, a : a + tokens, :])
                    a = a + tokens

        def planes_at(g, s0, n, kib):
            return (at("planes%d_%d" % (g, s0), [P, 2, 2 * n], BF16, kib), g, s0, n)

        def gather(piece, u):
            planes, g, s0, n = piece
            window = tables[g][:].bitcast(U32)[:, u * T : (u + 1) * T]
            nc.vector.tensor_copy(planes[:, u, :].bitcast(U32), window.indirect(offs_t[:, s0 // 16 : (s0 + n) // 16]))

        def weave(engine, name, halves, t0, n, kib):
            t = at(name, [P, 4 * n], BF16, kib)
            words = halves.bitcast(U32).rearrange("p (u n) -> p n u", u=2)[:, t0 : t0 + n, :]
            to = t[:].bitcast(U32).rearrange("p (n u) -> p n u", u=2)
            if engine == "S":
                nc.scalar.copy(to, words)
            else:
                nc.gpsimd.tensor_copy(to, words)
            return t

        def group_slots(engine, piece, kib):
            planes, g, s0, n = piece
            return weave(engine, "slots%d_%d" % (g, s0), planes[:].rearrange("p u m -> p (u m)"), 0, n, kib)

        cells = {}

        def cell(first, n, kib=None):
            t = at("cell%d" % first, [P, n * 1024], BF16, kib or cell_at(first))
            for k in range(n):
                cells[first + k] = (t, k)

        def load_w(e, kib, n=1):
            raw = at("w%d" % e, [P, n * G, 4, N], F32, kib)
            nc.sync.dma_start(raw[:], w_view[:, G * e : G * (e + n)])
            return raw

        def cast_w(engine, e, raw, a, z):
            t, k = cells[e]
            dst = t[:, (k * G + a) * 512 : (k * G + z) * 512]
            if engine == "G":
                cast("G", dst.rearrange("p (g n j) -> p g n j", n=N, j=4), raw[:, a:z].rearrange("p g j n -> p g n j"))
            elif z - a == 1:
                to = dst.rearrange("p (c i j) -> p c j i", i=4, j=4)
                cast(engine, to, raw[:, a].rearrange("p j (c i) -> p c j i", i=4))
            else:
                to = dst.rearrange("p (g c i j) -> p g c j i", c=N // 4, i=4, j=4)
                cast(engine, to, raw[:, a:z].rearrange("p g j (c i) -> p g c j i", i=4))

        def load_and_cast_w(e, engine, kib, n=1, scalar_passes=0):
            raw = load_w(e, kib, n)
            cast_w(engine, e, raw, 0, n * G - scalar_passes)
            if scalar_passes:
                cast_w("S", e, raw, n * G - scalar_passes, n * G)

        def quantise(name, src, codes_kib, scales_kib):
            n = src.shape[1] // 4
            c = at("codes_" + name, [P, n], U32, codes_kib)
            s = at("scales_" + name, [P, n], U8, scales_kib)
            nc.vector.quantize_mx(out=c[:].bitcast(FP8X4), scales=s[:], in_=src)
            return c, s

        w_codes = {}

        def quantise_w(e0, n, codes_kib, scales_kib):
            t, k0 = cells[e0]
            pair = quantise("w%d" % e0, t[:, k0 * 1024 : (k0 + n) * 1024], codes_kib, scales_kib)
            for k in range(n):
                w_codes[e0 + k] = (pair, k * G * N)

        slot_codes = {}

        def quantise_slots(g, s0, src, codes_kib, scales_kib):
            pair = quantise("s%d_%d" % (g, s0), src, codes_kib, scales_kib)
            for k in range(src.shape[1] // 4 // C):
                slot_codes[g, s0 // C + k] = (pair, k * C)

        def multiply(dst, e, moving, width):
            (c, s), col = w_codes[e]
            for g in range(G):
                (xc, xs), x0 = moving[g]
                nc.tensor.matmul_mx(
                    out=dst,
                    lhsT=c[:, col + g * N : col + (g + 1) * N].bitcast(FP8X4),
                    lhsT_scale=s[:, col + g * N : col + (g + 1) * N],
                    rhs=xc[:, x0 : x0 + width].bitcast(FP8X4),
                    rhs_scale=xs[:, x0 : x0 + width],
                    start=(g == 0),
                    stop=(g == G - 1),
                )

        def turn(dst, terms):
            for k, term in enumerate(terms):
                nc.tensor.matmul(dst, term, ident[:], start=(k == 0), stop=(k == len(terms) - 1), is_transpose=True)

        def turn_onto(dst, term, start, stop):
            nc.tensor.matmul(dst, term, ident[:], start=start, stop=stop, is_transpose=True)

        def bank_at(name, shape, number):
            return psum.tile(shape, F32, name=name, offset=number * 2 * KB)

        def expert_bank(e0, n):
            bank = psum.tile([P, n, C], F32, name="bank", tag="bank", bufs=4)
            for k in range(n):
                multiply(bank[:, k, :], e0 + k, [slot_codes[g, e0 + k] for g in range(G)], C)
            for k in range(n):
                e = e0 + k
                nc.scalar.activation(y[:, e * C : (e + 1) * C], bank[:, k, :], IDENTITY, bias=b_t[:, e : e + 1])

        head = SCALAR_HEAD_TOKENS
        load_x(0, 0, 0, 1024, raw_at(0), (("V", 1024 - head), ("S", head)))
        load_x(0, 0, 1024, 512, raw_at(2), (("V", 256 - head // 2), ("S", head // 2)), cut=256)
        nc.sync.dma_start(offs_t[:], offs)
        load_x(0, 1, 0, 1024, raw_at(3), (("G", 512), ("S", 512)))
        load_x(0, 1, 1024, 512, PLANES_0 + 16, (("S", 512),))
        pieces0 = [planes_at(0, PIECE * q, PIECE, PLANES_0 + 8 * q) for q in range(3)]
        for u, q in ((0, 0), (0, 1), (1, 0), (1, 1), (0, 2), (1, 2)):
            gather(pieces0[q], u)
        cell(0, 4)
        cell(4, 2, 72)
        for e in range(4):
            load_and_cast_w(e, "G", raw_at(5 + e))
        tokens0 = weave("S", "tokens0", tables[0][:], 0, 1024, TOKENS_0)
        tokens0_end = weave("S", "tokens0_end", tables[0][:], 1024, 512, TOKENS_0_END)
        slots0 = [group_slots("S", pieces0[q], (SLOTS_0, SPARE + 20)[q]) for q in range(2)]
        load_and_cast_w(4, "G", raw_at(9), 2, scalar_passes=1)
        load_x(1, 0, 0, 512, raw_at(11), (("S", 512),))
        slots0.append(group_slots("S", pieces0[2], raw_at(11)))
        load_x(1, 0, 512, 1024, raw_at(13), (("S", 1024),))
        load_x(1, 1, 0, 1024, raw_at(15), (("S", 1024),))
        load_x(1, 1, 1024, 512, SPARE + 28, (("S", 512),))

        token_codes = {}
        token_codes[0, 0] = quantise("t0", tokens0[:], SPARE, raw_at(10))
        quantise_w(0, 4, SPARE + 16, raw_at(10) + 1)
        quantise_slots(0, 0, slots0[0][:], SPARE + 4, TOKENS_0 + 7)
        token_codes[0, 1024] = quantise("t0e", tokens0_end[:], TABLES + 4, cell_at(0))
        quantise_slots(0, 1024, slots0[1][:], SPARE + 8, SLOTS_0)
        quantise_slots(0, 2048, slots0[2][:], SPARE + 12, TABLES + 2)
        quantise_w(4, 2, TABLES + 7, PLANES_0 + 23.5)

        piece10 = planes_at(1, 0, PIECE, raw_at(12) + 2)
        piece11 = planes_at(1, PIECE, PIECE, SPARE + 22)
        piece12 = planes_at(1, 2 * PIECE, PIECE, SPARE + 30)
        for piece in (piece10, piece11, piece12):
            gather(piece, 0)
            gather(piece, 1)
        cell(6, 4, raw_at(10) + 2)
        cell(10, 4, 100)
        cell(14, 4, 108)
        cell(18, 2, 116)
        load_and_cast_w(6, "G", raw_at(0), 2)
        load_and_cast_w(8, "G", raw_at(2), 2)
        tokens1 = weave("S", "tokens1", tables[1][:], 0, 1024, raw_at(15))
        tokens1_end = weave("S", "tokens1_end", tables[1][:], 1024, 512, PLANES_0 + 8)
        load_and_cast_w(10, "S", raw_at(4))
        slots10 = group_slots("S", piece10, 84)
        load_and_cast_w(11, "G", raw_at(5), 2)
        load_and_cast_w(13, "S", 92)
        load_and_cast_w(14, "S", raw_at(7))
        slots11 = group_slots("S", piece11, 92)
        load_and_cast_w(15, "G", 76)
        load_and_cast_w(16, "G", PLANES_0, 2)
        load_and_cast_w(18, "S", raw_at(8))
        load_and_cast_w(19, "S", raw_at(9))
        slots12 = group_slots("S", piece12, raw_at(7))
        nc.sync.dma_start(b_t[:], b)
        cell(20, 3, 68)
        load_and_cast_w(20, "S", raw_at(0))
        load_and_cast_w(21, "S", raw_at(1))
        load_and_cast_w(22, "S", TOKENS_0)

        y = at("y", [P, S], F32, SLOTS_0 + 1)
        quantise_w(6, 4, SPARE + 38, PLANES_0 + 4)
        quantise_slots(1, 0, slots10[:], 36, PLANES_0 + 5)
        quantise_w(10, 4, 120, PLANES_0 + 6)
        quantise_slots(1, 1024, slots11[:], 40, raw_at(10) + 9)
        quantise_w(14, 4, 84, TABLES + 10)
        quantise_w(18, 2, SPARE + 20, PLANES_0 + 7)
        quantise_slots(1, 2048, slots12[:], SPARE + 34, TABLES + 11)
        cell(23, 1, 90)
        load_and_cast_w(23, "V", raw_at(3), scalar_passes=1)
        quantise_w(20, 2, 82, 100)
        quantise_w(22, 1, 88, 100.5)
        quantise_w(23, 1, 89, 100.75)
        for e in range(0, 20, 4):
            expert_bank(e, 4)
        expert_bank(20, 2)
        expert_bank(22, 2)
        cell(24, 1, raw_at(3) + 2)
        load_and_cast_w(E, "V", raw_at(4))
        gate_rows = held.tile([P, P], F32, name="gate_rows")
        nc.sync.dma_start(gate_rows[:], gate[0].rearrange("n (c t) -> (n c) t", t=P)[:P])
        gate_bank = psum.tile([P, P], F32, name="gate_bank", tag="shared0", bufs=1)
        turn(gate_bank[:], [gate_rows[:]])
        gate_columns = at("gate_columns", [P, T // P], F32, raw_at(3) + 1.5)
        nc.scalar.copy(gate_columns[:], gate_bank[:, : T // P])
        nc.sync.dma_start(pos1_t[:], pos1)
        nc.sync.dma_start(pos2_t[:], pos2)
        token_codes[1, 0] = quantise("t1", tokens1[:, :2048], 104, raw_at(3))
        quantise_w(E, 1, 101, 103)
        token_codes[1, 512] = quantise("t1b", tokens1[:, 2048:], 106, raw_at(3) + 0.5)
        token_codes[1, 1024] = quantise("t1e", tokens1_end[:], 108, raw_at(3) + 1)

        second_gate = at("second_gate", [P, T], F32, TABLES + 12)
        nc.sync.dma_start(second_gate[:], gate[1])
        first_gate = at("first_gate", [P, T - TURNED_TOKENS], F32, TABLES + 18)
        nc.sync.dma_start(first_gate[:], gate[0, :, TURNED_TOKENS:])
        wc, ws = w_codes[E][0]
        shared_turned = at("shared_turned", [P, TURNED_TOKENS], F32, raw_at(10) + 2)
        first_turned = at("first_turned", [P, TURNED_TOKENS], F32, raw_at(7))
        second = at("second", [P, T], F32, raw_at(13))
        last_first = at("last_first", [P, T - TURNED_TOKENS], F32, TABLES + 19)
        total = at("total", [P, T], F32, raw_at(5))
        turned = [(t0, min(t0 + 512, TURNED_TOKENS)) for t0 in range(0, TURNED_TOKENS, 512)]

        def token_operand(g, t0):
            first = max(a for (h, a) in token_codes if h == g and a <= t0)
            return token_codes[g, first], t0 - first

        def shared_product(c):
            t0, t1 = turned[c]
            bank = psum.tile([P, (t1 - t0) // P, N], F32, name="shared", tag="shared%d" % c, bufs=1)
            for j in range((t1 - t0) // P):
                for g in range(G):
                    (xc, xs), x0 = token_operand(g, t0 + P * j)
                    nc.tensor.matmul_mx(
                        out=bank[:, j, :],
                        lhsT=xc[:, x0 : x0 + P].bitcast(FP8X4),
                        lhsT_scale=xs[:, x0 : x0 + P],
                        rhs=wc[:, g * N : (g + 1) * N].bitcast(FP8X4),
                        rhs_scale=ws[:, g * N : (g + 1) * N],
                        start=(g == 0),
                        stop=(g == G - 1),
                    )
            return bank

        shared = [shared_product(c) for c in range(len(turned))]
        shared_end = psum.tile([P, T - TURNED_TOKENS], F32, name="shared_end", tag="shared_end", bufs=1)
        multiply(shared_end[:], E, [token_operand(g, TURNED_TOKENS) for g in range(G)], T - TURNED_TOKENS)

        across = []
        backs = []

        def fetch_first(c):
            t0, t1 = turned[c]
            t = at("first%d" % c, [P, t1 - t0], F32, (raw_at(10) + 2, PLANES_0, PLANES_0 + 2)[c])
            nc.scalar.activation(t[:], y[:].indirect(pos1_t[:, t0 // 16 : t1 // 16]), COPY)
            across.append(psum.tile([P, (t1 - t0) // P, P], F32, name="across", tag="bank", bufs=4))
            for j in range((t1 - t0) // P):
                turn(across[c][:, j, :], [t[:, P * j : P * (j + 1)]])

        def scale_and_turn_back(c):
            t0, t1 = turned[c]
            nc.scalar.copy(shared_turned[:, t0:t1], shared[c][:].rearrange("p j n -> p (j n)"))
            backs.append(psum.tile([P, (t1 - t0) // P, P], F32, name="back", tag="shared%d" % c, bufs=1))
            blocks = range(t0 // P, t1 // P)
            for block in blocks:
                cols = slice(P * block, P * (block + 1))
                turn_onto(backs[c][:, block - blocks[0], :], shared_turned[:, cols], block == blocks[0], False)
            for block in blocks:
                cols = slice(P * block, P * (block + 1))
                scale = gate_columns[:, block : block + 1]
                nc.scalar.activation(first_turned[:, cols], across[c][:, block - blocks[0], :], COPY, scale=scale)
                turn_onto(backs[c][:, block - blocks[0], :], first_turned[:, cols], False, block == blocks[-1])

        for c in range(len(turned)):
            fetch_first(c)
        for c in range(len(turned)):
            scale_and_turn_back(c)

        def fetch(dst, pos, t0, t1, gates):
            nc.vector.tensor_tensor(dst, y[:].indirect(pos[:, t0 // 16 : t1 // 16]), gates, MULT)

        def close(t0, t1, summed, term):
            nc.vector.scalar_tensor_tensor(total[:, t0:t1], summed, b_t[:, E : E + 1], term, ADD, ADD)
            nc.sync.dma_start(out[:, t0:t1], total[:, t0:t1])

        fetch(last_first[:], pos1_t, TURNED_TOKENS, T, first_gate[:])
        fetch(second[:, 1024:], pos2_t, 1024, T, second_gate[:, 1024:])
        fetch(second[:, :512], pos2_t, 0, 512, second_gate[:, :512])
        nc.vector.tensor_tensor(last_first[:], last_first[:], second[:, TURNED_TOKENS:], ADD)
        fetch(second[:, 512:1024], pos2_t, 512, 1024, second_gate[:, 512:1024])
        close(TURNED_TOKENS, T, shared_end[:], last_first[:])
        for c, (t0, t1) in enumerate(turned):
            close(t0, t1, backs[c][:].rearrange("p j n -> p (j n)"), second[:, t0:t1])
